import numpy as np, ml_dtypes
CORES = [16,17,18,19,32,33,34,35]
N = 8
import mx_ref
BF = ml_dtypes.bfloat16
def pick(q, e):
    c = np.concatenate([q[0].reshape(128, -1, 4), np.zeros((128, 1, 4), np.uint8)], axis=1); s = np.concatenate([q[1], np.ones((16, 1), np.uint8)], axis=1)
    return (np.ascontiguousarray(c[:, e].reshape(128, -1)), np.ascontiguousarray(s[:, e]))
def join(*qs):
    return (np.concatenate([q[0] for q in qs], axis=1), np.concatenate([q[1] for q in qs], axis=1))
def put(q, e, v):
    c, s = q[0].reshape(128, -1, 4).copy(), q[1].copy(); c[:, e] = v[0].reshape(128, -1, 4); s[:, e] = v[1]
    return (c.reshape(128, -1), s)
def pk(c, s):
    return (np.ascontiguousarray(c), mx_ref.live(s))
def emit(q):
    return q[0], q[1]
def decode(q):
    o = []
    for b in range(4):
        e = np.zeros((128, 128, 4), np.float32); e[np.arange(128), np.arange(128), b] = 1
        o.append(mx_ref.matmul(mx_ref.quantize(e.reshape(128, 512).astype(BF)), q))
    return np.stack(o, axis=2).reshape(128, -1)
def cut(t, i, w=512):
    return t[:, w * i:w * i + w]
def f(rng, *shape):
    return mx_ref.flush((rng.standard_normal(shape, dtype=np.float32) * np.exp2(rng.integers(-2, 3, shape[:-1] + (1,)))).astype(BF))
def wide(rng, *shape, cols=0):
    v = rng.standard_normal(shape, dtype=np.float32) * np.exp2(rng.integers(-12, 13, shape)).astype(np.float32)
    if cols: v *= np.repeat(np.exp2(rng.integers(-cols, cols + 1, shape[:-2] + (1, shape[-1] // 4))) * (rng.random(shape[:-2] + (1, shape[-1] // 4)) > 0.0625), 4, axis=-1).astype(np.float32)
    return mx_ref.flush(v.astype(BF))
T, L, O, LV, V, F = 32, 8, 2, 3, 224, 32
DI, DJ = np.array([1, 1, 0, 0]), np.array([1, 0, 1, 0])
def align(g):
    n = g.shape[0]
    p, back = np.zeros((n, L, L), np.float32), np.full((n, L, L), 3)
    for i in range(L):
        for j in range(L):
            if i == 0 and j == 0:
                p[:, i, j] = g[:, i, j]
                continue
            if i == 0: best, back[:, i, j] = p[:, i, j - 1], 2
            elif j == 0: best, back[:, i, j] = p[:, i - 1, j], 1
            else:
                c = np.stack([p[:, i - 1, j - 1], p[:, i - 1, j], p[:, i, j - 1]])
                best, back[:, i, j] = np.max(c, axis=0), np.argmax(c, axis=0)
            p[:, i, j] = g[:, i, j] + best
    m, i, j, low = np.arange(n), np.full(n, L - 1), np.full(n, L - 1), np.zeros((n, L), int)
    for s in range(2 * L - 1):
        low[m, i] = j
        k = back[m, i, j]
        i, j = i - DI[k], j - DJ[k]
    return low
def clear(v):
    v = v.astype(np.float32)
    v[np.abs(v) < np.float32(2.0 ** -14)] = 0
    return v.astype(BF)
def lay(v):
    return np.ascontiguousarray(v.transpose(0, 3, 1, 2, 4)).reshape(N, 128, 4 * T * L).astype(np.float32).astype(BF)
def setup_inputs(rng):
    return {"x": clear(f(rng, N, 128, 4 * T * L)), "w": f(rng, N, 128, 512 * O)}
def setup_inputs_ties(rng):
    kind = (np.arange(T) // N) % 3
    u = rng.choice([-1.0, 1.0], (T, 128, 4)) * np.exp2(rng.integers(-3, 4, (T, 1, 1)))
    s = rng.integers(-1, 2, (N, T, L)).astype(np.float64)
    m = rng.choice([-1.0, 1.0], (N, T, L))
    s[:, :, 0] = 1
    m[:, :, 0] = 1
    m[1::2] = 0
    s[:, kind == 0] = 1
    s[:, kind == 1] = m[:, kind == 1]
    return {"x": lay(s[:, :, :, None, None] * u[None, :, None]), "w": f(rng, N, 128, 512 * O)}
def setup_inputs_near(rng):
    kind = (np.arange(T) // N) % 3
    even, one = kind != 1, kind == 1
    u = rng.choice([-1.0, 1.0], (T, 1, 128, 4))
    v = np.zeros((N, T, L, 128, 4))
    v[:, even, :, :120] = u[even][:, :, :120]
    for r in range(N):
        v[r][one, 0, :64] = 4 * u[one][:, 0, :64]
        v[r][one, 1:, 64 + 6 * r:70 + 6 * r] = rng.choice([-1.0, 1.0], (int(np.count_nonzero(one)), L - 1, 6, 4))
    a = rng.integers(1, 4, (N, T, L)) * rng.choice([-1.0, 1.0], (N, T, L))
    a[:, kind == 2] = 1
    a[0::2][:, kind == 2, L - 1] = 3
    a[1::2][:, kind == 2, 0] = 3
    v[:, :, :, 127, 0] = a * np.where(one, 2.0 ** -6, 2.0 ** -5)[None, :, None]
    return {"x": lay(v * np.exp2(rng.integers(-3, 4, (1, T, 1, 1, 1)))), "w": f(rng, N, 128, 512 * O)}
def setup_inputs_far(rng):
    kind = (np.arange(T) // N) % 3
    deep, side = kind == 2, np.arange(T) // 2 % 2 == 1
    v = 1.5 + 0.5 * rng.random((N, T, L, 128, 4))
    v[:, deep] = 1
    ones = np.array([bin(k).count("1") for k in range(N)])
    c = ones[np.arange(N)[:, None] ^ rng.integers(0, N, T)[None, :]]
    e = -rng.integers(3, 9, (N, T, L))
    e[:, :, 0] = 0
    low = np.exp2(29.0 - c[:, :, None] + e) * (1 - 2 * (c % 2))[:, :, None]
    mixed = np.exp2(rng.integers(20, 30, (N, T, L))) * rng.choice([-1.0, 1.0], (N, T, L))
    mixed[:, :, 0] = 2.0 ** 29
    s = np.where((kind == 0)[None, :, None], low, mixed)
    s[0::2][:, deep] = 2.0 ** 30
    s[1::2][:, deep] = -2.0 ** 30
    s[0::2][:, deep & ~side, L - 1] = 2.0 ** 20
    s[1::2][:, deep & side, L - 1] = -2.0 ** 20
    return {"x": lay(v * s[:, :, :, None, None]), "w": f(rng, N, 128, 512 * O)}
def setup_inputs_warp(rng):
    p = rng.standard_normal((T, L, 128, 4)) * np.exp2(rng.integers(-2, 3, (T, 1, 128, 1)))
    i = np.sort(rng.integers(0, L, (N, T, L)), axis=2)
    v = p[np.arange(T)[None, :, None], i] + 0.25 * rng.standard_normal((N, T, L, 128, 4))
    return {"x": clear(lay(v)), "w": f(rng, N, 128, 512 * O)}
def setup_inputs_spread(rng):
    return {"x": clear(wide(rng, N, 128, 4 * T * L, cols=6)), "w": f(rng, N, 128, 512 * O)}
def check_inputs(d):
    b = []
    for k, least in (("x", 2.0 ** -14), ("w", 2.0 ** -30)):
        v = np.abs(d[k].astype(np.float32))
        if not (np.isfinite(v).all() and ((v == 0) | (v >= least) & (v <= 2.0 ** 30)).all()): b.append("a value of " + k)
    return b
def reference(x, w):
    y, pt = np.zeros((N, 128, O * V), np.float32), np.zeros((N, 1, V), np.float32)
    oc, osc = np.zeros((N, 128, 4 * F), np.uint8), np.zeros((N, 16, F), np.uint8)
    wq = [[mx_ref.quantize(np.ascontiguousarray(cut(w[r], o))) for o in range(O)] for r in range(N)]
    held = [mx_ref.quantize(np.ascontiguousarray(x[r])) for r in range(N)]
    at = 0
    for b in range(LV):
        n = T >> (b + 1)
        h = n * L
        new = []
        for r in range(N):
            p = r ^ (1 << b)
            k = np.arange((r >> b) & 1, T >> b, 2)
            e = (k[:, None] * L + np.arange(L)).reshape(-1)
            lower, upper = pick(held[min(r, p)], e), pick(held[max(r, p)], e)
            g = mx_ref.matmul(pick(lower, np.concatenate([np.arange(h), np.full(128 - h, -1)])), upper)[:h].reshape(n, L, n, L)
            j = align(g[np.arange(n), :, np.arange(n), :])
            met = pick(upper, (np.arange(n)[:, None] * L + j).reshape(-1))
            v = decode(join(lower, met))
            m = mx_ref.quantize(np.ascontiguousarray(((v[:, :4 * h] + v[:, 4 * h:]) * np.float32(0.5)).astype(BF)))
            pt[r, 0, at:at + h] = j.reshape(-1)
            for o in range(O): y[r, :, o * V + at:o * V + at + h] = mx_ref.matmul(wq[r][o], m)
            new.append(m)
        held = new
        at += h
    for r in range(N): oc[r], osc[r] = emit(held[r])
    return {"y": y, "pt": pt, "oc": oc, "osc": osc}

@@ -1,0 +1,500 @@
+from concourse.bass import DstId, RemoteDMATransfer
+from concourse.mybir import dt, AluOpType, ActivationFunctionType
+
+F32, BF, I32, U16, X4, U8 = "float32", "bfloat16", "int32", "uint16", "float8_e4m3fn_x4", "uint8"
+LOW = -1.0e29
+UNIT = 2.0 ** -22
+HDIAG = sum(i * 8 ** (i - 1) for i in range(1, 8)) + 0.5
+BATCHES = ((1, 3), (4, 5), (6, 7))
+GAP = 70
+
+
+def _sb(shape, d):
+    return ("sbuf", [128] + list(shape), d)
+
+
+SCRATCH = {
+    "xs": _sb([4, 8, 32], BF), "xt": _sb([1024], BF), "wt": _sb([1024], BF),
+    "sq": _sb([128], X4), "ss": _sb([128], U8), "lq": _sb([384], X4), "ls": _sb([384], U8),
+    "wq": _sb([256], X4), "ws": _sb([256], U8),
+    "et": _sb([2048], BF), "eq": _sb([512], X4), "es": _sb([512], U8),
+    "st": _sb([512], BF), "stq": _sb([128], X4), "sts": _sb([128], U8),
+    "pi": _sb([2], I32), "fi": _sb([10], I32), "ff": _sb([20], F32),
+    "uu": _sb([128], F32), "vv": _sb([128], BF), "tt": _sb([128], BF), "zz": _sb([256], BF),
+    "mk": _sb([128], F32), "c2": _sb([4], F32), "c4": _sb([2], F32),
+    "l0": _sb([4], U16), "l1": _sb([2], U16), "lh": _sb([2], U16),
+    "part": _sb([36], F32), "row": _sb([36, 8], F32), "ec": _sb([36, 8], F32), "kj": _sb([8], F32),
+    "gm": _sb([256], F32), "gb": _sb([256], F32), "tb": _sb([256], F32),
+    "pb": _sb([288], F32), "q0": _sb([32], F32), "q1": _sb([32], F32), "du": _sb([72], F32), "km": _sb([144], F32),
+    "hb": _sb([192], F32), "hx": _sb([16], F32), "jw": _sb([128], F32),
+    "fl": _sb([128], I32), "dg": _sb([128], I32), "flu": _sb([64], I32), "dgu": _sb([64], I32),
+    "xq": _sb([128], X4), "xsc": _sb([128], U8),
+    "o0": _sb([32], U16), "o1": _sb([32], U16), "o2": _sb([8], U16),
+    "d0": _sb([1536], F32), "d1": _sb([512], F32), "d2": _sb([256], F32),
+    "mt": _sb([512], BF),
+    "m0q": _sb([128], X4), "m0s": _sb([128], U8), "m1q": _sb([128], X4), "m1s": _sb([128], U8),
+    "hq": _sb([160], X4), "hs": _sb([160], U8), "m2q": _sb([128], X4), "m2s": _sb([128], U8),
+    "jt": _sb([896], BF), "jq": _sb([192], X4), "js": _sb([192], U8), "j2q": _sb([128], X4), "j2s": _sb([128], U8),
+    "y0": _sb([8, 4, 8], F32), "y1": _sb([8, 2, 8], F32), "y2": _sb([64], F32),
+    "p0": _sb([4, 4, 8], F32), "p1": _sb([4, 2, 8], F32), "p2": _sb([32], F32),
+}
+for _k in range(8):
+    SCRATCH["b%d" % _k] = ("psum", [128, 512], F32)
+NPOOL = 140
+SEMAPHORES = ["arr0", "arr2", "sent"] + ["s%d" % _k for _k in range(NPOOL)]
+
+
+def make_order(g, T):
+    Q = {"v": g.vector, "a": g.scalar, "t": g.tensor, "g": g, "s": g.sync}
+    known = {k: set() for k in Q}
+    st = {"next": 0}
+    free, total, batches, opened, wrote, read = {}, {}, [], {}, {}, {}
+
+    def wait(q, b):
+        if b in known[q]:
+            return
+        B = batches[b]
+        if opened.get(B["own"]) == b:
+            del opened[B["own"]]
+        Q[q].wait_ge(T.sem[B["sem"]], B["val"])
+        B["waited"] = True
+        known[q].add(b)
+        known[q].update(B["known"])
+
+    def new_sem(own):
+        for b in free.setdefault(own, []):
+            if b in known[own[0]]:
+                free[own].remove(b)
+                return batches[b]["sem"]
+        st["next"] += 1
+        assert st["next"] <= NPOOL
+        return "s%d" % (st["next"] - 1)
+
+    def op(q, fn, r=(), w=(), dma=False, cut=False):
+        deps = set()
+        for k in list(r) + list(w):
+            if k in wrote:
+                deps.add(wrote[k])
+        for k in w:
+            deps.update(read.get(k, ()))
+        for k in r:
+            if k[0] == "b" and len(k) == 2:
+                deps.update(b for b in read.get(k, ()) if batches[b]["own"][0] != q)
+        for b in sorted(deps, reverse=True):
+            wait(q, b)
+        own = (q, dma)
+        if cut and own in opened:
+            del opened[own]
+        if own not in opened:
+            sem = new_sem(own)
+            batches.append({"own": own, "sem": sem, "val": total.get(sem, 0), "known": set(), "waited": False})
+            opened[own] = len(batches) - 1
+            free[own].append(opened[own])
+        b = opened[own]
+        B = batches[b]
+        n = 16 if dma else 1
+        fn().then_inc(T.sem[B["sem"]], n)
+        B["val"] += n
+        total[B["sem"]] = B["val"]
+        B["known"].update(known[q])
+        for k in r:
+            read.setdefault(k, set()).add(b)
+        for k in w:
+            wrote[k] = b
+            read[k] = set()
+
+    def need(q, keys):
+        for k in keys:
+            wait(q, wrote[k])
+
+    def landed(key, sem, val):
+        batches.append({"own": None, "sem": sem, "val": val, "known": set(), "waited": False})
+        wrote[key] = len(batches) - 1
+
+    def close(q):
+        for dma in (False, True):
+            opened.pop((q, dma), None)
+
+    def finish():
+        for b in range(len(batches)):
+            if not batches[b]["waited"]:
+                wait("g", b)
+
+    return op, need, landed, close, finish
+
+
+def interleave(tasks):
+    tail = {}
+    for n in reversed(list(tasks)):
+        tail[n] = tasks[n][0] + max([GAP + tail[m] for m in tasks if n in tasks[m][1]] + [0])
+    done, order, now = {}, [], 0
+    while len(order) < len(tasks):
+        cand = [n for n in tasks if n not in done and all(d in done for d in tasks[n][1])]
+        at = {n: max([now] + [done[d] + GAP for d in tasks[n][1]]) for n in cand}
+        n = min(cand, key=lambda m: (at[m], -tail[m]))
+        now = at[n] + tasks[n][0]
+        done[n] = now
+        order.append(n)
+    return order
+
+
+def rank_program(g, core, T, topo):
+    r = T.rank_of(core)
+    if r is None:
+        return
+    op, need, landed, close, finish = make_order(g, T)
+    A, ACT = AluOpType, ActivationFunctionType
+    V, S, PE = g.vector, g.scalar, g.tensor
+    b0, b1, b2 = r & 1, (r >> 1) & 1, (r >> 2) & 1
+    bank = [T["b%d" % k] for k in range(8)]
+
+    def masks(dst, parts):
+        e = topo.engines(core, dst)
+        n = len(e) // parts
+        return [sum(1 << k for k in e[n * i:n * i + n]) for i in range(parts)], n
+
+    def dst_id(c):
+        a = topo.addr(c)
+        return DstId(rid=int(a[0]), pnc=int(a[1]))
+
+    def iota(out, pat, base, cm, key, small=True):
+        if small:
+            op("g", lambda: g.iota(out, pat, base, cm, allow_small_or_imprecise_dtypes=True), w=[key])
+        else:
+            op("g", lambda: g.iota(out, pat, base, cm), w=[key])
+
+    def fill(out, val, key, rd=()):
+        op("v", lambda: V.memset(out, val), r=rd, w=[key])
+
+    def ts(out, in0, s1, s2, o0, o1, rd, wr):
+        if o1 is None:
+            op("v", lambda: V.tensor_scalar(out, in0, s1, None, o0), r=rd, w=wr)
+        else:
+            op("v", lambda: V.tensor_scalar(out, in0, s1, s2, o0, o1), r=rd, w=wr)
+
+    def tt(out, in0, in1, o, rd, wr, cut=False):
+        op("v", lambda: V.tensor_tensor(out, in0, in1, o), r=rd, w=wr, cut=cut)
+
+    def scan(out, d0, d1, init, rd, wr):
+        op("v", lambda: V.tensor_tensor_scan(out, d0, d1, init, A.max, A.add), r=rd, w=wr, cut=True)
+
+    def copy(out, in_, rd, wr):
+        op("v", lambda: V.tensor_copy(out, in_), r=rd, w=wr)
+
+    def act(out, in_, rd, wr, scale=1.0, bias=None):
+        if bias is None:
+            op("a", lambda: S.activation(out, in_, ACT.Copy, scale=scale), r=rd, w=wr)
+        else:
+            op("a", lambda: S.activation(out, in_, ACT.Identity, bias=bias, scale=scale), r=rd, w=wr)
+
+    def afill(out, n, val, key):
+        act(out, T.zz[:, 0:n], ["zz"], [key], scale=0.0, bias=val)
+
+    def quant(q, s, tile, rd, wr):
+        op("v", lambda: V.quantize_mx(q, s, tile), r=rd, w=wr)
+
+    def mm(k, n, lq, ls, rq, rs, rd):
+        op("t", lambda: PE.matmul_mx(bank[k][:, 0:n], lq, ls, rq, rs, True, True), r=rd, w=["b%d" % k], cut=True)
+
+    def store(q, out, in_, rd):
+        eng = {"s": g.sync, "a": S, "g": g}[q]
+        op(q, lambda: eng.dma_start(out, in_), r=rd, dma=True)
+
+    op("s", lambda: g.sync.dma_start(T.xs[:], T.x[:]), w=["xs"], dma=True)
+    close("s")
+
+    iota(T.pi[:, 0:1], [[0, 1]], 0, 1, "pi", small=False)
+    close("g")
+    iota(T.kj[:], [[1, 8]], 0, 0, "kj")
+    close("g")
+    iota(T.vv[:], [[1, 128]], 0, -1, "vv")
+    close("g")
+    iota(T.uu[:], [[1, 16], [0, 8]], 0, 0, "uu")
+    iota(T.c2[:], [[2, 4]], 0, 0, "c2")
+    iota(T.c4[:], [[4, 2]], 0, 0, "c4")
+    close("g")
+    fill(T.zz[:], 0.0, "zz")
+    close("v")
+    fill(T.et[:], 0.0, "et")
+    for k, (sh, m) in enumerate([(5, 3), (3, 1), (2, 1), (0, 3), (2, 3), (3, 15), (0, 127), (0, 15), (0, 1)]):
+        ts(T.fi[:, k:k + 1], T.pi[:, 0:1], sh, m, A.logical_shift_right, A.bitwise_and, ["pi"], ["fi%d" % k])
+    afill(T.gb[:], 256, 0.0, "gb")
+    afill(T.gm[:, 128:192], 64, 0.0, "gmz")
+    afill(T.pb[:, 3:288:36], 8, LOW, "pad")
+    afill(T.q0[:], 32, LOW, "q0")
+    afill(T.q1[:], 32, LOW, "q1")
+    afill(T.hb[:], 192, -2.0, "hbz")
+    afill(T.jw[:], 128, 0.0, "jw")
+    act(T.q0[:, 0:1], T.zz[:, 0:1], ["zz"], ["q0"], scale=0.0, bias=0.0)
+    act(T.hb[:, 8:24], T.zz[:, 0:16], ["zz", "hbz"], ["hb0"], scale=0.0, bias=-0.5 * UNIT)
+    for i in range(1, 8):
+        act(T.jw[:, 2 * i:128:16], T.kj[:], ["kj", "jw"], ["jw%d" % i], scale=-UNIT * 8 ** (i - 1))
+    close("a")
+    close("v")
+
+    own = 192 * b0
+    keep1 = b2
+    order = [4 * par + (r ^ k) % 4 for k in (3, 1, 2, 0) for par in (1 - keep1, keep1)]
+    for k in (4, 5):
+        act(T.xt[:, 128 * k:128 * k + 128], T.xs[:, :, order[k], :], ["xs"], ["xt%d" % k])
+    close("a")
+    for k in (0, 1, 2, 3):
+        copy(T.xt[:, 128 * k:128 * k + 128], T.xs[:, :, order[k], :], ["xs"], ["xt%d" % k])
+    close("v")
+    for k in (6, 7):
+        copy(T.xt[:, 128 * k:128 * k + 128], T.xs[:, :, order[k], :], ["xs"], ["xt%d" % k])
+    close("v")
+    XA, XB = ["xt0", "xt1", "xt2", "xt3"], ["xt4", "xt5", "xt6", "xt7"]
+    quant(T.sq[:], T.ss[:], T.xt[:, 0:512], XA, ["sq"])
+    quant(T.lq[:, own:own + 128], T.ls[:, own:own + 128], T.xt[:, 512:1024], XB, ["lown"])
+    close("v")
+    need("g", ["sq", "lown"])
+    c1, c2, c3, c4 = (T.cores[r ^ k] for k in (1, 2, 3, 4))
+    ms, ne = masks(c1, 4)
+    for codes in (True, False):
+        src, mine = (T.sq, T.lq) if codes else (T.ss, T.ls)
+        view = (lambda t, a: t[:, a:a + 64].bitcast(dt.uint8)) if codes else (lambda t, a: t[:, a:a + 64])
+        pieces = [(src, 0, c1, own), (src, 64, c1, own + 64), (src, 0, c3, own + 128), (mine, own, c2, own + 128)]
+        g.remote_dma_fused([RemoteDMATransfer(dst_ids=[dst_id(c)], dma_engine_mask=ms[k], remote_sem=T.sem.arr0,
+                                              src=view(t, a), dst=view(mine, at))
+                            for k, (t, a, c, at) in enumerate(pieces)], local_sem=T.sem.sent)
+    sent = 8 * ne
+    landed("lin", "arr0", 8 * ne)
+
+    hb1, qb2 = 1 - b1, b2
+    segs = [(0, 8, [[32, 2], [4, 4]], 66), (8, 8, [[32, 2], [4, 4]], 82), (16, 8, [[32, 2], [8, 4]], 64 * hb1 + 2),
+            (24, 8, [[32, 2], [4, 4]], 2), (32, 4, [[8, 4]], 32 * qb2 + 2)]
+    for k, (at, n, pat, base) in enumerate(segs):
+        iota(T.part[:, at:at + n], pat, base, 0, "part%d" % k)
+    close("g")
+    iota(T.row[0:1, :, :], [[0, 288]], 0, 0, "row")
+    close("g")
+    iota(T.tt[:], [[0, 8], [1, 4], [0, 4]], 0, 0, "tt")
+    close("g")
+    need("g", ["row"])
+    iota(T.row[0:1, 0:32, 1:8:4], [[0, 4], [1, 8], [0, 2]], 0, 0, "r0")
+    iota(T.row[0:1, 0:16, 2:8:4], [[1, 2], [0, 16]], 1, 0, "r1")
+    iota(T.row[0:1, 32:36, 1:8:4], [[1, 4], [0, 2]], 0, 0, "r2")
+    close("g")
+    col = lambda k: T.ff[:, k:k + 1]
+    copy(T.ff[:, 0:9], T.fi[:, 0:9], ["fi%d" % k for k in range(9)], ["ff"])
+    close("v")
+    for b in range(4):
+        ts(T.et[:, 512 * b + b:512 * b + 512:4], T.vv[:], 0.0, None, A.is_equal, None, ["vv", "et"], ["et%d" % b])
+    close("v")
+    ts(col(10), col(0), 32.0, col(1), A.mult, A.add, ["ff"], ["f10"])
+    ts(col(11), col(0), 32.0, col(4), A.mult, A.add, ["ff"], ["f11"])
+    ts(T.lh[:, 0:1], col(7), col(8), 7.0, A.add, A.add, ["ff"], ["lh"])
+    close("v")
+    ts(T.mk[:], T.uu[:], col(5), None, A.is_equal, None, ["uu", "ff"], ["mk"])
+    close("v")
+    ts(col(12), col(2), 128.0, col(10), A.mult, A.add, ["ff", "f10"], ["f12"])
+    ts(col(13), col(3), 8.0, col(11), A.mult, A.add, ["ff", "f11"], ["f13"])
+    close("v")
+    quant(T.eq[:], T.es[:], T.et[:], ["et0", "et1", "et2", "et3"], ["eq"])
+    close("v")
+    ts(col(14), col(3), 8.0, col(12), A.mult, A.add, ["ff", "f12"], ["f14"])
+    ts(T.l1[:], T.c4[:], col(13), None, A.add, None, ["c4", "f13"], ["l1"])
+    ts(T.l0[:], T.c2[:], col(14), None, A.add, None, ["c2", "f14"], ["l0"])
+    close("v")
+    parts = ["part%d" % k for k in range(5)]
+    fill(T.ec[:, :, 0], 0.0, "ec0")
+    for i in range(1, 8):
+        ts(T.ec[:, :, i], T.part[:], col(6), -8.0 ** (1 - i) / UNIT, A.is_equal, A.mult, parts + ["ff"], ["ec%d" % i])
+    for t in range(4):
+        ts(T.st[:, t:512:4], T.tt[:], float(t), 4.0, A.is_equal, A.mult, ["tt"], ["st%d" % t])
+    close("v")
+    for t, val in enumerate((0.0, 32.0, 256.0, 0.0)):
+        fill(T.st[0:1, t:512:4], val, "st%d" % t)
+    close("v")
+    ecs = ["ec%d" % i for i in range(8)]
+    ts(T.ec[0:1, :, :], T.row[0:1, :, :], -1.0 / (UNIT * HDIAG), -0.5 / (UNIT * HDIAG), A.mult, A.add, ["row", "r0", "r1", "r2"], ecs)
+    close("v")
+    quant(T.stq[:], T.sts[:], T.st[:], ["st0", "st1", "st2", "st3"], ["stq"])
+    close("v")
+    jws = ["jw"] + ["jw%d" % i for i in range(1, 8)]
+    path = T.hb[:, 191:192]
+
+    def decode(n, q, s, rd):
+        for b in range(4):
+            mm(b, n, T.eq[:, 128 * b:128 * b + 128], T.es[:, 128 * b:128 * b + 128], q, s, ["eq"] + rd)
+
+    def cells(ja, jb, back):
+        a, b = 9 * ja + 1 - back, 9 * jb + 9 - back
+        return T.pb[:, 4 * a + 3:4 * b:4]
+
+    def align(lst, lkey, step, at, nm, xo, xkeys, xw):
+        copy(T.gb[:, 2:256:step], T.gm[:].indirect(lst[:]), ["gm1", "gm2", "gmz", lkey], ["gb"])
+        op("v", lambda: V.transpose(T.tb[:], T.gb[:]), r=["gb"], w=["tb"])
+        tasks, calls = {}, {}
+        for j in range(8):
+            if j:
+                tasks["x%d" % j] = (64, ["p%d" % (j - 1)])
+                calls["x%d" % j] = lambda j=j: tt(T.q1[:, 0:32:4], cells(j, j, 10), cells(j, j, 9), A.max, ["pad", "pb%d" % (j - 1)], ["q1"], True)
+            tasks["p%d" % j] = (64, ["x%d" % j] if j else [])
+            calls["p%d" % j] = lambda j=j: scan(T.pb[:, 36 * j + 4:36 * j + 36], (T.q1 if j else T.q0)[:], T.tb[:, j:256:8], LOW,
+                                                ["tb", "q1" if j else "q0"], ["pb%d" % j])
+        for ja, jb in BATCHES:
+            a, b = 9 * ja + 1, 9 * jb + 9
+            src = ["pad"] + ["pb%d" % j for j in range(ja - 1, jb + 1)]
+            cost = max(64, 2 * (b - a))
+            tasks["m%d" % ja] = (cost, ["p%d" % jb])
+            calls["m%d" % ja] = lambda ja=ja, jb=jb, a=a, b=b, src=src: tt(T.du[:, a:b], cells(ja, jb, 10), cells(ja, jb, 1), A.max, src, ["du%d" % ja], True)
+            tasks["d%d" % ja] = (cost, ["p%d" % jb])
+            calls["d%d" % ja] = lambda ja=ja, jb=jb, a=a, b=b, src=src: tt(T.km[:, 2 * a:2 * b:2], cells(ja, jb, 1), cells(ja, jb, 10), A.is_gt, src, ["kd%d" % ja], True)
+            tasks["l%d" % ja] = (cost, ["m%d" % ja])
+            calls["l%d" % ja] = lambda ja=ja, jb=jb, a=a, b=b, src=src: tt(T.km[:, 2 * a + 1:2 * b:2], T.du[:, a:b], cells(ja, jb, 9), A.is_ge, src + ["du%d" % ja], ["kl%d" % ja], True)
+            for j in range(ja, jb + 1):
+                tasks["g%d" % j] = (85, ["d%d" % ja, "l%d" % ja] + (["h%d" % (j - 1)] if j > 1 else []))
+                calls["g%d" % j] = lambda j=j, ja=ja: tt(T.hx[:], T.hb[:, 24 * j - 24:24 * j].indirect(T.lh[:, 0:1]), T.km[:, 18 * j + 2:18 * j + 18], A.subtract,
+                                                         ["hbz", "hb%d" % (j - 1), "lh", "kd%d" % ja, "kl%d" % ja], ["hx"], True)
+                tasks["h%d" % j] = (64, ["g%d" % j])
+                calls["h%d" % j] = lambda j=j: scan(T.hb[:, 24 * j + 8:24 * j + 24], T.hx[:], T.jw[:, 16 * j:16 * j + 16], -2.0, ["hx", "hbz"] + jws, ["hb%d" % j])
+        for n in interleave(tasks):
+            calls[n]()
+        n = 8 * nm
+        ts(T.fl[:, 0:n], T.ec[:, at:at + nm, :], path, -0.5, A.mult, A.add, ["hb7"] + ecs, ["fl"])
+        ts(T.dg[:, 0:n], T.fl[:, 0:n], 7, None, A.bitwise_and, None, ["fl"], ["dg"])
+        copy(T.xt[:, xo:xo + n], T.dg[:, 0:n], ["dg"], xw)
+        quant(T.xq[:], T.xsc[:], T.xt[:, xo:xo + 512], xkeys, ["xq"])
+        mm(5, 128, T.stq[:], T.sts[:], T.xq[:], T.xsc[:], ["stq", "xq"])
+        close("v")
+
+    def offsets(out, n, okey):
+        ts(out[:], bank[5][:, 0:n], col(3), None, A.add, None, ["b5", "ff"], [okey])
+
+    def masked(k, a, n, m, at, key):
+        tt(T.gm[:, at:at + n], bank[k][:, a:a + n], T.mk[:, m:m + n], A.mult, ["b%d" % k, "mk"], [key])
+
+    def blend(at, n, win, lst, da, rd, wr):
+        tt(T.mt[:, at:at + n], win.indirect(lst), da, A.add, rd, wr)
+
+    L = ["lin", "lown"]
+    mm(4, 128, T.lq[:, 192:320], T.ls[:, 192:320], T.lq[:, 0:128], T.ls[:, 0:128], L)
+    mm(5, 128, T.lq[:, 256:384], T.ls[:, 256:384], T.lq[:, 64:192], T.ls[:, 64:192], L)
+    decode(384, T.lq[:], T.ls[:], L)
+    masked(4, 0, 128, 0, 0, "gm1")
+    masked(5, 64, 64, 64, 192, "gm2")
+    op("s", lambda: g.sync.dma_start(T.wt[:], T.w[:]), r=["lin"], w=["wt"], dma=True)
+    close("s")
+    for b in range(4):
+        act(T.d0[:, b:1536:4], bank[b][:, 0:384], ["b%d" % b], ["d0%d" % b], scale=0.5)
+    close("a")
+    D0 = ["d0%d" % b for b in range(4)]
+    align(T.l0, "l0", 4, 0, 16, 0, XA, ["xt0"])
+    ts(T.flu[:], T.ec[:, 24:32, :], path, -0.5, A.mult, A.add, ["hb7"] + ecs, ["flu"])
+    close("v")
+    offsets(T.o0, 32, "o0")
+    close("v")
+    ts(T.dgu[:], T.flu[:], 7, None, A.bitwise_and, None, ["flu"], ["dgu"])
+    close("v")
+    blend(0, 512, T.d0[:, 768:1536], T.o0[:], T.d0[:, 256:768], D0 + ["o0"], ["mt0", "mt1"])
+    quant(T.m0q[:], T.m0s[:], T.mt[:], ["mt0", "mt1"], ["m0"])
+    close("v")
+    copy(T.xt[:, 576:640], T.dgu[:], ["dgu", "xt4"], ["xu"])
+    close("v")
+
+    ha1 = 1 - hb1
+    mm(4, 128, T.m0q[:], T.m0s[:], T.m0q[:], T.m0s[:], ["m0"])
+    decode(128, T.m0q[:], T.m0s[:], ["m0"])
+    masked(4, 64 * ha1, 64, 64 * hb1, 64 * hb1, "gm1")
+    for b in range(4):
+        act(T.d1[:, b:512:4], bank[b][:, 0:128], ["b%d" % b], ["d1%d" % b], scale=0.5)
+    close("a")
+    D1 = ["d1%d" % b for b in range(4)]
+    win1 = T.d1[:, 256 * hb1:256 * hb1 + 256]
+    align(T.l1, "l1", 8, 16, 8, 512, XB + ["xu"], ["xt4"])
+    offsets(T.o1, 32, "o1")
+    blend(0, 128, win1, T.o1[:, 0:8], T.d1[:, 256 * ha1:256 * ha1 + 128], D1 + ["o1"], ["mt0"])
+    quant(T.m1q[:], T.m1s[:], T.mt[:], ["mt0", "mt1"], ["m1"])
+    close("v")
+    need("g", ["m1"])
+    (m8,), n8 = masks(c4, 1)
+    rid, pid = int(topo.addr(c4)[0]), int(topo.addr(c4)[1])
+    g.remote_dma(T.hq[:, 0:32].bitcast(dt.uint8), T.m1q[:, 0:32].bitcast(dt.uint8), T.sem.arr2, T.sem.sent, pid, rid, m8)
+    g.remote_dma(T.hs[:, 0:32], T.m1s[:, 0:32], T.sem.arr2, T.sem.sent, pid, rid, m8)
+    sent += 2 * n8
+    landed("hin", "arr2", 2 * n8)
+
+    blend(0, 128, win1, T.o1[:, 8:16], T.d1[:, 256 * ha1 + 128:256 * ha1 + 256], D1 + ["o1"], ["mt0"])
+    blend(128, 256, T.d0[:, 768:1536], T.o1[:, 16:32], T.d0[:, 0:256], D0 + ["o1"], ["mt1"])
+    close("v")
+    fill(T.jt[:], 0.0, "jt")
+    close("v")
+    quant(T.hq[:, 32:160], T.hs[:, 32:160], T.mt[:], ["mt0", "mt1"], ["hown"])
+    close("v")
+    quant(T.wq[:], T.ws[:], T.wt[:], ["wt"], ["wq"])
+    close("v")
+    act(T.jt[:, 0:256:4], T.xt[:, 0:64], ["xt0", "jt"], ["j0"])
+    act(T.jt[:, 256:768:4], T.xt[:, 512:640], ["xt4", "xu", "jt"], ["j1"])
+    close("a")
+    quant(T.jq[:], T.js[:], T.jt[:, 0:768], ["j0", "j1"], ["jq"])
+    close("v")
+
+    def prod(o, q, s, rd):
+        mm(6 + o, 128, T.wq[:, 128 * o:128 * o + 128], T.ws[:, 128 * o:128 * o + 128], q, s, ["wq"] + rd)
+
+    pars = (1 - keep1, keep1)
+    for o in range(2):
+        prod(o, T.m0q[:], T.m0s[:], ["m0"])
+    for o in range(2):
+        for h in range(2):
+            act(T.y0[:, 4 * o:4 * o + 4, 2 * pars[h] + b1, :], bank[6 + o][:, 32 * h:32 * h + 32], ["b%d" % (6 + o)], ["y0k%d%d" % (o, h)])
+        close("a")
+    for o in range(2):
+        prod(o, T.m1q[:], T.m1s[:], ["m1"])
+    for o in range(2):
+        act(T.y1[:, 4 * o:4 * o + 4, 1 - keep1, :], bank[6 + o][:, 0:32], ["b%d" % (6 + o)], ["y1s%d" % o])
+        close("a")
+
+    qa2 = 1 - qb2
+    H = ["hin", "hown"]
+    mm(4, 128, T.hq[:, 0:128], T.hs[:, 0:128], T.hq[:, 0:128], T.hs[:, 0:128], H)
+    decode(128, T.hq[:, 0:128], T.hs[:, 0:128], H)
+    masked(4, 32 * qa2, 32, 32 * qb2, 32 * qb2, "gm1")
+    for b in range(4):
+        act(T.d2[:, b:256:4], bank[b][:, 0:64], ["b%d" % b], ["d2%d" % b], scale=0.5)
+    close("a")
+    for o in range(2):
+        prod(o, T.hq[:, 32:160], T.hs[:, 32:160], ["hown"])
+    mm(0, 192, T.stq[:], T.sts[:], T.jq[:], T.js[:], ["stq", "jq"])
+    for o in range(2):
+        act(T.y1[:, 4 * o:4 * o + 4, keep1, :], bank[6 + o][:, 0:32], ["b%d" % (6 + o)], ["y1k%d" % o])
+        for h in range(2):
+            act(T.y0[:, 4 * o:4 * o + 4, 2 * pars[h] + 1 - b1, :], bank[6 + o][:, 32 + 32 * h:64 + 32 * h], ["b%d" % (6 + o)], ["y0u%d%d" % (o, h)])
+        close("a")
+        store("s", T.y[:, 224 * o:224 * o + 128], T.y0[:, 4 * o:4 * o + 4, :, :], ["y0%s%d%d" % (u, o, h) for u in "ku" for h in range(2)])
+        store("s", T.y[:, 224 * o + 128:224 * o + 192], T.y1[:, 4 * o:4 * o + 4, :, :], ["y1k%d" % o, "y1s%d" % o])
+    for h in range(2):
+        act(T.p0[0:1, :, 2 * pars[h] + b1, :], bank[0][0:1, 32 * h:32 * h + 32], ["b0"], ["p0k%d" % h], scale=0.25)
+        act(T.p1[0:1, :, pars[h], :], bank[0][0:1, 64 + 32 * h:96 + 32 * h], ["b0"], ["p1%d" % h], scale=0.25)
+        act(T.p0[0:1, :, 2 * pars[h] + 1 - b1, :], bank[0][0:1, 128 + 32 * h:160 + 32 * h], ["b0"], ["p0u%d" % h], scale=0.25)
+    close("a")
+    store("g", T.pt[0:1, 0:128], T.p0[0:1, :, :, :], ["p0k0", "p0k1", "p0u0", "p0u1"])
+    store("g", T.pt[0:1, 128:192], T.p1[0:1, :, :, :], ["p10", "p11"])
+    align(T.l1, "l1", 8, 32, 4, 128, XA + ["xt4", "xu"], ["xt1"])
+    act(T.jt[:, 768:896:4], T.xt[:, 128:160], ["xt1", "jt"], ["j3"])
+    close("a")
+    D2 = ["d2%d" % b for b in range(4)]
+    offsets(T.o2, 8, "o2")
+    blend(0, 128, T.d2[:, 128 * qb2:128 * qb2 + 128], T.o2[:], T.d2[:, 128 * qa2:128 * qa2 + 128], D2 + ["o2"], ["mt0"])
+    quant(T.m2q[:], T.m2s[:], T.mt[:], ["mt0", "mt1"], ["m2"])
+    close("v")
+    quant(T.j2q[:], T.j2s[:], T.jt[:, 384:896], ["j1", "j3"], ["j2q"])
+    close("v")
+    for o in range(2):
+        prod(o, T.m2q[:], T.m2s[:], ["m2"])
+    mm(0, 128, T.stq[:], T.sts[:], T.j2q[:], T.j2s[:], ["stq", "j2q"])
+    store("s", T.oc[:, 0:128], T.m2q[:, 0:32].bitcast(dt.uint8), ["m2"])
+    for k in range(4):
+        store("sg"[k % 2], T.osc[4 * k:4 * k + 4, 0:32], T.m2s[32 * k:32 * k + 4, 0:32], ["m2"])
+    copy(T.y2[:, 0:32], bank[6][:, 0:32], ["b6"], ["y20"])
+    close("v")
+    act(T.y2[:, 32:64], bank[7][:, 0:32], ["b7"], ["y21"])
+    close("a")
+    ts(T.p2[0:1, :], bank[0][0:1, 96:128], 0.25, None, A.mult, None, ["b0"], ["p2"])
+    store("s", T.y[:, 192:224], T.y2[:, 0:32], ["y20"])
+    store("a", T.y[:, 416:448], T.y2[:, 32:64], ["y21"])
+    store("g", T.pt[0:1, 192:224], T.p2[0:1, :], ["p2"])
+    g.wait_ge(T.sem.sent, sent)
+    finish()

@@ -5,8 +5,8 @@ F32, BF, I32, U16, X4, U8 = "float32", "bfloat16", "int32", "uint16", "float8_e4
 LOW = -1.0e29
 UNIT = 2.0 ** -22
 HDIAG = sum(i * 8 ** (i - 1) for i in range(1, 8)) + 0.5
-BATCHES = ((1, 3), (4, 5), (6, 7))
-GAP = 70
+BATCHES = tuple((j, j) for j in range(1, 8))
+GAP = 200
 
 
 def _sb(shape, d):
@@ -25,13 +25,13 @@ SCRATCH = {
     "l0": _sb([4], U16), "l1": _sb([2], U16), "lh": _sb([2], U16),
     "part": _sb([36], F32), "row": _sb([36, 8], F32), "ec": _sb([36, 8], F32), "kj": _sb([8], F32),
     "gm": _sb([256], F32), "gb": _sb([256], F32), "tb": _sb([256], F32),
-    "pb": _sb([288], F32), "q0": _sb([32], F32), "q1": _sb([32], F32), "du": _sb([72], F32), "km": _sb([144], F32),
-    "hb": _sb([192], F32), "hx": _sb([16], F32), "jw": _sb([128], F32),
+    "pb": _sb([288], F32), "q0": _sb([32], F32), "q1": _sb([32], F32), "du": _sb([72], F32), "dv": _sb([24], F32),
+    "km": _sb([144], F32), "hb": _sb([192], F32), "hx": _sb([16], F32), "jw": _sb([128], F32),
     "fl": _sb([128], I32), "dg": _sb([128], I32), "flu": _sb([64], I32), "dgu": _sb([64], I32),
     "xq": _sb([128], X4), "xsc": _sb([128], U8),
     "o0": _sb([32], U16), "o1": _sb([32], U16), "o2": _sb([8], U16),
     "d0": _sb([1536], F32), "d1": _sb([512], F32), "d2": _sb([256], F32),
-    "mt": _sb([512], BF),
+    "mt": _sb([512], BF), "mu": _sb([512], BF),
     "m0q": _sb([128], X4), "m0s": _sb([128], U8), "m1q": _sb([128], X4), "m1s": _sb([128], U8),
     "hq": _sb([160], X4), "hs": _sb([160], U8), "m2q": _sb([128], X4), "m2s": _sb([128], U8),
     "jt": _sb([896], BF), "jq": _sb([192], X4), "js": _sb([192], U8), "j2q": _sb([128], X4), "j2s": _sb([128], U8),
@@ -131,7 +131,8 @@ def interleave(tasks):
     while len(order) < len(tasks):
         cand = [n for n in tasks if n not in done and all(d in done for d in tasks[n][1])]
         at = {n: max([now] + [done[d] + GAP for d in tasks[n][1]]) for n in cand}
-        n = min(cand, key=lambda m: (at[m], -tail[m]))
+        first = min(at.values())
+        n = min(cand, key=lambda m: (at[m] > first + 20, -tail[m]))
         now = at[n] + tasks[n][0]
         done[n] = now
         order.append(n)
@@ -166,11 +167,11 @@ def rank_program(g, core, T, topo):
     def fill(out, val, key, rd=()):
         op("v", lambda: V.memset(out, val), r=rd, w=[key])
 
-    def ts(out, in0, s1, s2, o0, o1, rd, wr):
+    def ts(out, in0, s1, s2, o0, o1, rd, wr, cut=False):
         if o1 is None:
-            op("v", lambda: V.tensor_scalar(out, in0, s1, None, o0), r=rd, w=wr)
+            op("v", lambda: V.tensor_scalar(out, in0, s1, None, o0), r=rd, w=wr, cut=cut)
         else:
-            op("v", lambda: V.tensor_scalar(out, in0, s1, s2, o0, o1), r=rd, w=wr)
+            op("v", lambda: V.tensor_scalar(out, in0, s1, s2, o0, o1), r=rd, w=wr, cut=cut)
 
     def tt(out, in0, in1, o, rd, wr, cut=False):
         op("v", lambda: V.tensor_tensor(out, in0, in1, o), r=rd, w=wr, cut=cut)
@@ -197,7 +198,7 @@ def rank_program(g, core, T, topo):
         op("t", lambda: PE.matmul_mx(bank[k][:, 0:n], lq, ls, rq, rs, True, True), r=rd, w=["b%d" % k], cut=True)
 
     def store(q, out, in_, rd):
-        eng = {"s": g.sync, "a": S, "g": g}[q]
+        eng = {"s": g.sync, "a": S}[q]
         op(q, lambda: eng.dma_start(out, in_), r=rd, dma=True)
 
     op("s", lambda: g.sync.dma_start(T.xs[:], T.x[:]), w=["xs"], dma=True)
@@ -225,6 +226,7 @@ def rank_program(g, core, T, topo):
     afill(T.q1[:], 32, LOW, "q1")
     afill(T.hb[:], 192, -2.0, "hbz")
     afill(T.jw[:], 128, 0.0, "jw")
+    afill(T.mu[:, 384:512], 128, 0.0, "muz")
     act(T.q0[:, 0:1], T.zz[:, 0:1], ["zz"], ["q0"], scale=0.0, bias=0.0)
     act(T.hb[:, 8:24], T.zz[:, 0:16], ["zz", "hbz"], ["hb0"], scale=0.0, bias=-0.5 * UNIT)
     for i in range(1, 8):
@@ -235,17 +237,18 @@ def rank_program(g, core, T, topo):
     own = 192 * b0
     keep1 = b2
     order = [4 * par + (r ^ k) % 4 for k in (3, 1, 2, 0) for par in (1 - keep1, keep1)]
-    for k in (4, 5):
+    for k in (6, 7):
         act(T.xt[:, 128 * k:128 * k + 128], T.xs[:, :, order[k], :], ["xs"], ["xt%d" % k])
     close("a")
     for k in (0, 1, 2, 3):
         copy(T.xt[:, 128 * k:128 * k + 128], T.xs[:, :, order[k], :], ["xs"], ["xt%d" % k])
     close("v")
-    for k in (6, 7):
+    for k in (4, 5):
         copy(T.xt[:, 128 * k:128 * k + 128], T.xs[:, :, order[k], :], ["xs"], ["xt%d" % k])
     close("v")
     XA, XB = ["xt0", "xt1", "xt2", "xt3"], ["xt4", "xt5", "xt6", "xt7"]
     quant(T.sq[:], T.ss[:], T.xt[:, 0:512], XA, ["sq"])
+    close("v")
     quant(T.lq[:, own:own + 128], T.ls[:, own:own + 128], T.xt[:, 512:1024], XB, ["lown"])
     close("v")
     need("g", ["sq", "lown"])
@@ -295,10 +298,12 @@ def rank_program(g, core, T, topo):
     close("v")
     ts(col(14), col(3), 8.0, col(12), A.mult, A.add, ["ff", "f12"], ["f14"])
     ts(T.l1[:], T.c4[:], col(13), None, A.add, None, ["c4", "f13"], ["l1"])
+    close("v")
+    fill(T.ec[:, :, 0], 0.0, "ec0")
+    close("v")
     ts(T.l0[:], T.c2[:], col(14), None, A.add, None, ["c2", "f14"], ["l0"])
     close("v")
     parts = ["part%d" % k for k in range(5)]
-    fill(T.ec[:, :, 0], 0.0, "ec0")
     for i in range(1, 8):
         ts(T.ec[:, :, i], T.part[:], col(6), -8.0 ** (1 - i) / UNIT, A.is_equal, A.mult, parts + ["ff"], ["ec%d" % i])
     for t in range(4):
@@ -312,6 +317,9 @@ def rank_program(g, core, T, topo):
     close("v")
     quant(T.stq[:], T.sts[:], T.st[:], ["st0", "st1", "st2", "st3"], ["stq"])
     close("v")
+    for k in range(4):
+        afill(T.jt[:, 224 * k:224 * k + 224], 224, 0.0, "jt")
+    close("a")
     jws = ["jw"] + ["jw%d" % i for i in range(1, 8)]
     path = T.hb[:, 191:192]
 
@@ -327,47 +335,68 @@ def rank_program(g, core, T, topo):
         copy(T.gb[:, 2:256:step], T.gm[:].indirect(lst[:]), ["gm1", "gm2", "gmz", lkey], ["gb"])
         op("v", lambda: V.transpose(T.tb[:], T.gb[:]), r=["gb"], w=["tb"])
         tasks, calls = {}, {}
+
+        def task(name, cost, needs, fn):
+            tasks[name] = (cost, needs)
+            calls[name] = fn
+
         for j in range(8):
             if j:
-                tasks["x%d" % j] = (64, ["p%d" % (j - 1)])
-                calls["x%d" % j] = lambda j=j: tt(T.q1[:, 0:32:4], cells(j, j, 10), cells(j, j, 9), A.max, ["pad", "pb%d" % (j - 1)], ["q1"], True)
-            tasks["p%d" % j] = (64, ["x%d" % j] if j else [])
-            calls["p%d" % j] = lambda j=j: scan(T.pb[:, 36 * j + 4:36 * j + 36], (T.q1 if j else T.q0)[:], T.tb[:, j:256:8], LOW,
-                                                ["tb", "q1" if j else "q0"], ["pb%d" % j])
+                task("x%d" % j, 64, ["p%d" % (j - 1)], lambda j=j: tt(T.q1[:, 0:32:4], cells(j, j, 10), cells(j, j, 9), A.max, ["pad", "pb%d" % (j - 1)], ["q1"], True))
+            task("p%d" % j, 64, ["x%d" % j] if j else [],
+                 lambda j=j: scan(T.pb[:, 36 * j + 4:36 * j + 36], (T.q1 if j else T.q0)[:], T.tb[:, j:256:8], LOW, ["tb", "q1" if j else "q0"], ["pb%d" % j]))
         for ja, jb in BATCHES:
             a, b = 9 * ja + 1, 9 * jb + 9
             src = ["pad"] + ["pb%d" % j for j in range(ja - 1, jb + 1)]
             cost = max(64, 2 * (b - a))
-            tasks["m%d" % ja] = (cost, ["p%d" % jb])
-            calls["m%d" % ja] = lambda ja=ja, jb=jb, a=a, b=b, src=src: tt(T.du[:, a:b], cells(ja, jb, 10), cells(ja, jb, 1), A.max, src, ["du%d" % ja], True)
-            tasks["d%d" % ja] = (cost, ["p%d" % jb])
-            calls["d%d" % ja] = lambda ja=ja, jb=jb, a=a, b=b, src=src: tt(T.km[:, 2 * a:2 * b:2], cells(ja, jb, 1), cells(ja, jb, 10), A.is_gt, src, ["kd%d" % ja], True)
-            tasks["l%d" % ja] = (cost, ["m%d" % ja])
-            calls["l%d" % ja] = lambda ja=ja, jb=jb, a=a, b=b, src=src: tt(T.km[:, 2 * a + 1:2 * b:2], T.du[:, a:b], cells(ja, jb, 9), A.is_ge, src + ["du%d" % ja], ["kl%d" % ja], True)
+            kl = T.km[:, 2 * a + 1:2 * b:2]
+            if ja == 7:
+                task("a7", 64, ["p6"], lambda: tt(T.dv[:, 0:8], cells(7, 7, 10), cells(7, 7, 9), A.is_ge, ["pad", "pb6"], ["dv0"], True))
+                task("b7", 64, ["a7"], lambda: ts(T.dv[:, 8:16], T.dv[:, 0:8], LOW, None, A.mult, None, ["dv0"], ["dv1"], True))
+                task("c7", 64, ["b7"], lambda: tt(T.dv[:, 16:24], T.dv[:, 8:16], cells(7, 7, 9), A.add, ["dv1", "pb6"], ["dv2"], True))
+                task("l7", 64, ["c7", "p7"], lambda kl=kl: tt(kl, cells(7, 7, 1), T.dv[:, 16:24], A.is_ge, ["pad", "pb7", "dv2"], ["kl7"], True))
+            else:
+                task("m%d" % ja, cost, ["p%d" % jb], lambda ja=ja, jb=jb, a=a, b=b, src=src: tt(T.du[:, a:b], cells(ja, jb, 10), cells(ja, jb, 1), A.max, src, ["du%d" % ja], True))
+                task("l%d" % ja, cost, ["m%d" % ja], lambda ja=ja, jb=jb, a=a, b=b, src=src, kl=kl: tt(kl, T.du[:, a:b], cells(ja, jb, 9), A.is_ge, src + ["du%d" % ja], ["kl%d" % ja], True))
+            task("d%d" % ja, cost, ["p%d" % jb], lambda ja=ja, jb=jb, a=a, b=b, src=src: tt(T.km[:, 2 * a:2 * b:2], cells(ja, jb, 1), cells(ja, jb, 10), A.is_gt, src, ["kd%d" % ja], True))
             for j in range(ja, jb + 1):
-                tasks["g%d" % j] = (85, ["d%d" % ja, "l%d" % ja] + (["h%d" % (j - 1)] if j > 1 else []))
-                calls["g%d" % j] = lambda j=j, ja=ja: tt(T.hx[:], T.hb[:, 24 * j - 24:24 * j].indirect(T.lh[:, 0:1]), T.km[:, 18 * j + 2:18 * j + 18], A.subtract,
-                                                         ["hbz", "hb%d" % (j - 1), "lh", "kd%d" % ja, "kl%d" % ja], ["hx"], True)
-                tasks["h%d" % j] = (64, ["g%d" % j])
-                calls["h%d" % j] = lambda j=j: scan(T.hb[:, 24 * j + 8:24 * j + 24], T.hx[:], T.jw[:, 16 * j:16 * j + 16], -2.0, ["hx", "hbz"] + jws, ["hb%d" % j])
+                task("g%d" % j, 85, ["d%d" % ja, "l%d" % ja] + (["h%d" % (j - 1)] if j > 1 else []),
+                     lambda j=j, ja=ja: tt(T.hx[:], T.hb[:, 24 * j - 24:24 * j].indirect(T.lh[:, 0:1]), T.km[:, 18 * j + 2:18 * j + 18], A.subtract,
+                                           ["hbz", "hb%d" % (j - 1), "lh", "kd%d" % ja, "kl%d" % ja], ["hx"], True))
+                task("h%d" % j, 64, ["g%d" % j],
+                     lambda j=j: scan(T.hb[:, 24 * j + 8:24 * j + 24], T.hx[:], T.jw[:, 16 * j:16 * j + 16], -2.0, ["hx", "hbz"] + jws, ["hb%d" % j]))
         for n in interleave(tasks):
             calls[n]()
         n = 8 * nm
         ts(T.fl[:, 0:n], T.ec[:, at:at + nm, :], path, -0.5, A.mult, A.add, ["hb7"] + ecs, ["fl"])
+        close("v")
+        if at == 0:
+            ts(T.flu[:], T.ec[:, 24:32, :], path, -0.5, A.mult, A.add, ["hb7"] + ecs, ["flu"])
+            close("v")
         ts(T.dg[:, 0:n], T.fl[:, 0:n], 7, None, A.bitwise_and, None, ["fl"], ["dg"])
+        close("v")
+        if at == 0:
+            ts(T.dgu[:], T.flu[:], 7, None, A.bitwise_and, None, ["flu"], ["dgu"])
+            close("v")
         copy(T.xt[:, xo:xo + n], T.dg[:, 0:n], ["dg"], xw)
+        close("v")
+        if at == 0:
+            copy(T.xt[:, 576:640], T.dgu[:], ["dgu", "xt4"], ["xu"])
+            close("v")
         quant(T.xq[:], T.xsc[:], T.xt[:, xo:xo + 512], xkeys, ["xq"])
         mm(5, 128, T.stq[:], T.sts[:], T.xq[:], T.xsc[:], ["stq", "xq"])
         close("v")
 
     def offsets(out, n, okey):
         ts(out[:], bank[5][:, 0:n], col(3), None, A.add, None, ["b5", "ff"], [okey])
+        close("v")
 
     def masked(k, a, n, m, at, key):
         tt(T.gm[:, at:at + n], bank[k][:, a:a + n], T.mk[:, m:m + n], A.mult, ["b%d" % k, "mk"], [key])
 
-    def blend(at, n, win, lst, da, rd, wr):
-        tt(T.mt[:, at:at + n], win.indirect(lst), da, A.add, rd, wr)
+    def blend(tile, at, n, win, lst, da, rd, wr):
+        tt(tile[:, at:at + n], win.indirect(lst), da, A.add, rd, wr)
+        close("v")
 
     L = ["lin", "lown"]
     mm(4, 128, T.lq[:, 192:320], T.ls[:, 192:320], T.lq[:, 0:128], T.ls[:, 0:128], L)
@@ -382,31 +411,41 @@ def rank_program(g, core, T, topo):
     close("a")
     D0 = ["d0%d" % b for b in range(4)]
     align(T.l0, "l0", 4, 0, 16, 0, XA, ["xt0"])
-    ts(T.flu[:], T.ec[:, 24:32, :], path, -0.5, A.mult, A.add, ["hb7"] + ecs, ["flu"])
+    quant(T.wq[:], T.ws[:], T.wt[:], ["wt"], ["wq"])
     close("v")
     offsets(T.o0, 32, "o0")
-    close("v")
-    ts(T.dgu[:], T.flu[:], 7, None, A.bitwise_and, None, ["flu"], ["dgu"])
-    close("v")
-    blend(0, 512, T.d0[:, 768:1536], T.o0[:], T.d0[:, 256:768], D0 + ["o0"], ["mt0", "mt1"])
-    quant(T.m0q[:], T.m0s[:], T.mt[:], ["mt0", "mt1"], ["m0"])
-    close("v")
-    copy(T.xt[:, 576:640], T.dgu[:], ["dgu", "xt4"], ["xu"])
+    blend(T.mt, 0, 512, T.d0[:, 768:1536], T.o0[:], T.d0[:, 256:768], D0 + ["o0"], ["mt0"])
+    quant(T.m0q[:], T.m0s[:], T.mt[:], ["mt0"], ["m0"])
     close("v")
 
+    def prod(o, q, s, rd):
+        mm(6 + o, 128, T.wq[:, 128 * o:128 * o + 128], T.ws[:, 128 * o:128 * o + 128], q, s, ["wq"] + rd)
+
     ha1 = 1 - hb1
+    pars = (1 - keep1, keep1)
     mm(4, 128, T.m0q[:], T.m0s[:], T.m0q[:], T.m0s[:], ["m0"])
     decode(128, T.m0q[:], T.m0s[:], ["m0"])
+    for o in range(2):
+        prod(o, T.m0q[:], T.m0s[:], ["m0"])
     masked(4, 64 * ha1, 64, 64 * hb1, 64 * hb1, "gm1")
     for b in range(4):
         act(T.d1[:, b:512:4], bank[b][:, 0:128], ["b%d" % b], ["d1%d" % b], scale=0.5)
     close("a")
+    for o in range(2):
+        for h in range(2):
+            act(T.y0[:, 4 * o:4 * o + 4, 2 * pars[h] + b1, :], bank[6 + o][:, 32 * h:32 * h + 32], ["b%d" % (6 + o)], ["y0k%d%d" % (o, h)])
+        close("a")
+    act(T.jt[:, 0:256:4], T.xt[:, 0:64], ["xt0", "jt"], ["j0"])
+    close("a")
     D1 = ["d1%d" % b for b in range(4)]
     win1 = T.d1[:, 256 * hb1:256 * hb1 + 256]
     align(T.l1, "l1", 8, 16, 8, 512, XB + ["xu"], ["xt4"])
+    act(T.jt[:, 256:768:4], T.xt[:, 512:640], ["xt4", "xu", "jt"], ["j1"])
+    close("a")
     offsets(T.o1, 32, "o1")
-    blend(0, 128, win1, T.o1[:, 0:8], T.d1[:, 256 * ha1:256 * ha1 + 128], D1 + ["o1"], ["mt0"])
-    quant(T.m1q[:], T.m1s[:], T.mt[:], ["mt0", "mt1"], ["m1"])
+    blend(T.mt, 0, 128, win1, T.o1[:, 0:8], T.d1[:, 256 * ha1:256 * ha1 + 128], D1 + ["o1"], ["mt0"])
+    blend(T.mu, 0, 128, win1, T.o1[:, 8:16], T.d1[:, 256 * ha1 + 128:256 * ha1 + 256], D1 + ["o1"], ["mu0"])
+    quant(T.m1q[:], T.m1s[:], T.mt[:], ["mt0"], ["m1"])
     close("v")
     need("g", ["m1"])
     (m8,), n8 = masks(c4, 1)
@@ -416,85 +455,66 @@ def rank_program(g, core, T, topo):
     sent += 2 * n8
     landed("hin", "arr2", 2 * n8)
 
-    blend(0, 128, win1, T.o1[:, 8:16], T.d1[:, 256 * ha1 + 128:256 * ha1 + 256], D1 + ["o1"], ["mt0"])
-    blend(128, 256, T.d0[:, 768:1536], T.o1[:, 16:32], T.d0[:, 0:256], D0 + ["o1"], ["mt1"])
-    close("v")
-    fill(T.jt[:], 0.0, "jt")
-    close("v")
-    quant(T.hq[:, 32:160], T.hs[:, 32:160], T.mt[:], ["mt0", "mt1"], ["hown"])
-    close("v")
-    quant(T.wq[:], T.ws[:], T.wt[:], ["wt"], ["wq"])
-    close("v")
-    act(T.jt[:, 0:256:4], T.xt[:, 0:64], ["xt0", "jt"], ["j0"])
-    act(T.jt[:, 256:768:4], T.xt[:, 512:640], ["xt4", "xu", "jt"], ["j1"])
-    close("a")
+    blend(T.mu, 128, 256, T.d0[:, 768:1536], T.o1[:, 16:32], T.d0[:, 0:256], D0 + ["o1"], ["mu1"])
     quant(T.jq[:], T.js[:], T.jt[:, 0:768], ["j0", "j1"], ["jq"])
     close("v")
-
-    def prod(o, q, s, rd):
-        mm(6 + o, 128, T.wq[:, 128 * o:128 * o + 128], T.ws[:, 128 * o:128 * o + 128], q, s, ["wq"] + rd)
-
-    pars = (1 - keep1, keep1)
-    for o in range(2):
-        prod(o, T.m0q[:], T.m0s[:], ["m0"])
-    for o in range(2):
-        for h in range(2):
-            act(T.y0[:, 4 * o:4 * o + 4, 2 * pars[h] + b1, :], bank[6 + o][:, 32 * h:32 * h + 32], ["b%d" % (6 + o)], ["y0k%d%d" % (o, h)])
-        close("a")
+    quant(T.hq[:, 32:160], T.hs[:, 32:160], T.mu[:], ["mu0", "mu1", "muz"], ["hown"])
+    close("v")
     for o in range(2):
         prod(o, T.m1q[:], T.m1s[:], ["m1"])
+    mm(0, 192, T.stq[:], T.sts[:], T.jq[:], T.js[:], ["stq", "jq"])
     for o in range(2):
         act(T.y1[:, 4 * o:4 * o + 4, 1 - keep1, :], bank[6 + o][:, 0:32], ["b%d" % (6 + o)], ["y1s%d" % o])
         close("a")
+    for o in range(2):
+        prod(o, T.hq[:, 32:160], T.hs[:, 32:160], ["hown"])
+    for h in range(2):
+        act(T.p0[0:1, :, 2 * pars[h] + b1, :], bank[0][0:1, 32 * h:32 * h + 32], ["b0"], ["p0k%d" % h], scale=0.25)
+        act(T.p1[0:1, :, pars[h], :], bank[0][0:1, 64 + 32 * h:96 + 32 * h], ["b0"], ["p1%d" % h], scale=0.25)
+        act(T.p0[0:1, :, 2 * pars[h] + 1 - b1, :], bank[0][0:1, 128 + 32 * h:160 + 32 * h], ["b0"], ["p0u%d" % h], scale=0.25)
+    close("a")
 
     qa2 = 1 - qb2
     H = ["hin", "hown"]
     mm(4, 128, T.hq[:, 0:128], T.hs[:, 0:128], T.hq[:, 0:128], T.hs[:, 0:128], H)
     decode(128, T.hq[:, 0:128], T.hs[:, 0:128], H)
     masked(4, 32 * qa2, 32, 32 * qb2, 32 * qb2, "gm1")
-    for b in range(4):
-        act(T.d2[:, b:256:4], bank[b][:, 0:64], ["b%d" % b], ["d2%d" % b], scale=0.5)
-    close("a")
-    for o in range(2):
-        prod(o, T.hq[:, 32:160], T.hs[:, 32:160], ["hown"])
-    mm(0, 192, T.stq[:], T.sts[:], T.jq[:], T.js[:], ["stq", "jq"])
     for o in range(2):
         act(T.y1[:, 4 * o:4 * o + 4, keep1, :], bank[6 + o][:, 0:32], ["b%d" % (6 + o)], ["y1k%d" % o])
         for h in range(2):
             act(T.y0[:, 4 * o:4 * o + 4, 2 * pars[h] + 1 - b1, :], bank[6 + o][:, 32 + 32 * h:64 + 32 * h], ["b%d" % (6 + o)], ["y0u%d%d" % (o, h)])
         close("a")
+    for b in range(4):
+        act(T.d2[:, b:256:4], bank[b][:, 0:64], ["b%d" % b], ["d2%d" % b], scale=0.5)
+    close("a")
+    store("s", T.pt[0:1, 0:128], T.p0[0:1, :, :, :], ["p0k0", "p0k1", "p0u0", "p0u1"])
+    store("s", T.pt[0:1, 128:192], T.p1[0:1, :, :, :], ["p10", "p11"])
+    for o in range(2):
         store("s", T.y[:, 224 * o:224 * o + 128], T.y0[:, 4 * o:4 * o + 4, :, :], ["y0%s%d%d" % (u, o, h) for u in "ku" for h in range(2)])
         store("s", T.y[:, 224 * o + 128:224 * o + 192], T.y1[:, 4 * o:4 * o + 4, :, :], ["y1k%d" % o, "y1s%d" % o])
-    for h in range(2):
-        act(T.p0[0:1, :, 2 * pars[h] + b1, :], bank[0][0:1, 32 * h:32 * h + 32], ["b0"], ["p0k%d" % h], scale=0.25)
-        act(T.p1[0:1, :, pars[h], :], bank[0][0:1, 64 + 32 * h:96 + 32 * h], ["b0"], ["p1%d" % h], scale=0.25)
-        act(T.p0[0:1, :, 2 * pars[h] + 1 - b1, :], bank[0][0:1, 128 + 32 * h:160 + 32 * h], ["b0"], ["p0u%d" % h], scale=0.25)
-    close("a")
-    store("g", T.pt[0:1, 0:128], T.p0[0:1, :, :, :], ["p0k0", "p0k1", "p0u0", "p0u1"])
-    store("g", T.pt[0:1, 128:192], T.p1[0:1, :, :, :], ["p10", "p11"])
     align(T.l1, "l1", 8, 32, 4, 128, XA + ["xt4", "xu"], ["xt1"])
     act(T.jt[:, 768:896:4], T.xt[:, 128:160], ["xt1", "jt"], ["j3"])
     close("a")
+    quant(T.j2q[:], T.j2s[:], T.jt[:, 384:896], ["j1", "j3"], ["j2q"])
+    close("v")
+    mm(0, 128, T.stq[:], T.sts[:], T.j2q[:], T.j2s[:], ["stq", "j2q"])
+    act(T.p2[0:1, :], bank[0][0:1, 96:128], ["b0"], ["p2"], scale=0.25)
+    close("a")
+    store("s", T.pt[0:1, 192:224], T.p2[0:1, :], ["p2"])
     D2 = ["d2%d" % b for b in range(4)]
     offsets(T.o2, 8, "o2")
-    blend(0, 128, T.d2[:, 128 * qb2:128 * qb2 + 128], T.o2[:], T.d2[:, 128 * qa2:128 * qa2 + 128], D2 + ["o2"], ["mt0"])
-    quant(T.m2q[:], T.m2s[:], T.mt[:], ["mt0", "mt1"], ["m2"])
-    close("v")
-    quant(T.j2q[:], T.j2s[:], T.jt[:, 384:896], ["j1", "j3"], ["j2q"])
+    blend(T.mt, 0, 128, T.d2[:, 128 * qb2:128 * qb2 + 128], T.o2[:], T.d2[:, 128 * qa2:128 * qa2 + 128], D2 + ["o2"], ["mt0"])
+    quant(T.m2q[:], T.m2s[:], T.mt[:], ["mt0"], ["m2"])
     close("v")
     for o in range(2):
         prod(o, T.m2q[:], T.m2s[:], ["m2"])
-    mm(0, 128, T.stq[:], T.sts[:], T.j2q[:], T.j2s[:], ["stq", "j2q"])
     store("s", T.oc[:, 0:128], T.m2q[:, 0:32].bitcast(dt.uint8), ["m2"])
     for k in range(4):
-        store("sg"[k % 2], T.osc[4 * k:4 * k + 4, 0:32], T.m2s[32 * k:32 * k + 4, 0:32], ["m2"])
-    copy(T.y2[:, 0:32], bank[6][:, 0:32], ["b6"], ["y20"])
-    close("v")
-    act(T.y2[:, 32:64], bank[7][:, 0:32], ["b7"], ["y21"])
-    close("a")
-    ts(T.p2[0:1, :], bank[0][0:1, 96:128], 0.25, None, A.mult, None, ["b0"], ["p2"])
+        store("sa"[k % 2], T.osc[4 * k:4 * k + 4, 0:32], T.m2s[32 * k:32 * k + 4, 0:32], ["m2"])
+    for o in range(2):
+        copy(T.y2[:, 32 * o:32 * o + 32], bank[6 + o][:, 0:32], ["b%d" % (6 + o)], ["y2%d" % o])
+        close("v")
     store("s", T.y[:, 192:224], T.y2[:, 0:32], ["y20"])
     store("a", T.y[:, 416:448], T.y2[:, 32:64], ["y21"])
-    store("g", T.pt[0:1, 192:224], T.p2[0:1, :], ["p2"])
     g.wait_ge(T.sem.sent, sent)
     finish()

@@ -5,8 +5,8 @@ F32, BF, I32, U16, X4, U8 = "float32", "bfloat16", "int32", "uint16", "float8_e4
 LOW = -1.0e29
 UNIT = 2.0 ** -22
 HDIAG = sum(i * 8 ** (i - 1) for i in range(1, 8)) + 0.5
-BATCHES = tuple((j, j) for j in range(1, 8))
-GAP = 200
+ORDER = ("p0 s0 x1 s1 p1 s2 x2 d1 m1 p2 l1 x3 m2 g1 d2 p3 l2 h1 x4 m3 g2 d3 p4 l3 h2 x5 m4 g3 d4 p5 l4 h3 x6 m5 g4 d5 p6 "
+         "l5 h4 m6 x7 g5 d6 l6 p7 h5 m7 g6 d7 l7 h6 s3 g7 s4 h7").split()
 
 
 def _sb(shape, d):
@@ -20,12 +20,12 @@ SCRATCH = {
     "et": _sb([2048], BF), "eq": _sb([512], X4), "es": _sb([512], U8),
     "st": _sb([512], BF), "stq": _sb([128], X4), "sts": _sb([128], U8),
     "pi": _sb([2], I32), "fi": _sb([10], I32), "ff": _sb([20], F32),
-    "uu": _sb([128], F32), "vv": _sb([128], BF), "tt": _sb([128], BF), "zz": _sb([256], BF),
+    "uu": _sb([128], F32), "vv": _sb([128], BF), "tt": _sb([128], BF), "zz": _sb([288], BF),
     "mk": _sb([128], F32), "c2": _sb([4], F32), "c4": _sb([2], F32),
     "l0": _sb([4], U16), "l1": _sb([2], U16), "lh": _sb([2], U16),
     "part": _sb([36], F32), "row": _sb([36, 8], F32), "ec": _sb([36, 8], F32), "kj": _sb([8], F32),
     "gm": _sb([256], F32), "gb": _sb([256], F32), "tb": _sb([256], F32),
-    "pb": _sb([288], F32), "q0": _sb([32], F32), "q1": _sb([32], F32), "du": _sb([72], F32), "dv": _sb([24], F32),
+    "pb": _sb([288], F32), "q0": _sb([32], F32), "q1": _sb([32], F32), "du": _sb([72], F32),
     "km": _sb([144], F32), "hb": _sb([192], F32), "hx": _sb([16], F32), "jw": _sb([128], F32),
     "fl": _sb([128], I32), "dg": _sb([128], I32), "flu": _sb([64], I32), "dgu": _sb([64], I32),
     "xq": _sb([128], X4), "xsc": _sb([128], U8),
@@ -115,28 +115,12 @@ def make_order(g, T):
         for dma in (False, True):
             opened.pop((q, dma), None)
 
-    def finish():
+    def finish(q):
         for b in range(len(batches)):
             if not batches[b]["waited"]:
-                wait("g", b)
+                wait(q, b)
 
     return op, need, landed, close, finish
-
-
-def interleave(tasks):
-    tail = {}
-    for n in reversed(list(tasks)):
-        tail[n] = tasks[n][0] + max([GAP + tail[m] for m in tasks if n in tasks[m][1]] + [0])
-    done, order, now = {}, [], 0
-    while len(order) < len(tasks):
-        cand = [n for n in tasks if n not in done and all(d in done for d in tasks[n][1])]
-        at = {n: max([now] + [done[d] + GAP for d in tasks[n][1]]) for n in cand}
-        first = min(at.values())
-        n = min(cand, key=lambda m: (at[m] > first + 20, -tail[m]))
-        now = at[n] + tasks[n][0]
-        done[n] = now
-        order.append(n)
-    return order
 
 
 def rank_program(g, core, T, topo):
@@ -193,6 +177,7 @@ def rank_program(g, core, T, topo):
 
     def quant(q, s, tile, rd, wr):
         op("v", lambda: V.quantize_mx(q, s, tile), r=rd, w=wr)
+        close("v")
 
     def mm(k, n, lq, ls, rq, rs, rd):
         op("t", lambda: PE.matmul_mx(bank[k][:, 0:n], lq, ls, rq, rs, True, True), r=rd, w=["b%d" % k], cut=True)
@@ -204,18 +189,29 @@ def rank_program(g, core, T, topo):
     op("s", lambda: g.sync.dma_start(T.xs[:], T.x[:]), w=["xs"], dma=True)
     close("s")
 
+    hb1, qb2 = 1 - b1, 3 - b2
+    fill(T.zz[:], 0.0, "zz")
+    close("v")
+    act(T.row[0:1, :, :], T.zz[0:1, :], ["zz"], ["row"])
+    close("a")
     iota(T.pi[:, 0:1], [[0, 1]], 0, 1, "pi", small=False)
     close("g")
     iota(T.kj[:], [[1, 8]], 0, 0, "kj")
-    close("g")
     iota(T.vv[:], [[1, 128]], 0, -1, "vv")
-    close("g")
     iota(T.uu[:], [[1, 16], [0, 8]], 0, 0, "uu")
     iota(T.c2[:], [[2, 4]], 0, 0, "c2")
     iota(T.c4[:], [[4, 2]], 0, 0, "c4")
     close("g")
-    fill(T.zz[:], 0.0, "zz")
-    close("v")
+    segs = [(0, 16, [[16, 2], [32, 2], [4, 4]], 66), (16, 8, [[32, 2], [8, 4]], 64 * hb1 + 2),
+            (24, 8, [[32, 2], [4, 4]], 2), (32, 4, [[8, 4]], 32 * qb2 + 2)]
+    for k, (at, n, pat, base) in enumerate(segs):
+        iota(T.part[:, at:at + n], pat, base, 0, "part%d" % k)
+    need("g", ["row"])
+    iota(T.row[0:1, :, 1:8:4], [[0, 5], [1, 8], [0, 2]][0:0] + [[0, 72]], 0, 0, "r2") if False else None
+    iota(T.row[0:1, 0:32, 1:8:4], [[0, 4], [1, 8], [0, 2]], 0, 0, "r0")
+    iota(T.row[0:1, 0:16, 2:8:4], [[1, 2], [0, 16]], 1, 0, "r1")
+    iota(T.row[0:1, 32:36, 1:8:4], [[1, 4], [0, 2]], 0, 0, "r2")
+    close("g")
     fill(T.et[:], 0.0, "et")
     for k, (sh, m) in enumerate([(5, 3), (3, 1), (2, 1), (0, 3), (2, 3), (3, 15), (0, 127), (0, 15), (0, 1)]):
         ts(T.fi[:, k:k + 1], T.pi[:, 0:1], sh, m, A.logical_shift_right, A.bitwise_and, ["pi"], ["fi%d" % k])
@@ -226,11 +222,8 @@ def rank_program(g, core, T, topo):
     afill(T.q1[:], 32, LOW, "q1")
     afill(T.hb[:], 192, -2.0, "hbz")
     afill(T.jw[:], 128, 0.0, "jw")
-    afill(T.mu[:, 384:512], 128, 0.0, "muz")
     act(T.q0[:, 0:1], T.zz[:, 0:1], ["zz"], ["q0"], scale=0.0, bias=0.0)
     act(T.hb[:, 8:24], T.zz[:, 0:16], ["zz", "hbz"], ["hb0"], scale=0.0, bias=-0.5 * UNIT)
-    for i in range(1, 8):
-        act(T.jw[:, 2 * i:128:16], T.kj[:], ["kj", "jw"], ["jw%d" % i], scale=-UNIT * 8 ** (i - 1))
     close("a")
     close("v")
 
@@ -248,10 +241,8 @@ def rank_program(g, core, T, topo):
     close("v")
     XA, XB = ["xt0", "xt1", "xt2", "xt3"], ["xt4", "xt5", "xt6", "xt7"]
     quant(T.sq[:], T.ss[:], T.xt[:, 0:512], XA, ["sq"])
-    close("v")
     quant(T.lq[:, own:own + 128], T.ls[:, own:own + 128], T.xt[:, 512:1024], XB, ["lown"])
-    close("v")
-    need("g", ["sq", "lown"])
+    need("g", ["lown", "sq"])
     c1, c2, c3, c4 = (T.cores[r ^ k] for k in (1, 2, 3, 4))
     ms, ne = masks(c1, 4)
     for codes in (True, False):
@@ -264,21 +255,12 @@ def rank_program(g, core, T, topo):
     sent = 8 * ne
     landed("lin", "arr0", 8 * ne)
 
-    hb1, qb2 = 1 - b1, b2
-    segs = [(0, 8, [[32, 2], [4, 4]], 66), (8, 8, [[32, 2], [4, 4]], 82), (16, 8, [[32, 2], [8, 4]], 64 * hb1 + 2),
-            (24, 8, [[32, 2], [4, 4]], 2), (32, 4, [[8, 4]], 32 * qb2 + 2)]
-    for k, (at, n, pat, base) in enumerate(segs):
-        iota(T.part[:, at:at + n], pat, base, 0, "part%d" % k)
-    close("g")
-    iota(T.row[0:1, :, :], [[0, 288]], 0, 0, "row")
-    close("g")
     iota(T.tt[:], [[0, 8], [1, 4], [0, 4]], 0, 0, "tt")
     close("g")
-    need("g", ["row"])
-    iota(T.row[0:1, 0:32, 1:8:4], [[0, 4], [1, 8], [0, 2]], 0, 0, "r0")
-    iota(T.row[0:1, 0:16, 2:8:4], [[1, 2], [0, 16]], 1, 0, "r1")
-    iota(T.row[0:1, 32:36, 1:8:4], [[1, 4], [0, 2]], 0, 0, "r2")
-    close("g")
+    for i in range(1, 8):
+        act(T.jw[:, 2 * i:128:16], T.kj[:], ["kj", "jw"], ["jw%d" % i], scale=-UNIT * 8 ** (i - 1))
+    afill(T.mu[:, 0:128], 128, 0.0, "muz")
+    close("a")
     col = lambda k: T.ff[:, k:k + 1]
     copy(T.ff[:, 0:9], T.fi[:, 0:9], ["fi%d" % k for k in range(9)], ["ff"])
     close("v")
@@ -290,83 +272,82 @@ def rank_program(g, core, T, topo):
     ts(T.lh[:, 0:1], col(7), col(8), 7.0, A.add, A.add, ["ff"], ["lh"])
     close("v")
     ts(T.mk[:], T.uu[:], col(5), None, A.is_equal, None, ["uu", "ff"], ["mk"])
+    fill(T.ec[:, :, 0], 0.0, "ec0")
     close("v")
     ts(col(12), col(2), 128.0, col(10), A.mult, A.add, ["ff", "f10"], ["f12"])
     ts(col(13), col(3), 8.0, col(11), A.mult, A.add, ["ff", "f11"], ["f13"])
     close("v")
-    quant(T.eq[:], T.es[:], T.et[:], ["et0", "et1", "et2", "et3"], ["eq"])
-    close("v")
+    parts = ["part%d" % k for k in range(len(segs))]
+
+    def powers(lo, hi):
+        for i in range(lo, hi):
+            ts(T.ec[:, :, i], T.part[:], col(6), -8.0 ** (1 - i) / UNIT, A.is_equal, A.mult, parts + ["ff"], ["ec%d" % i])
+        close("v")
+
+    powers(1, 4)
     ts(col(14), col(3), 8.0, col(12), A.mult, A.add, ["ff", "f12"], ["f14"])
     ts(T.l1[:], T.c4[:], col(13), None, A.add, None, ["c4", "f13"], ["l1"])
     close("v")
-    fill(T.ec[:, :, 0], 0.0, "ec0")
-    close("v")
+    powers(4, 8)
     ts(T.l0[:], T.c2[:], col(14), None, A.add, None, ["c2", "f14"], ["l0"])
     close("v")
-    parts = ["part%d" % k for k in range(5)]
-    for i in range(1, 8):
-        ts(T.ec[:, :, i], T.part[:], col(6), -8.0 ** (1 - i) / UNIT, A.is_equal, A.mult, parts + ["ff"], ["ec%d" % i])
-    for t in range(4):
-        ts(T.st[:, t:512:4], T.tt[:], float(t), 4.0, A.is_equal, A.mult, ["tt"], ["st%d" % t])
-    close("v")
-    for t, val in enumerate((0.0, 32.0, 256.0, 0.0)):
-        fill(T.st[0:1, t:512:4], val, "st%d" % t)
-    close("v")
+    quant(T.eq[:], T.es[:], T.et[:], ["et0", "et1", "et2", "et3"], ["eq"])
     ecs = ["ec%d" % i for i in range(8)]
     ts(T.ec[0:1, :, :], T.row[0:1, :, :], -1.0 / (UNIT * HDIAG), -0.5 / (UNIT * HDIAG), A.mult, A.add, ["row", "r0", "r1", "r2"], ecs)
     close("v")
-    quant(T.stq[:], T.sts[:], T.st[:], ["st0", "st1", "st2", "st3"], ["stq"])
-    close("v")
     for k in range(4):
-        afill(T.jt[:, 224 * k:224 * k + 224], 224, 0.0, "jt")
+        afill(T.jt[:, 224 * k:224 * k + 224], 224, 0.0, "jt%d" % k)
     close("a")
+    JT = ["jt%d" % k for k in range(4)]
     jws = ["jw"] + ["jw%d" % i for i in range(1, 8)]
     path = T.hb[:, 191:192]
+
+    def spare(k):
+        close("v")
+        if k < 2:
+            for t in (2 * k, 2 * k + 1):
+                ts(T.st[:, t:512:4], T.tt[:], float(t), 4.0, A.is_equal, A.mult, ["tt"], ["st%d" % t])
+        elif k < 4:
+            for t in (2 * k - 4, 2 * k - 3):
+                fill(T.st[0:1, t:512:4], (0.0, 32.0, 256.0, 0.0)[t], "st%d" % t)
+        else:
+            quant(T.stq[:], T.sts[:], T.st[:], ["st0", "st1", "st2", "st3"], ["stq"])
+        close("v")
 
     def decode(n, q, s, rd):
         for b in range(4):
             mm(b, n, T.eq[:, 128 * b:128 * b + 128], T.es[:, 128 * b:128 * b + 128], q, s, ["eq"] + rd)
 
-    def cells(ja, jb, back):
-        a, b = 9 * ja + 1 - back, 9 * jb + 9 - back
-        return T.pb[:, 4 * a + 3:4 * b:4]
+    def cells(j, back):
+        a = 9 * j + 1 - back
+        return T.pb[:, 4 * a + 3:4 * a + 32:4]
 
-    def align(lst, lkey, step, at, nm, xo, xkeys, xw):
-        copy(T.gb[:, 2:256:step], T.gm[:].indirect(lst[:]), ["gm1", "gm2", "gmz", lkey], ["gb"])
+    def step(kind, j):
+        a, src = 9 * j + 1, ["pad", "pb%d" % (j - 1), "pb%d" % j]
+        if kind == "x":
+            tt(T.q1[:, 0:32:4], cells(j, 10), cells(j, 9), A.max, src[:2], ["q1"], True)
+        elif kind == "p":
+            scan(T.pb[:, 36 * j + 4:36 * j + 36], (T.q1 if j else T.q0)[:], T.tb[:, j:256:8], LOW, ["tb", "q1" if j else "q0"], ["pb%d" % j])
+        elif kind == "m":
+            tt(T.du[:, a:a + 8], cells(j, 10), cells(j, 1), A.max, src, ["du%d" % j], True)
+        elif kind == "d":
+            tt(T.km[:, 2 * a:2 * a + 16:2], cells(j, 1), cells(j, 10), A.is_gt, src, ["kd%d" % j], True)
+        elif kind == "l":
+            tt(T.km[:, 2 * a + 1:2 * a + 16:2], T.du[:, a:a + 8], cells(j, 9), A.is_ge, src + ["du%d" % j], ["kl%d" % j], True)
+        elif kind == "g":
+            tt(T.hx[:], T.hb[:, 24 * j - 24:24 * j].indirect(T.lh[:, 0:1]), T.km[:, 2 * a:2 * a + 16], A.subtract,
+               ["hbz", "hb%d" % (j - 1), "lh", "kd%d" % j, "kl%d" % j], ["hx"], True)
+        else:
+            scan(T.hb[:, 24 * j + 8:24 * j + 24], T.hx[:], T.jw[:, 16 * j:16 * j + 16], -2.0, ["hx", "hbz"] + jws, ["hb%d" % j])
+
+    def align(lst, lkey, stride, at, nm, xo, xkeys, xw):
+        copy(T.gb[:, 2:256:stride], T.gm[:].indirect(lst[:]), ["gm1", "gm2", "gmz", lkey], ["gb"])
         op("v", lambda: V.transpose(T.tb[:], T.gb[:]), r=["gb"], w=["tb"])
-        tasks, calls = {}, {}
-
-        def task(name, cost, needs, fn):
-            tasks[name] = (cost, needs)
-            calls[name] = fn
-
-        for j in range(8):
-            if j:
-                task("x%d" % j, 64, ["p%d" % (j - 1)], lambda j=j: tt(T.q1[:, 0:32:4], cells(j, j, 10), cells(j, j, 9), A.max, ["pad", "pb%d" % (j - 1)], ["q1"], True))
-            task("p%d" % j, 64, ["x%d" % j] if j else [],
-                 lambda j=j: scan(T.pb[:, 36 * j + 4:36 * j + 36], (T.q1 if j else T.q0)[:], T.tb[:, j:256:8], LOW, ["tb", "q1" if j else "q0"], ["pb%d" % j]))
-        for ja, jb in BATCHES:
-            a, b = 9 * ja + 1, 9 * jb + 9
-            src = ["pad"] + ["pb%d" % j for j in range(ja - 1, jb + 1)]
-            cost = max(64, 2 * (b - a))
-            kl = T.km[:, 2 * a + 1:2 * b:2]
-            if ja == 7:
-                task("a7", 64, ["p6"], lambda: tt(T.dv[:, 0:8], cells(7, 7, 10), cells(7, 7, 9), A.is_ge, ["pad", "pb6"], ["dv0"], True))
-                task("b7", 64, ["a7"], lambda: ts(T.dv[:, 8:16], T.dv[:, 0:8], LOW, None, A.mult, None, ["dv0"], ["dv1"], True))
-                task("c7", 64, ["b7"], lambda: tt(T.dv[:, 16:24], T.dv[:, 8:16], cells(7, 7, 9), A.add, ["dv1", "pb6"], ["dv2"], True))
-                task("l7", 64, ["c7", "p7"], lambda kl=kl: tt(kl, cells(7, 7, 1), T.dv[:, 16:24], A.is_ge, ["pad", "pb7", "dv2"], ["kl7"], True))
-            else:
-                task("m%d" % ja, cost, ["p%d" % jb], lambda ja=ja, jb=jb, a=a, b=b, src=src: tt(T.du[:, a:b], cells(ja, jb, 10), cells(ja, jb, 1), A.max, src, ["du%d" % ja], True))
-                task("l%d" % ja, cost, ["m%d" % ja], lambda ja=ja, jb=jb, a=a, b=b, src=src, kl=kl: tt(kl, T.du[:, a:b], cells(ja, jb, 9), A.is_ge, src + ["du%d" % ja], ["kl%d" % ja], True))
-            task("d%d" % ja, cost, ["p%d" % jb], lambda ja=ja, jb=jb, a=a, b=b, src=src: tt(T.km[:, 2 * a:2 * b:2], cells(ja, jb, 1), cells(ja, jb, 10), A.is_gt, src, ["kd%d" % ja], True))
-            for j in range(ja, jb + 1):
-                task("g%d" % j, 85, ["d%d" % ja, "l%d" % ja] + (["h%d" % (j - 1)] if j > 1 else []),
-                     lambda j=j, ja=ja: tt(T.hx[:], T.hb[:, 24 * j - 24:24 * j].indirect(T.lh[:, 0:1]), T.km[:, 18 * j + 2:18 * j + 18], A.subtract,
-                                           ["hbz", "hb%d" % (j - 1), "lh", "kd%d" % ja, "kl%d" % ja], ["hx"], True))
-                task("h%d" % j, 64, ["g%d" % j],
-                     lambda j=j: scan(T.hb[:, 24 * j + 8:24 * j + 24], T.hx[:], T.jw[:, 16 * j:16 * j + 16], -2.0, ["hx", "hbz"] + jws, ["hb%d" % j]))
-        for n in interleave(tasks):
-            calls[n]()
+        for name in ORDER:
+            if name[0] != "s":
+                step(name[0], int(name[1]))
+            elif at == 0:
+                spare(int(name[1]))
         n = 8 * nm
         ts(T.fl[:, 0:n], T.ec[:, at:at + nm, :], path, -0.5, A.mult, A.add, ["hb7"] + ecs, ["fl"])
         close("v")
@@ -385,7 +366,6 @@ def rank_program(g, core, T, topo):
             close("v")
         quant(T.xq[:], T.xsc[:], T.xt[:, xo:xo + 512], xkeys, ["xq"])
         mm(5, 128, T.stq[:], T.sts[:], T.xq[:], T.xsc[:], ["stq", "xq"])
-        close("v")
 
     def offsets(out, n, okey):
         ts(out[:], bank[5][:, 0:n], col(3), None, A.add, None, ["b5", "ff"], [okey])
@@ -412,11 +392,9 @@ def rank_program(g, core, T, topo):
     D0 = ["d0%d" % b for b in range(4)]
     align(T.l0, "l0", 4, 0, 16, 0, XA, ["xt0"])
     quant(T.wq[:], T.ws[:], T.wt[:], ["wt"], ["wq"])
-    close("v")
     offsets(T.o0, 32, "o0")
     blend(T.mt, 0, 512, T.d0[:, 768:1536], T.o0[:], T.d0[:, 256:768], D0 + ["o0"], ["mt0"])
     quant(T.m0q[:], T.m0s[:], T.mt[:], ["mt0"], ["m0"])
-    close("v")
 
     def prod(o, q, s, rd):
         mm(6 + o, 128, T.wq[:, 128 * o:128 * o + 128], T.ws[:, 128 * o:128 * o + 128], q, s, ["wq"] + rd)
@@ -435,77 +413,73 @@ def rank_program(g, core, T, topo):
         for h in range(2):
             act(T.y0[:, 4 * o:4 * o + 4, 2 * pars[h] + b1, :], bank[6 + o][:, 32 * h:32 * h + 32], ["b%d" % (6 + o)], ["y0k%d%d" % (o, h)])
         close("a")
-    act(T.jt[:, 0:256:4], T.xt[:, 0:64], ["xt0", "jt"], ["j0"])
+    act(T.jt[:, 0:256:4], T.xt[:, 0:64], ["xt0"] + JT, ["j0"])
     close("a")
     D1 = ["d1%d" % b for b in range(4)]
     win1 = T.d1[:, 256 * hb1:256 * hb1 + 256]
     align(T.l1, "l1", 8, 16, 8, 512, XB + ["xu"], ["xt4"])
-    act(T.jt[:, 256:768:4], T.xt[:, 512:640], ["xt4", "xu", "jt"], ["j1"])
+    act(T.jt[:, 256:768:4], T.xt[:, 512:640], ["xt4", "xu"] + JT, ["j1"])
     close("a")
     offsets(T.o1, 32, "o1")
     blend(T.mt, 0, 128, win1, T.o1[:, 0:8], T.d1[:, 256 * ha1:256 * ha1 + 128], D1 + ["o1"], ["mt0"])
-    blend(T.mu, 0, 128, win1, T.o1[:, 8:16], T.d1[:, 256 * ha1 + 128:256 * ha1 + 256], D1 + ["o1"], ["mu0"])
     quant(T.m1q[:], T.m1s[:], T.mt[:], ["mt0"], ["m1"])
-    close("v")
     need("g", ["m1"])
     (m8,), n8 = masks(c4, 1)
     rid, pid = int(topo.addr(c4)[0]), int(topo.addr(c4)[1])
-    g.remote_dma(T.hq[:, 0:32].bitcast(dt.uint8), T.m1q[:, 0:32].bitcast(dt.uint8), T.sem.arr2, T.sem.sent, pid, rid, m8)
-    g.remote_dma(T.hs[:, 0:32], T.m1s[:, 0:32], T.sem.arr2, T.sem.sent, pid, rid, m8)
+    g.remote_dma(T.hq[:, 128:160].bitcast(dt.uint8), T.m1q[:, 0:32].bitcast(dt.uint8), T.sem.arr2, T.sem.sent, pid, rid, m8)
+    g.remote_dma(T.hs[:, 128:160], T.m1s[:, 0:32], T.sem.arr2, T.sem.sent, pid, rid, m8)
     sent += 2 * n8
     landed("hin", "arr2", 2 * n8)
 
+    blend(T.mu, 384, 128, win1, T.o1[:, 8:16], T.d1[:, 256 * ha1 + 128:256 * ha1 + 256], D1 + ["o1"], ["mu0"])
     blend(T.mu, 128, 256, T.d0[:, 768:1536], T.o1[:, 16:32], T.d0[:, 0:256], D0 + ["o1"], ["mu1"])
     quant(T.jq[:], T.js[:], T.jt[:, 0:768], ["j0", "j1"], ["jq"])
-    close("v")
-    quant(T.hq[:, 32:160], T.hs[:, 32:160], T.mu[:], ["mu0", "mu1", "muz"], ["hown"])
-    close("v")
+    quant(T.hq[:, 0:128], T.hs[:, 0:128], T.mu[:], ["mu0", "mu1", "muz"], ["hown"])
     for o in range(2):
         prod(o, T.m1q[:], T.m1s[:], ["m1"])
     mm(0, 192, T.stq[:], T.sts[:], T.jq[:], T.js[:], ["stq", "jq"])
     for o in range(2):
         act(T.y1[:, 4 * o:4 * o + 4, 1 - keep1, :], bank[6 + o][:, 0:32], ["b%d" % (6 + o)], ["y1s%d" % o])
         close("a")
-    for o in range(2):
-        prod(o, T.hq[:, 32:160], T.hs[:, 32:160], ["hown"])
     for h in range(2):
         act(T.p0[0:1, :, 2 * pars[h] + b1, :], bank[0][0:1, 32 * h:32 * h + 32], ["b0"], ["p0k%d" % h], scale=0.25)
         act(T.p1[0:1, :, pars[h], :], bank[0][0:1, 64 + 32 * h:96 + 32 * h], ["b0"], ["p1%d" % h], scale=0.25)
         act(T.p0[0:1, :, 2 * pars[h] + 1 - b1, :], bank[0][0:1, 128 + 32 * h:160 + 32 * h], ["b0"], ["p0u%d" % h], scale=0.25)
     close("a")
 
-    qa2 = 1 - qb2
+    qa2 = 5 - qb2
     H = ["hin", "hown"]
-    mm(4, 128, T.hq[:, 0:128], T.hs[:, 0:128], T.hq[:, 0:128], T.hs[:, 0:128], H)
-    decode(128, T.hq[:, 0:128], T.hs[:, 0:128], H)
-    masked(4, 32 * qa2, 32, 32 * qb2, 32 * qb2, "gm1")
+    mm(4, 128, T.hq[:, 32:160], T.hs[:, 32:160], T.hq[:, 32:160], T.hs[:, 32:160], H)
     for o in range(2):
-        act(T.y1[:, 4 * o:4 * o + 4, keep1, :], bank[6 + o][:, 0:32], ["b%d" % (6 + o)], ["y1k%d" % o])
+        prod(o, T.hq[:, 0:128], T.hs[:, 0:128], ["hown"])
+    decode(128, T.hq[:, 32:160], T.hs[:, 32:160], H)
+    masked(4, 32 * qa2, 32, 32 * qb2, 32 * qb2, "gm1")
+    for b in range(4):
+        act(T.d2[:, b:256:4], bank[b][:, 64:128], ["b%d" % b], ["d2%d" % b], scale=0.5)
+    close("a")
+    for o in range(2):
+        act(T.y1[:, 4 * o:4 * o + 4, keep1, :], bank[6 + o][:, 96:128], ["b%d" % (6 + o)], ["y1k%d" % o])
         for h in range(2):
             act(T.y0[:, 4 * o:4 * o + 4, 2 * pars[h] + 1 - b1, :], bank[6 + o][:, 32 + 32 * h:64 + 32 * h], ["b%d" % (6 + o)], ["y0u%d%d" % (o, h)])
         close("a")
-    for b in range(4):
-        act(T.d2[:, b:256:4], bank[b][:, 0:64], ["b%d" % b], ["d2%d" % b], scale=0.5)
-    close("a")
     store("s", T.pt[0:1, 0:128], T.p0[0:1, :, :, :], ["p0k0", "p0k1", "p0u0", "p0u1"])
     store("s", T.pt[0:1, 128:192], T.p1[0:1, :, :, :], ["p10", "p11"])
     for o in range(2):
-        store("s", T.y[:, 224 * o:224 * o + 128], T.y0[:, 4 * o:4 * o + 4, :, :], ["y0%s%d%d" % (u, o, h) for u in "ku" for h in range(2)])
-        store("s", T.y[:, 224 * o + 128:224 * o + 192], T.y1[:, 4 * o:4 * o + 4, :, :], ["y1k%d" % o, "y1s%d" % o])
+        store("sa"[o], T.y[:, 224 * o:224 * o + 128], T.y0[:, 4 * o:4 * o + 4, :, :], ["y0%s%d%d" % (u, o, h) for u in "ku" for h in range(2)])
+        store("sa"[o], T.y[:, 224 * o + 128:224 * o + 192], T.y1[:, 4 * o:4 * o + 4, :, :], ["y1k%d" % o, "y1s%d" % o])
     align(T.l1, "l1", 8, 32, 4, 128, XA + ["xt4", "xu"], ["xt1"])
-    act(T.jt[:, 768:896:4], T.xt[:, 128:160], ["xt1", "jt"], ["j3"])
+    act(T.jt[:, 768:896:4], T.xt[:, 128:160], ["xt1"] + JT, ["j3"])
     close("a")
     quant(T.j2q[:], T.j2s[:], T.jt[:, 384:896], ["j1", "j3"], ["j2q"])
-    close("v")
     mm(0, 128, T.stq[:], T.sts[:], T.j2q[:], T.j2s[:], ["stq", "j2q"])
     act(T.p2[0:1, :], bank[0][0:1, 96:128], ["b0"], ["p2"], scale=0.25)
     close("a")
-    store("s", T.pt[0:1, 192:224], T.p2[0:1, :], ["p2"])
+    store("a", T.pt[0:1, 192:224], T.p2[0:1, :], ["p2"])
     D2 = ["d2%d" % b for b in range(4)]
     offsets(T.o2, 8, "o2")
-    blend(T.mt, 0, 128, T.d2[:, 128 * qb2:128 * qb2 + 128], T.o2[:], T.d2[:, 128 * qa2:128 * qa2 + 128], D2 + ["o2"], ["mt0"])
+    ha2, hb2 = qa2 - 2, qb2 - 2
+    blend(T.mt, 0, 128, T.d2[:, 128 * hb2:128 * hb2 + 128], T.o2[:], T.d2[:, 128 * ha2:128 * ha2 + 128], D2 + ["o2"], ["mt0"])
     quant(T.m2q[:], T.m2s[:], T.mt[:], ["mt0"], ["m2"])
-    close("v")
     for o in range(2):
         prod(o, T.m2q[:], T.m2s[:], ["m2"])
     store("s", T.oc[:, 0:128], T.m2q[:, 0:32].bitcast(dt.uint8), ["m2"])
@@ -517,4 +491,4 @@ def rank_program(g, core, T, topo):
     store("s", T.y[:, 192:224], T.y2[:, 0:32], ["y20"])
     store("a", T.y[:, 416:448], T.y2[:, 32:64], ["y21"])
     g.wait_ge(T.sem.sent, sent)
-    finish()
+    finish("s")

@@ -3,10 +3,9 @@ from concourse.mybir import dt, AluOpType, ActivationFunctionType
 
 F32, BF, I32, U16, X4, U8 = "float32", "bfloat16", "int32", "uint16", "float8_e4m3fn_x4", "uint8"
 LOW = -1.0e29
-UNIT = 2.0 ** -22
-HDIAG = sum(i * 8 ** (i - 1) for i in range(1, 8)) + 0.5
-ORDER = ("p0 s0 x1 s1 p1 s2 x2 d1 m1 p2 l1 x3 m2 g1 d2 p3 l2 h1 x4 m3 g2 d3 p4 l3 h2 x5 m4 g3 d4 p5 l4 h3 x6 m5 g4 d5 p6 "
-         "l5 h4 m6 x7 g5 d6 l6 p7 h5 m7 g6 d7 l7 h6 s3 g7 s4 h7").split()
+UNIT = 0.125
+ORDER = ("p0 a0 a1 x1 b0 p1 q1 b1 m1 p2 q2 d1 l1 d2 p3 q3 l2 h1 g1 d3 p4 q4 l3 h2 g2 d4 p5 q5 l4 h3 g3 d5 p6 q6 l5 h4 g4 d6 "
+         "p7 l6 h5 g5 d7 l7 h6 g6 h7").split()
 
 
 def _sb(shape, d):
@@ -14,34 +13,33 @@ def _sb(shape, d):
 
 
 SCRATCH = {
-    "xs": _sb([4, 8, 32], BF), "xt": _sb([1024], BF), "wt": _sb([1024], BF),
-    "sq": _sb([128], X4), "ss": _sb([128], U8), "lq": _sb([384], X4), "ls": _sb([384], U8),
+    "xs": _sb([8, 4, 32], BF), "xt": _sb([1024], BF), "wt": _sb([1024], BF),
+    "sq": _sb([128], X4), "ss": _sb([128], U8), "lq": _sb([512], X4), "ls": _sb([512], U8),
     "wq": _sb([256], X4), "ws": _sb([256], U8),
     "et": _sb([2048], BF), "eq": _sb([512], X4), "es": _sb([512], U8),
     "st": _sb([512], BF), "stq": _sb([128], X4), "sts": _sb([128], U8),
-    "pi": _sb([2], I32), "fi": _sb([10], I32), "ff": _sb([20], F32),
-    "uu": _sb([128], F32), "vv": _sb([128], BF), "tt": _sb([128], BF), "zz": _sb([288], BF),
-    "mk": _sb([128], F32), "c2": _sb([4], F32), "c4": _sb([2], F32),
-    "l0": _sb([4], U16), "l1": _sb([2], U16), "lh": _sb([2], U16),
-    "part": _sb([36], F32), "row": _sb([36, 8], F32), "ec": _sb([36, 8], F32), "kj": _sb([8], F32),
-    "gm": _sb([256], F32), "gb": _sb([256], F32), "tb": _sb([256], F32),
-    "pb": _sb([288], F32), "q0": _sb([32], F32), "q1": _sb([32], F32), "du": _sb([72], F32),
-    "km": _sb([144], F32), "hb": _sb([192], F32), "hx": _sb([16], F32), "jw": _sb([128], F32),
-    "fl": _sb([128], I32), "dg": _sb([128], I32), "flu": _sb([64], I32), "dgu": _sb([64], I32),
-    "xq": _sb([128], X4), "xsc": _sb([128], U8),
+    "pi": _sb([2], I32), "fi": _sb([8], I32), "ff": _sb([12], F32),
+    "uu": _sb([128], F32), "vv": _sb([128], BF), "tt": _sb([128], BF), "zz": _sb([368], BF),
+    "mk": _sb([128], F32), "cl": _sb([16], F32), "l0": _sb([16], U16), "lg": _sb([4], U16),
+    "kj": _sb([32], F32), "ke": _sb([8], F32), "ma": _sb([8, 2, 2], F32), "mb": _sb([32], F32),
+    "gm": _sb([128], F32), "gb": _sb([256], F32), "tb": _sb([256], F32), "g3": _sb([96], F32), "g4": _sb([128], F32),
+    "pb": _sb([36], F32), "q0": _sb([32], F32), "q1": _sb([32], F32), "du": _sb([8], F32),
+    "pr": _sb([720], F32), "p7": _sb([32], F32),
+    "km": _sb([320], F32), "hz": _sb([32], F32), "hr": _sb([1104], F32), "h7": _sb([32], F32),
+    "xa": _sb([512], BF), "xb": _sb([512], BF), "xq": _sb([128], X4), "xsc": _sb([128], U8),
     "o0": _sb([32], U16), "o1": _sb([32], U16), "o2": _sb([8], U16),
-    "d0": _sb([1536], F32), "d1": _sb([512], F32), "d2": _sb([256], F32),
+    "d0": _sb([1024], F32), "dy": _sb([512], F32), "d2": _sb([256], F32),
+    "d1a": _sb([4, 2, 32], F32), "d1b": _sb([256], F32), "d1s": _sb([256], F32),
     "mt": _sb([512], BF), "mu": _sb([512], BF),
     "m0q": _sb([128], X4), "m0s": _sb([128], U8), "m1q": _sb([128], X4), "m1s": _sb([128], U8),
     "hq": _sb([160], X4), "hs": _sb([160], U8), "m2q": _sb([128], X4), "m2s": _sb([128], U8),
-    "jt": _sb([896], BF), "jq": _sb([192], X4), "js": _sb([192], U8), "j2q": _sb([128], X4), "j2s": _sb([128], U8),
-    "y0": _sb([8, 4, 8], F32), "y1": _sb([8, 2, 8], F32), "y2": _sb([64], F32),
-    "p0": _sb([4, 4, 8], F32), "p1": _sb([4, 2, 8], F32), "p2": _sb([32], F32),
+    "ya": _sb([24, 2, 8], F32), "y2": _sb([64], F32),
+    "pc": _sb([12], F32), "pf": _sb([128], F32), "p0": _sb([8, 2, 8], F32),
 }
 for _k in range(8):
     SCRATCH["b%d" % _k] = ("psum", [128, 512], F32)
 NPOOL = 140
-SEMAPHORES = ["arr0", "arr2", "sent"] + ["s%d" % _k for _k in range(NPOOL)]
+SEMAPHORES = ["arr0", "arry", "arr2", "sent"] + ["s%d" % _k for _k in range(NPOOL)]
 
 
 def make_order(g, T):
@@ -133,20 +131,18 @@ def rank_program(g, core, T, topo):
     b0, b1, b2 = r & 1, (r >> 1) & 1, (r >> 2) & 1
     bank = [T["b%d" % k] for k in range(8)]
 
-    def masks(dst, parts):
-        e = topo.engines(core, dst)
-        n = len(e) // parts
-        return [sum(1 << k for k in e[n * i:n * i + n]) for i in range(parts)], n
+    def mask_of(e):
+        return sum(1 << k for k in e)
 
     def dst_id(c):
         a = topo.addr(c)
         return DstId(rid=int(a[0]), pnc=int(a[1]))
 
-    def iota(out, pat, base, cm, key, small=True):
+    def iota(out, pat, base, cm, key, small=True, rd=()):
         if small:
-            op("g", lambda: g.iota(out, pat, base, cm, allow_small_or_imprecise_dtypes=True), w=[key])
+            op("g", lambda: g.iota(out, pat, base, cm, allow_small_or_imprecise_dtypes=True), r=rd, w=[key])
         else:
-            op("g", lambda: g.iota(out, pat, base, cm), w=[key])
+            op("g", lambda: g.iota(out, pat, base, cm), r=rd, w=[key])
 
     def fill(out, val, key, rd=()):
         op("v", lambda: V.memset(out, val), r=rd, w=[key])
@@ -160,11 +156,11 @@ def rank_program(g, core, T, topo):
     def tt(out, in0, in1, o, rd, wr, cut=False):
         op("v", lambda: V.tensor_tensor(out, in0, in1, o), r=rd, w=wr, cut=cut)
 
-    def scan(out, d0, d1, init, rd, wr):
-        op("v", lambda: V.tensor_tensor_scan(out, d0, d1, init, A.max, A.add), r=rd, w=wr, cut=True)
+    def scan(out, d0, d1, init, o1, rd, wr):
+        op("v", lambda: V.tensor_tensor_scan(out, d0, d1, init, A.max, o1), r=rd, w=wr, cut=True)
 
-    def copy(out, in_, rd, wr):
-        op("v", lambda: V.tensor_copy(out, in_), r=rd, w=wr)
+    def copy(out, in_, rd, wr, cut=False):
+        op("v", lambda: V.tensor_copy(out, in_), r=rd, w=wr, cut=cut)
 
     def act(out, in_, rd, wr, scale=1.0, bias=None):
         if bias is None:
@@ -182,312 +178,310 @@ def rank_program(g, core, T, topo):
     def mm(k, n, lq, ls, rq, rs, rd):
         op("t", lambda: PE.matmul_mx(bank[k][:, 0:n], lq, ls, rq, rs, True, True), r=rd, w=["b%d" % k], cut=True)
 
-    def store(q, out, in_, rd):
+    def store(q, out, in_, rd, wr=()):
         eng = {"s": g.sync, "a": S}[q]
-        op(q, lambda: eng.dma_start(out, in_), r=rd, dma=True)
+        op(q, lambda: eng.dma_start(out, in_), r=rd, w=wr, dma=True)
 
     op("s", lambda: g.sync.dma_start(T.xs[:], T.x[:]), w=["xs"], dma=True)
     close("s")
 
-    hb1, qb2 = 1 - b1, 3 - b2
-    fill(T.zz[:], 0.0, "zz")
-    close("v")
-    act(T.row[0:1, :, :], T.zz[0:1, :], ["zz"], ["row"])
-    close("a")
+    ha1, hb1 = 1 - b1, b1
+    qa2, qb2 = 2 + b2, 3 - b2
     iota(T.pi[:, 0:1], [[0, 1]], 0, 1, "pi", small=False)
     close("g")
-    iota(T.kj[:], [[1, 8]], 0, 0, "kj")
+    iota(T.kj[:], [[1, 32]], 0, 0, "kj")
+    iota(T.cl[:], [[1, 8], [16, 2]], 0, 0, "cl")
+    close("g")
     iota(T.vv[:], [[1, 128]], 0, -1, "vv")
     iota(T.uu[:], [[1, 16], [0, 8]], 0, 0, "uu")
-    iota(T.c2[:], [[2, 4]], 0, 0, "c2")
-    iota(T.c4[:], [[4, 2]], 0, 0, "c4")
-    close("g")
-    segs = [(0, 16, [[16, 2], [32, 2], [4, 4]], 66), (16, 8, [[32, 2], [8, 4]], 64 * hb1 + 2),
-            (24, 8, [[32, 2], [4, 4]], 2), (32, 4, [[8, 4]], 32 * qb2 + 2)]
-    for k, (at, n, pat, base) in enumerate(segs):
-        iota(T.part[:, at:at + n], pat, base, 0, "part%d" % k)
-    need("g", ["row"])
-    iota(T.row[0:1, :, 1:8:4], [[0, 5], [1, 8], [0, 2]][0:0] + [[0, 72]], 0, 0, "r2") if False else None
-    iota(T.row[0:1, 0:32, 1:8:4], [[0, 4], [1, 8], [0, 2]], 0, 0, "r0")
-    iota(T.row[0:1, 0:16, 2:8:4], [[1, 2], [0, 16]], 1, 0, "r1")
-    iota(T.row[0:1, 32:36, 1:8:4], [[1, 4], [0, 2]], 0, 0, "r2")
-    close("g")
-    fill(T.et[:], 0.0, "et")
-    for k, (sh, m) in enumerate([(5, 3), (3, 1), (2, 1), (0, 3), (2, 3), (3, 15), (0, 127), (0, 15), (0, 1)]):
-        ts(T.fi[:, k:k + 1], T.pi[:, 0:1], sh, m, A.logical_shift_right, A.bitwise_and, ["pi"], ["fi%d" % k])
-    afill(T.gb[:], 256, 0.0, "gb")
-    afill(T.gm[:, 128:192], 64, 0.0, "gmz")
-    afill(T.pb[:, 3:288:36], 8, LOW, "pad")
-    afill(T.q0[:], 32, LOW, "q0")
-    afill(T.q1[:], 32, LOW, "q1")
-    afill(T.hb[:], 192, -2.0, "hbz")
-    afill(T.jw[:], 128, 0.0, "jw")
-    act(T.q0[:, 0:1], T.zz[:, 0:1], ["zz"], ["q0"], scale=0.0, bias=0.0)
-    act(T.hb[:, 8:24], T.zz[:, 0:16], ["zz", "hbz"], ["hb0"], scale=0.0, bias=-0.5 * UNIT)
-    close("a")
-    close("v")
-
-    own = 192 * b0
-    keep1 = b2
-    order = [4 * par + (r ^ k) % 4 for k in (3, 1, 2, 0) for par in (1 - keep1, keep1)]
-    for k in (6, 7):
-        act(T.xt[:, 128 * k:128 * k + 128], T.xs[:, :, order[k], :], ["xs"], ["xt%d" % k])
-    close("a")
-    for k in (0, 1, 2, 3):
-        copy(T.xt[:, 128 * k:128 * k + 128], T.xs[:, :, order[k], :], ["xs"], ["xt%d" % k])
-    close("v")
-    for k in (4, 5):
-        copy(T.xt[:, 128 * k:128 * k + 128], T.xs[:, :, order[k], :], ["xs"], ["xt%d" % k])
-    close("v")
-    XA, XB = ["xt0", "xt1", "xt2", "xt3"], ["xt4", "xt5", "xt6", "xt7"]
-    quant(T.sq[:], T.ss[:], T.xt[:, 0:512], XA, ["sq"])
-    quant(T.lq[:, own:own + 128], T.ls[:, own:own + 128], T.xt[:, 512:1024], XB, ["lown"])
-    need("g", ["lown", "sq"])
-    c1, c2, c3, c4 = (T.cores[r ^ k] for k in (1, 2, 3, 4))
-    ms, ne = masks(c1, 4)
-    for codes in (True, False):
-        src, mine = (T.sq, T.lq) if codes else (T.ss, T.ls)
-        view = (lambda t, a: t[:, a:a + 64].bitcast(dt.uint8)) if codes else (lambda t, a: t[:, a:a + 64])
-        pieces = [(src, 0, c1, own), (src, 64, c1, own + 64), (src, 0, c3, own + 128), (mine, own, c2, own + 128)]
-        g.remote_dma_fused([RemoteDMATransfer(dst_ids=[dst_id(c)], dma_engine_mask=ms[k], remote_sem=T.sem.arr0,
-                                              src=view(t, a), dst=view(mine, at))
-                            for k, (t, a, c, at) in enumerate(pieces)], local_sem=T.sem.sent)
-    sent = 8 * ne
-    landed("lin", "arr0", 8 * ne)
-
     iota(T.tt[:], [[0, 8], [1, 4], [0, 4]], 0, 0, "tt")
     close("g")
-    for i in range(1, 8):
-        act(T.jw[:, 2 * i:128:16], T.kj[:], ["kj", "jw"], ["jw%d" % i], scale=-UNIT * 8 ** (i - 1))
-    afill(T.mu[:, 0:128], 128, 0.0, "muz")
+    fill(T.zz[:], 0.0, "zz")
+    close("v")
+    fill(T.et[:], 0.0, "et")
+    close("v")
+    for k, (sh, m) in enumerate([(0, 3), (0, 7), (3, 15), (2, 31), (0, 104), (0, 16), (3, 1)]):
+        ts(T.fi[:, k:k + 1], T.pi[:, 0:1], sh, m, A.logical_shift_right, A.bitwise_and, ["pi"], ["fi%d" % k])
+    close("v")
+    afill(T.pr[:, 0:360], 360, LOW, "prz0")
+    afill(T.pr[:, 360:720], 360, LOW, "prz1")
+    afill(T.km[:], 320, 0.0, "kmz")
+    afill(T.pb[:, 3:4], 1, LOW, "pad")
+    afill(T.q0[:], 32, LOW, "top")
+    afill(T.q1[:], 32, LOW, "x1")
+    close("a")
+    afill(T.q0[:, 0:1], 1, 0.0, "top")
     close("a")
     col = lambda k: T.ff[:, k:k + 1]
-    copy(T.ff[:, 0:9], T.fi[:, 0:9], ["fi%d" % k for k in range(9)], ["ff"])
+    copy(T.ff[:, 0:7], T.fi[:, 0:7], ["fi%d" % k for k in range(7)], ["ff"])
     close("v")
+
+    order = [(r ^ k) % 4 for k in (1, 3, 0, 2)]
+    act(T.xt[:, 512:768], T.xs[:, :, order[2], :], ["xs"], ["xt2"])
+    close("a")
+    for k in (0, 1):
+        copy(T.xt[:, 256 * k:256 * k + 256], T.xs[:, :, order[k], :], ["xs"], ["xt%d" % k])
+    close("v")
+    copy(T.xt[:, 768:1024], T.xs[:, :, order[3], :], ["xs"], ["xt3"])
+    close("v")
+    quant(T.sq[:], T.ss[:], T.xt[:, 0:512], ["xt0", "xt1"], ["sq"])
+    quant(T.lq[:, 192:320], T.ls[:, 192:320], T.xt[:, 512:1024], ["xt2", "xt3"], ["lown"])
+    need("g", ["lown", "sq"])
+    c1, c2, c3, c4 = (T.cores[r ^ k] for k in (1, 2, 3, 4))
+    e = topo.engines(core, c1)
+    n4 = len(e) // 4
+    e0, e1, e2, e3 = (e[n4 * k:n4 * k + n4] for k in range(4))
+
+    def view(t, a, codes):
+        return t[:, a:a + 64].bitcast(dt.uint8) if codes else t[:, a:a + 64]
+
+    for codes in (True, False):
+        src, mine = (T.sq, T.lq) if codes else (T.ss, T.ls)
+        es = (e0, e1, e2 + e3) if codes else (e2, e3, e0 + e1)
+        pieces = [(src, 0, c1, 64), (src, 64, c3, 0), (mine, 256, c2, 128)]
+        g.remote_dma_fused([RemoteDMATransfer(dst_ids=[dst_id(c)], dma_engine_mask=mask_of(es[k]), remote_sem=T.sem.arr0,
+                                              src=view(t, a, codes), dst=view(mine, at, codes))
+                            for k, (t, a, c, at) in enumerate(pieces)], local_sem=T.sem.sent)
+    rid, pid = int(topo.addr(c1)[0]), int(topo.addr(c1)[1])
+    g.remote_dma(view(T.lq, 320, True), view(T.sq, 64, True), T.sem.arry, T.sem.sent, pid, rid, mask_of(e))
+    g.remote_dma(view(T.ls, 320, False), view(T.ss, 64, False), T.sem.arry, T.sem.sent, pid, rid, mask_of(e))
+    sent = 4 * len(e)
+    landed("lin", "arr0", 2 * len(e))
+    landed("yin", "arry", 2 * len(e))
+
+    for k in range(3):
+        afill(T.hr[:, 368 * k:368 * k + 368], 368, 0.0, "hrz%d" % k)
+    afill(T.hz[:], 32, 0.0, "hzz")
+    afill(T.g3[:, 0:96:3], 32, 0.0, "g3z")
+    afill(T.g4[:], 128, 0.0, "g4z")
+    afill(T.mu[:, 0:128], 128, 0.0, "muz")
+    close("a")
+    fill(T.xa[:], 0.0, "xaz")
+    fill(T.xb[:], 0.0, "xbz")
+    close("v")
+    iota(T.xa[0:1, 1:128:4], [[1, 16], [0, 2]], 0, 0, "xa1", rd=["xaz"])
+    iota(T.xb[0:1, 1:64:4], [[2 * b2 - 1, 2], [2, 4], [0, 2]], 1 - b2, 0, "xb1", rd=["xbz"])
+    iota(T.xb[0:1, 65:128:4], [[1, 8], [0, 2]], 0, 0, "xb2", rd=["xbz"])
+    close("g")
     for b in range(4):
         ts(T.et[:, 512 * b + b:512 * b + 512:4], T.vv[:], 0.0, None, A.is_equal, None, ["vv", "et"], ["et%d" % b])
     close("v")
-    ts(col(10), col(0), 32.0, col(1), A.mult, A.add, ["ff"], ["f10"])
-    ts(col(11), col(0), 32.0, col(4), A.mult, A.add, ["ff"], ["f11"])
-    ts(T.lh[:, 0:1], col(7), col(8), 7.0, A.add, A.add, ["ff"], ["lh"])
-    close("v")
-    ts(T.mk[:], T.uu[:], col(5), None, A.is_equal, None, ["uu", "ff"], ["mk"])
-    fill(T.ec[:, :, 0], 0.0, "ec0")
-    close("v")
-    ts(col(12), col(2), 128.0, col(10), A.mult, A.add, ["ff", "f10"], ["f12"])
-    ts(col(13), col(3), 8.0, col(11), A.mult, A.add, ["ff", "f11"], ["f13"])
-    close("v")
-    parts = ["part%d" % k for k in range(len(segs))]
-
-    def powers(lo, hi):
-        for i in range(lo, hi):
-            ts(T.ec[:, :, i], T.part[:], col(6), -8.0 ** (1 - i) / UNIT, A.is_equal, A.mult, parts + ["ff"], ["ec%d" % i])
-        close("v")
-
-    powers(1, 4)
-    ts(col(14), col(3), 8.0, col(12), A.mult, A.add, ["ff", "f12"], ["f14"])
-    ts(T.l1[:], T.c4[:], col(13), None, A.add, None, ["c4", "f13"], ["l1"])
-    close("v")
-    powers(4, 8)
-    ts(T.l0[:], T.c2[:], col(14), None, A.add, None, ["c2", "f14"], ["l0"])
+    ts(T.ke[:], T.kj[:, 0:8], col(1), None, A.is_equal, None, ["kj", "ff"], ["ke"])
+    ts(T.ma[:], T.kj[:], col(3), 1.0 / UNIT, A.is_equal, A.mult, ["kj", "ff"], ["ma"])
+    ts(col(8), col(1), 32.0, col(5), A.mult, A.add, ["ff"], ["f8"])
     close("v")
     quant(T.eq[:], T.es[:], T.et[:], ["et0", "et1", "et2", "et3"], ["eq"])
-    ecs = ["ec%d" % i for i in range(8)]
-    ts(T.ec[0:1, :, :], T.row[0:1, :, :], -1.0 / (UNIT * HDIAG), -0.5 / (UNIT * HDIAG), A.mult, A.add, ["row", "r0", "r1", "r2"], ecs)
+    ts(col(9), col(6), 2.0, col(8), A.mult, A.add, ["ff", "f8"], ["f9"])
     close("v")
-    for k in range(4):
-        afill(T.jt[:, 224 * k:224 * k + 224], 224, 0.0, "jt%d" % k)
+    ts(T.mk[:], T.uu[:], col(2), None, A.is_equal, None, ["uu", "ff"], ["mk"])
+    ts(T.l0[:], T.cl[:], col(4), None, A.add, None, ["cl", "ff"], ["l0"])
+    close("v")
+    for u in range(2):
+        ts(T.lg[:, 2 * u:2 * u + 2], T.kj[:, u:8:4], col(9), None, A.add, None, ["kj", "f9"], ["lg%d" % u])
+    close("v")
+    if not b0 and b1:
+        quant(T.lq[:, 384:512], T.ls[:, 384:512], T.xt[:, 0:512], ["xt0", "xt1"], ["lpad"])
+    kp = lambda j: 3 + j % 2
+    kh = lambda j: 5 - j % 2
+    HRZ = ["hrz0", "hrz1", "hrz2"]
+    act(T.hz[:, 2:32:4], T.ke[:], ["ke", "hzz"], ["hc1"], scale=UNIT)
+    for j in range(1, 7):
+        a = 184 * (j - 1) + 8 + 2 * kh(j)
+        act(T.hr[:, a:a + 160:20], T.ke[:], ["ke"] + HRZ, ["hc%d" % (j + 1)], scale=(j + 1) * UNIT)
+    act(T.mb[:, 0:8], T.ma[:, 4 * hb1:4 * hb1 + 4, 1 - b2, :], ["ma"], ["mb0"])
+    act(T.mb[:, 8:16], T.ma[:, 4 * hb1:4 * hb1 + 4, b2, :], ["ma"], ["mb1"])
+    act(T.mb[:, 16:32], T.ma[:, 4 * ha1:4 * ha1 + 4, :, :], ["ma"], ["mb2"])
     close("a")
-    JT = ["jt%d" % k for k in range(4)]
-    jws = ["jw"] + ["jw%d" % i for i in range(1, 8)]
-    path = T.hb[:, 191:192]
-
-    def spare(k):
-        close("v")
-        if k < 2:
-            for t in (2 * k, 2 * k + 1):
-                ts(T.st[:, t:512:4], T.tt[:], float(t), 4.0, A.is_equal, A.mult, ["tt"], ["st%d" % t])
-        elif k < 4:
-            for t in (2 * k - 4, 2 * k - 3):
-                fill(T.st[0:1, t:512:4], (0.0, 32.0, 256.0, 0.0)[t], "st%d" % t)
-        else:
-            quant(T.stq[:], T.sts[:], T.st[:], ["st0", "st1", "st2", "st3"], ["stq"])
-        close("v")
+    fill(T.st[:], 0.0, "stz")
+    close("v")
+    ts(T.st[:, 0:512:4], T.tt[:], col(0), 4.0, A.is_equal, A.mult, ["tt", "ff", "stz"], ["st0"])
+    fill(T.st[0:1, 1:512:4], 32.0, "st1", ["stz"])
+    close("v")
+    quant(T.stq[:], T.sts[:], T.st[:], ["st0", "st1"], ["stq"])
+    path = T.h7[:, 31:32]
 
     def decode(n, q, s, rd):
         for b in range(4):
             mm(b, n, T.eq[:, 128 * b:128 * b + 128], T.es[:, 128 * b:128 * b + 128], q, s, ["eq"] + rd)
 
-    def cells(j, back):
-        a = 9 * j + 1 - back
-        return T.pb[:, 4 * a + 3:4 * a + 32:4]
+    def run(t, a, n, s):
+        return t[:, a:a + s * (n - 1) + 1:s]
 
-    def step(kind, j):
-        a, src = 9 * j + 1, ["pad", "pb%d" % (j - 1), "pb%d" % j]
-        if kind == "x":
-            tt(T.q1[:, 0:32:4], cells(j, 10), cells(j, 9), A.max, src[:2], ["q1"], True)
-        elif kind == "p":
-            scan(T.pb[:, 36 * j + 4:36 * j + 36], (T.q1 if j else T.q0)[:], T.tb[:, j:256:8], LOW, ["tb", "q1" if j else "q0"], ["pb%d" % j])
+    def sums(j, back):
+        if j == 0:
+            return run(T.pb, 7 - 4 * back, 8, 4), ["pad", "p0"]
+        return run(T.pr, 120 * (j - 1) + 12 + kp(j) - 12 * back, 8, 12), ["prz0", "prz1", "p%d" % j]
+
+    def step(name):
+        kind, j = name[0], int(name[1])
+        if kind in "ab":
+            t, k = (T.g3, 3) if kind == "a" else (T.g4, 4)
+            copy(run(t, 1 + j, 32, k), T.tb[:, 8 * j:256].indirect(T.lg[:, 2 * (k - 3):2 * (k - 3) + 2]),
+                 ["tb", "g%dz" % k, "lg%d" % (k - 3)], ["s" + name], True)
+        elif kind == "x":
+            tt(T.q1[:, 0:32:4], sums(0, 1)[0], sums(0, 0)[0], A.max, sums(0, 0)[1], ["x1"], True)
         elif kind == "m":
-            tt(T.du[:, a:a + 8], cells(j, 10), cells(j, 1), A.max, src, ["du%d" % j], True)
-        elif kind == "d":
-            tt(T.km[:, 2 * a:2 * a + 16:2], cells(j, 1), cells(j, 10), A.is_gt, src, ["kd%d" % j], True)
-        elif kind == "l":
-            tt(T.km[:, 2 * a + 1:2 * a + 16:2], T.du[:, a:a + 8], cells(j, 9), A.is_ge, src + ["du%d" % j], ["kl%d" % j], True)
-        elif kind == "g":
-            tt(T.hx[:], T.hb[:, 24 * j - 24:24 * j].indirect(T.lh[:, 0:1]), T.km[:, 2 * a:2 * a + 16], A.subtract,
-               ["hbz", "hb%d" % (j - 1), "lh", "kd%d" % j, "kl%d" % j], ["hx"], True)
+            tt(T.du[:], sums(0, 1)[0], sums(1, 1)[0], A.max, sums(0, 0)[1] + sums(1, 0)[1], ["du"], True)
+        elif kind in "pq":
+            k, n = kp(j), kp(j + 1)
+            if j == 0:
+                return scan(T.pb[:, 4:36], T.q0[:], T.tb[:, 0:256:8], LOW, A.add, ["tb", "top"], ["p0"])
+            at = 120 * (j - 1) + (12 + k if kind == "p" else 24) - n * (3 if j == 1 else 2)
+            out = T.p7[:] if j == 7 else run(T.pr, at, 8 * k, n)
+            if j == 1:
+                return scan(out, T.q1[:], T.tb[:, 1:256:8], LOW, A.add, ["tb", "x1", "prz0", "prz1"], [name])
+            t, u = (T.g3, "a") if k == 3 else (T.g4, "b")
+            scan(out, run(T.pr, 120 * (j - 2) + 12, 8 * k, n), t[:, 8 * k * (j // 2):8 * k * (j // 2 + 1)], LOW, A.add,
+                 ["s%s0" % u, "s%s1" % u, "p%d" % (j - 1), "q%d" % (j - 1)], [name])
+        elif kind in "dl":
+            m = T.du[:] if j == 1 else T.p7[:, 0:32:4] if j == 7 else run(T.pr, 120 * (j - 1) + 12 + kp(j) - 2 * kp(j + 1), 8, 12)
+            s, rd = sums(j - 1, int(kind == "d"))
+            if name == "d1":
+                m = sums(1, 1)[0]
+            tt(run(T.km, 40 * j + (0 if kind == "d" else 2), 8, kh(j)), s, m, A.is_ge if kind == "d" else A.is_gt,
+               rd + ["kmz", "p%d" % j] + (["du"] if name == "l1" else []), ["k" + name], True)
         else:
-            scan(T.hb[:, 24 * j + 8:24 * j + 24], T.hx[:], T.jw[:, 16 * j:16 * j + 16], -2.0, ["hx", "hbz"] + jws, ["hb%d" % j])
+            k, n = kh(j), kh(j + 1)
+            at = 184 * (j - 1) + (8 + 3 * k if kind == "h" else 28 + k) - 3 * n
+            scan(T.h7[:] if j == 7 else run(T.hr, at, 8 * k, n), T.hz[:] if j == 1 else run(T.hr, 184 * (j - 2) + 8, 8 * k, n),
+                 T.km[:, 40 * j:40 * j + 8 * k], 0.0, A.subtract,
+                 HRZ + ["hc%d" % j, "h%d" % (j - 1), "g%d" % (j - 1), "kd%d" % j, "kl%d" % j], [name])
 
-    def align(lst, lkey, stride, at, nm, xo, xkeys, xw):
-        copy(T.gb[:, 2:256:stride], T.gm[:].indirect(lst[:]), ["gm1", "gm2", "gmz", lkey], ["gb"])
+    def align(x, n, m, rd, key, slot):
+        copy(T.gb[:], T.gm[:].indirect(T.l0[:]), ["gm0", "gm1", "gm2", "gm3", "l0"], ["gb"])
         op("v", lambda: V.transpose(T.tb[:], T.gb[:]), r=["gb"], w=["tb"])
         for name in ORDER:
-            if name[0] != "s":
-                step(name[0], int(name[1]))
-            elif at == 0:
-                spare(int(name[1]))
-        n = 8 * nm
-        ts(T.fl[:, 0:n], T.ec[:, at:at + nm, :], path, -0.5, A.mult, A.add, ["hb7"] + ecs, ["fl"])
+            step(name)
+        ts(x[:, 0:4 * n:4], m, path, None, A.mult, None, ["h7"] + rd, [key])
         close("v")
-        if at == 0:
-            ts(T.flu[:], T.ec[:, 24:32, :], path, -0.5, A.mult, A.add, ["hb7"] + ecs, ["flu"])
-            close("v")
-        ts(T.dg[:, 0:n], T.fl[:, 0:n], 7, None, A.bitwise_and, None, ["fl"], ["dg"])
-        close("v")
-        if at == 0:
-            ts(T.dgu[:], T.flu[:], 7, None, A.bitwise_and, None, ["flu"], ["dgu"])
-            close("v")
-        copy(T.xt[:, xo:xo + n], T.dg[:, 0:n], ["dg"], xw)
-        close("v")
-        if at == 0:
-            copy(T.xt[:, 576:640], T.dgu[:], ["dgu", "xt4"], ["xu"])
-            close("v")
-        quant(T.xq[:], T.xsc[:], T.xt[:, xo:xo + 512], xkeys, ["xq"])
+        act(T.pc[:, slot:slot + 1], path, ["h7"], ["pc%d" % slot], scale=1.0 / UNIT)
+        close("a")
+        quant(T.xq[:], T.xsc[:], x[:], [key] + rd, ["xq"])
         mm(5, 128, T.stq[:], T.sts[:], T.xq[:], T.xsc[:], ["stq", "xq"])
 
     def offsets(out, n, okey):
-        ts(out[:], bank[5][:, 0:n], col(3), None, A.add, None, ["b5", "ff"], [okey])
+        ts(out[:], bank[5][:, 0:n], col(0), None, A.add, None, ["b5", "ff"], [okey])
         close("v")
 
-    def masked(k, a, n, m, at, key):
-        tt(T.gm[:, at:at + n], bank[k][:, a:a + n], T.mk[:, m:m + n], A.mult, ["b%d" % k, "mk"], [key])
+    def masked(k, a, n, at):
+        tt(T.gm[:, at:at + n], bank[k][:, a:a + n], T.mk[:, at:at + n], A.mult, ["b%d" % k, "mk"],
+           ["gm%d" % q for q in range(at // 32, (at + n) // 32)])
+        close("v")
 
     def blend(tile, at, n, win, lst, da, rd, wr):
         tt(tile[:, at:at + n], win.indirect(lst), da, A.add, rd, wr)
         close("v")
 
+    def win(a):
+        return T.lq[:, a:a + 128], T.ls[:, a:a + 128]
+
     L = ["lin", "lown"]
-    mm(4, 128, T.lq[:, 192:320], T.ls[:, 192:320], T.lq[:, 0:128], T.ls[:, 0:128], L)
-    mm(5, 128, T.lq[:, 256:384], T.ls[:, 256:384], T.lq[:, 64:192], T.ls[:, 64:192], L)
-    decode(384, T.lq[:], T.ls[:], L)
-    masked(4, 0, 128, 0, 0, "gm1")
-    masked(5, 64, 64, 64, 192, "gm2")
-    op("s", lambda: g.sync.dma_start(T.wt[:], T.w[:]), r=["lin"], w=["wt"], dma=True)
+    a0, u0 = 128 * (1 - b0), 128 * b0
+    mm(4, 128, *win(u0), *win(a0), L)
+    decode(256, T.lq[:, 0:256], T.ls[:, 0:256], L)
+    masked(4, 0, 128, 0)
+    op("s", lambda: g.sync.dma_start(T.wt[:], T.w[:]), r=["lin", "yin"], w=["wt"], dma=True)
     close("s")
     for b in range(4):
-        act(T.d0[:, b:1536:4], bank[b][:, 0:384], ["b%d" % b], ["d0%d" % b], scale=0.5)
+        act(T.d0[:, b:1024:4], bank[b][:, 0:256], ["b%d" % b], ["d0%d" % b], scale=0.5)
     close("a")
     D0 = ["d0%d" % b for b in range(4)]
-    align(T.l0, "l0", 4, 0, 16, 0, XA, ["xt0"])
-    quant(T.wq[:], T.ws[:], T.wt[:], ["wt"], ["wq"])
+    ay, uy = 256 + 64 * b0, 320 - 64 * b0
+    Y = ["lin", "lown", "yin"] + (["lpad"] if not b0 and b1 else [])
+    mm(6, 128, *win(uy - 64 * ha1), *win(256), Y)
+    align(T.xa, 32, T.ma[:], ["ma", "xaz", "xa1"], "xa0", 0)
+    masked(6, ay - 256, 64, 64 * ha1)
     offsets(T.o0, 32, "o0")
-    blend(T.mt, 0, 512, T.d0[:, 768:1536], T.o0[:], T.d0[:, 256:768], D0 + ["o0"], ["mt0"])
+    blend(T.mt, 0, 512, T.d0[:, 4 * u0:4 * u0 + 512], T.o0[:], T.d0[:, 4 * a0:4 * a0 + 512], D0 + ["o0"], ["mt0"])
     quant(T.m0q[:], T.m0s[:], T.mt[:], ["mt0"], ["m0"])
+    store("s", T.pf[0:1, 0:64], T.pc[64:128, 0:1], ["pc0"], ["pfk"])
+    close("s")
 
-    def prod(o, q, s, rd):
-        mm(6 + o, 128, T.wq[:, 128 * o:128 * o + 128], T.ws[:, 128 * o:128 * o + 128], q, s, ["wq"] + rd)
-
-    ha1 = 1 - hb1
-    pars = (1 - keep1, keep1)
     mm(4, 128, T.m0q[:], T.m0s[:], T.m0q[:], T.m0s[:], ["m0"])
     decode(128, T.m0q[:], T.m0s[:], ["m0"])
-    for o in range(2):
-        prod(o, T.m0q[:], T.m0s[:], ["m0"])
-    masked(4, 64 * ha1, 64, 64 * hb1, 64 * hb1, "gm1")
+    masked(4, 64 * ha1, 64, 64 * hb1)
     for b in range(4):
-        act(T.d1[:, b:512:4], bank[b][:, 0:128], ["b%d" % b], ["d1%d" % b], scale=0.5)
-    close("a")
-    for o in range(2):
-        for h in range(2):
-            act(T.y0[:, 4 * o:4 * o + 4, 2 * pars[h] + b1, :], bank[6 + o][:, 32 * h:32 * h + 32], ["b%d" % (6 + o)], ["y0k%d%d" % (o, h)])
+        act(T.d1a[:, :, :, b:32:4], bank[b][:, 64 * ha1:64 * ha1 + 64], ["b%d" % b], ["d1a%d" % b], scale=0.5)
+        act(T.d1b[:, b:256:4], bank[b][:, 64 * hb1:64 * hb1 + 64], ["b%d" % b], ["d1b%d" % b], scale=0.5)
         close("a")
-    act(T.jt[:, 0:256:4], T.xt[:, 0:64], ["xt0"] + JT, ["j0"])
+    decode(128, *win(256), Y)
+    for h, par in enumerate((1 - b2, b2)):
+        act(T.d1s[:, 128 * h:128 * h + 128], T.d1a[:, :, par, :], ["d1a%d" % b for b in range(4)], ["d1s%d" % h])
     close("a")
-    D1 = ["d1%d" % b for b in range(4)]
-    win1 = T.d1[:, 256 * hb1:256 * hb1 + 256]
-    align(T.l1, "l1", 8, 16, 8, 512, XB + ["xu"], ["xt4"])
-    act(T.jt[:, 256:768:4], T.xt[:, 512:640], ["xt4", "xu"] + JT, ["j1"])
+    for b in range(4):
+        act(T.dy[:, b:512:4], bank[b][:, 0:128], ["b%d" % b], ["dy%d" % b], scale=0.5)
     close("a")
+    D1 = ["d1b%d" % b for b in range(4)] + ["d1s0", "d1s1"]
+    DY = ["dy%d" % b for b in range(4)]
+    align(T.xb, 32, T.mb[:], ["mb0", "mb1", "mb2", "xbz", "xb1", "xb2"], "xb0", 4)
     offsets(T.o1, 32, "o1")
-    blend(T.mt, 0, 128, win1, T.o1[:, 0:8], T.d1[:, 256 * ha1:256 * ha1 + 128], D1 + ["o1"], ["mt0"])
+    blend(T.mt, 0, 128, T.d1b[:], T.o1[:, 0:8], T.d1s[:, 0:128], D1 + ["o1"], ["mt0"])
     quant(T.m1q[:], T.m1s[:], T.mt[:], ["mt0"], ["m1"])
     need("g", ["m1"])
-    (m8,), n8 = masks(c4, 1)
+    e8 = topo.engines(core, c4)
     rid, pid = int(topo.addr(c4)[0]), int(topo.addr(c4)[1])
-    g.remote_dma(T.hq[:, 128:160].bitcast(dt.uint8), T.m1q[:, 0:32].bitcast(dt.uint8), T.sem.arr2, T.sem.sent, pid, rid, m8)
-    g.remote_dma(T.hs[:, 128:160], T.m1s[:, 0:32], T.sem.arr2, T.sem.sent, pid, rid, m8)
-    sent += 2 * n8
-    landed("hin", "arr2", 2 * n8)
+    g.remote_dma(T.hq[:, 128:160].bitcast(dt.uint8), T.m1q[:, 0:32].bitcast(dt.uint8), T.sem.arr2, T.sem.sent, pid, rid, mask_of(e8))
+    g.remote_dma(T.hs[:, 128:160], T.m1s[:, 0:32], T.sem.arr2, T.sem.sent, pid, rid, mask_of(e8))
+    sent += 2 * len(e8)
+    landed("hin", "arr2", 2 * len(e8))
 
-    blend(T.mu, 384, 128, win1, T.o1[:, 8:16], T.d1[:, 256 * ha1 + 128:256 * ha1 + 256], D1 + ["o1"], ["mu0"])
-    blend(T.mu, 128, 256, T.d0[:, 768:1536], T.o1[:, 16:32], T.d0[:, 0:256], D0 + ["o1"], ["mu1"])
-    quant(T.jq[:], T.js[:], T.jt[:, 0:768], ["j0", "j1"], ["jq"])
+    blend(T.mu, 384, 128, T.d1b[:], T.o1[:, 8:16], T.d1s[:, 128:256], D1 + ["o1"], ["mu0"])
+    blend(T.mu, 128, 256, T.dy[:, 4 * (uy - 256):4 * (uy - 256) + 256], T.o1[:, 16:32],
+          T.dy[:, 4 * (ay - 256):4 * (ay - 256) + 256], DY + ["o1"], ["mu1"])
+    quant(T.wq[:], T.ws[:], T.wt[:], ["wt"], ["wq"])
     quant(T.hq[:, 0:128], T.hs[:, 0:128], T.mu[:], ["mu0", "mu1", "muz"], ["hown"])
-    for o in range(2):
-        prod(o, T.m1q[:], T.m1s[:], ["m1"])
-    mm(0, 192, T.stq[:], T.sts[:], T.jq[:], T.js[:], ["stq", "jq"])
-    for o in range(2):
-        act(T.y1[:, 4 * o:4 * o + 4, 1 - keep1, :], bank[6 + o][:, 0:32], ["b%d" % (6 + o)], ["y1s%d" % o])
-        close("a")
-    for h in range(2):
-        act(T.p0[0:1, :, 2 * pars[h] + b1, :], bank[0][0:1, 32 * h:32 * h + 32], ["b0"], ["p0k%d" % h], scale=0.25)
-        act(T.p1[0:1, :, pars[h], :], bank[0][0:1, 64 + 32 * h:96 + 32 * h], ["b0"], ["p1%d" % h], scale=0.25)
-        act(T.p0[0:1, :, 2 * pars[h] + 1 - b1, :], bank[0][0:1, 128 + 32 * h:160 + 32 * h], ["b0"], ["p0u%d" % h], scale=0.25)
-    close("a")
 
-    qa2 = 5 - qb2
+    def prod(k, q, s, rd):
+        for o in range(2):
+            mm(k + o, 128, T.wq[:, 128 * o:128 * o + 128], T.ws[:, 128 * o:128 * o + 128], q, s, ["wq"] + rd)
+
+    prod(0, T.m0q[:], T.m0s[:], ["m0"])
+    prod(2, T.m1q[:], T.m1s[:], ["m1"])
+    prod(6, T.hq[:, 0:128], T.hs[:, 0:128], ["hown"])
+    for o in range(2):
+        act(T.ya[:, 12 * o:12 * o + 8, b1, :], bank[o][:, 64:128], ["b%d" % o], ["ya0%d" % o])
+        act(T.ya[:, 12 * o + 8:12 * o + 12, 1 - b2, :], bank[2 + o][:, 0:32], ["b%d" % (2 + o)], ["ya1%d" % o])
+        close("a")
+    for o in range(2):
+        act(T.ya[:, 12 * o:12 * o + 8, 1 - b1, :], bank[6 + o][:, 32:96], ["b%d" % (6 + o)], ["ya2%d" % o])
+        act(T.ya[:, 12 * o + 8:12 * o + 12, b2, :], bank[6 + o][:, 96:128], ["b%d" % (6 + o)], ["ya3%d" % o])
+        close("a")
+
     H = ["hin", "hown"]
     mm(4, 128, T.hq[:, 32:160], T.hs[:, 32:160], T.hq[:, 32:160], T.hs[:, 32:160], H)
-    for o in range(2):
-        prod(o, T.hq[:, 0:128], T.hs[:, 0:128], ["hown"])
     decode(128, T.hq[:, 32:160], T.hs[:, 32:160], H)
-    masked(4, 32 * qa2, 32, 32 * qb2, 32 * qb2, "gm1")
+    masked(4, 32 * qa2, 32, 32 * qb2)
     for b in range(4):
         act(T.d2[:, b:256:4], bank[b][:, 64:128], ["b%d" % b], ["d2%d" % b], scale=0.5)
     close("a")
+    store("s", T.pf[0:1, 64:128], T.pc[64 * ha1:64 * ha1 + 64, 4:5], ["pc4", "hin"], ["pfu"])
+    close("s")
+    store("s", T.pt[0:1, 128:192], T.pc[64 * hb1:64 * hb1 + 64, 4:5], ["pc4"])
     for o in range(2):
-        act(T.y1[:, 4 * o:4 * o + 4, keep1, :], bank[6 + o][:, 96:128], ["b%d" % (6 + o)], ["y1k%d" % o])
-        for h in range(2):
-            act(T.y0[:, 4 * o:4 * o + 4, 2 * pars[h] + 1 - b1, :], bank[6 + o][:, 32 + 32 * h:64 + 32 * h], ["b%d" % (6 + o)], ["y0u%d%d" % (o, h)])
-        close("a")
-    store("s", T.pt[0:1, 0:128], T.p0[0:1, :, :, :], ["p0k0", "p0k1", "p0u0", "p0u1"])
-    store("s", T.pt[0:1, 128:192], T.p1[0:1, :, :, :], ["p10", "p11"])
-    for o in range(2):
-        store("sa"[o], T.y[:, 224 * o:224 * o + 128], T.y0[:, 4 * o:4 * o + 4, :, :], ["y0%s%d%d" % (u, o, h) for u in "ku" for h in range(2)])
-        store("sa"[o], T.y[:, 224 * o + 128:224 * o + 192], T.y1[:, 4 * o:4 * o + 4, :, :], ["y1k%d" % o, "y1s%d" % o])
-    align(T.l1, "l1", 8, 32, 4, 128, XA + ["xt4", "xu"], ["xt1"])
-    act(T.jt[:, 768:896:4], T.xt[:, 128:160], ["xt1"] + JT, ["j3"])
+        store("sa"[o], T.y[:, 224 * o:224 * o + 192], T.ya[:, 12 * o:12 * o + 12, :, :], ["ya%d%d" % (u, o) for u in range(4)])
+    close("s")
     close("a")
-    quant(T.j2q[:], T.j2s[:], T.jt[:, 384:896], ["j1", "j3"], ["j2q"])
-    mm(0, 128, T.stq[:], T.sts[:], T.j2q[:], T.j2s[:], ["stq", "j2q"])
-    act(T.p2[0:1, :], bank[0][0:1, 96:128], ["b0"], ["p2"], scale=0.25)
+    act(T.p0[0:1, :, b1, :], T.pf[0:1, 0:64], ["pfk"], ["p0k"])
+    act(T.p0[0:1, :, 1 - b1, :], T.pf[0:1, 64:128], ["pfu"], ["p0u"])
     close("a")
-    store("a", T.pt[0:1, 192:224], T.p2[0:1, :], ["p2"])
+    store("s", T.pt[0:1, 0:128], T.p0[0:1, :, :, :], ["p0k", "p0u"])
+    close("s")
+    align(T.xa, 8, T.ma[:, 2 * qb2:2 * qb2 + 2, :, :], ["ma", "xaz", "xa1"], "xa0", 8)
+    store("a", T.pt[0:1, 192:224], T.pc[32 * qb2:32 * qb2 + 32, 8:9], ["pc8"])
+    close("a")
     D2 = ["d2%d" % b for b in range(4)]
     offsets(T.o2, 8, "o2")
     ha2, hb2 = qa2 - 2, qb2 - 2
     blend(T.mt, 0, 128, T.d2[:, 128 * hb2:128 * hb2 + 128], T.o2[:], T.d2[:, 128 * ha2:128 * ha2 + 128], D2 + ["o2"], ["mt0"])
     quant(T.m2q[:], T.m2s[:], T.mt[:], ["mt0"], ["m2"])
-    for o in range(2):
-        prod(o, T.m2q[:], T.m2s[:], ["m2"])
+    prod(6, T.m2q[:], T.m2s[:], ["m2"])
     store("s", T.oc[:, 0:128], T.m2q[:, 0:32].bitcast(dt.uint8), ["m2"])
     for k in range(4):
         store("sa"[k % 2], T.osc[4 * k:4 * k + 4, 0:32], T.m2s[32 * k:32 * k + 4, 0:32], ["m2"])
-    for o in range(2):
-        copy(T.y2[:, 32 * o:32 * o + 32], bank[6 + o][:, 0:32], ["b%d" % (6 + o)], ["y2%d" % o])
-        close("v")
+    copy(T.y2[:, 0:32], bank[6][:, 0:32], ["b6"], ["y20"])
+    close("v")
+    act(T.y2[:, 32:64], bank[7][:, 0:32], ["b7"], ["y21"])
+    close("a")
     store("s", T.y[:, 192:224], T.y2[:, 0:32], ["y20"])
     store("a", T.y[:, 416:448], T.y2[:, 32:64], ["y21"])
     g.wait_ge(T.sem.sent, sent)

@@ -4,7 +4,7 @@ from concourse.mybir import dt, AluOpType, ActivationFunctionType
 F32, BF, I32, U16, X4, U8 = "float32", "bfloat16", "int32", "uint16", "float8_e4m3fn_x4", "uint8"
 LOW = -1.0e29
 UNIT = 0.125
-ORDER = ("p0 a0 a1 x1 b0 p1 q1 b1 m1 p2 q2 d1 l1 d2 p3 q3 l2 h1 g1 d3 p4 q4 l3 h2 g2 d4 p5 q5 l4 h3 g3 d5 p6 q6 l5 h4 g4 d6 "
+ORDER = ("b0 p0 q0 b1 a0 a1 p1 q1 d1 p2 q2 l1 d2 p3 q3 h1 g1 l2 d3 p4 q4 l3 h2 g2 d4 p5 q5 l4 h3 g3 d5 p6 q6 l5 h4 g4 d6 "
          "p7 l6 h5 g5 d7 l7 h6 g6 h7").split()
 
 
@@ -16,20 +16,19 @@ SCRATCH = {
     "xs": _sb([8, 4, 32], BF), "xt": _sb([1024], BF), "wt": _sb([1024], BF),
     "sq": _sb([128], X4), "ss": _sb([128], U8), "lq": _sb([512], X4), "ls": _sb([512], U8),
     "wq": _sb([256], X4), "ws": _sb([256], U8),
-    "et": _sb([2048], BF), "eq": _sb([512], X4), "es": _sb([512], U8),
+    "et": _sb([520], BF), "eq": _sb([512], X4), "es": _sb([512], U8),
     "st": _sb([512], BF), "stq": _sb([128], X4), "sts": _sb([128], U8),
     "pi": _sb([2], I32), "fi": _sb([8], I32), "ff": _sb([12], F32),
-    "uu": _sb([128], F32), "vv": _sb([128], BF), "tt": _sb([128], BF), "zz": _sb([368], BF),
+    "uu": _sb([128], F32), "vv": _sb([128], BF), "tt": _sb([128], BF), "zz": _sb([420], BF),
     "mk": _sb([128], F32), "cl": _sb([16], F32), "l0": _sb([16], U16), "lg": _sb([4], U16),
-    "kj": _sb([32], F32), "ke": _sb([8], F32), "ma": _sb([8, 2, 2], F32), "mb": _sb([32], F32),
+    "kj": _sb([32], F32), "ke": _sb([8], F32), "ma": _sb([8, 2, 2], F32),
     "gm": _sb([128], F32), "gb": _sb([256], F32), "tb": _sb([256], F32), "g3": _sb([96], F32), "g4": _sb([128], F32),
-    "pb": _sb([36], F32), "q0": _sb([32], F32), "q1": _sb([32], F32), "du": _sb([8], F32),
-    "pr": _sb([720], F32), "p7": _sb([32], F32),
-    "km": _sb([320], F32), "hz": _sb([32], F32), "hr": _sb([1104], F32), "h7": _sb([32], F32),
-    "xa": _sb([512], BF), "xb": _sb([512], BF), "xq": _sb([128], X4), "xsc": _sb([128], U8),
+    "q0": _sb([32], F32), "pr": _sb([840], F32), "p7": _sb([24], F32),
+    "km": _sb([280], F32), "k7": _sb([384], F32), "hz": _sb([32], F32), "hr": _sb([1728], F32),
+    "xa": _sb([512], BF), "xq": _sb([128], X4), "xsc": _sb([128], U8),
     "o0": _sb([32], U16), "o1": _sb([32], U16), "o2": _sb([8], U16),
-    "d0": _sb([1024], F32), "dy": _sb([512], F32), "d2": _sb([256], F32),
-    "d1a": _sb([4, 2, 32], F32), "d1b": _sb([256], F32), "d1s": _sb([256], F32),
+    "d0": _sb([1024], F32), "dy": _sb([512], F32), "dz": _sb([256], F32), "d2": _sb([512], F32), "d2a": _sb([128], F32),
+    "d1a": _sb([4, 2, 32], F32), "d1f": _sb([512], F32), "d1s": _sb([256], F32),
     "mt": _sb([512], BF), "mu": _sb([512], BF),
     "m0q": _sb([128], X4), "m0s": _sb([128], U8), "m1q": _sb([128], X4), "m1s": _sb([128], U8),
     "hq": _sb([160], X4), "hs": _sb([160], U8), "m2q": _sb([128], X4), "m2s": _sb([128], U8),
@@ -138,11 +137,11 @@ def rank_program(g, core, T, topo):
         a = topo.addr(c)
         return DstId(rid=int(a[0]), pnc=int(a[1]))
 
-    def iota(out, pat, base, cm, key, small=True, rd=()):
+    def iota(out, pat, base, cm, key, small=True):
         if small:
-            op("g", lambda: g.iota(out, pat, base, cm, allow_small_or_imprecise_dtypes=True), r=rd, w=[key])
+            op("g", lambda: g.iota(out, pat, base, cm, allow_small_or_imprecise_dtypes=True), w=[key])
         else:
-            op("g", lambda: g.iota(out, pat, base, cm), r=rd, w=[key])
+            op("g", lambda: g.iota(out, pat, base, cm), w=[key])
 
     def fill(out, val, key, rd=()):
         op("v", lambda: V.memset(out, val), r=rd, w=[key])
@@ -182,6 +181,9 @@ def rank_program(g, core, T, topo):
         eng = {"s": g.sync, "a": S}[q]
         op(q, lambda: eng.dma_start(out, in_), r=rd, w=wr, dma=True)
 
+    def run(t, a, n, s):
+        return t[:, a:a + s * (n - 1) + 1:s]
+
     op("s", lambda: g.sync.dma_start(T.xs[:], T.x[:]), w=["xs"], dma=True)
     close("s")
 
@@ -192,28 +194,35 @@ def rank_program(g, core, T, topo):
     iota(T.kj[:], [[1, 32]], 0, 0, "kj")
     iota(T.cl[:], [[1, 8], [16, 2]], 0, 0, "cl")
     close("g")
-    iota(T.vv[:], [[1, 128]], 0, -1, "vv")
     iota(T.uu[:], [[1, 16], [0, 8]], 0, 0, "uu")
+    close("g")
+    iota(T.vv[:], [[1, 128]], 0, -1, "vv")
+    close("g")
     iota(T.tt[:], [[0, 8], [1, 4], [0, 4]], 0, 0, "tt")
     close("g")
     fill(T.zz[:], 0.0, "zz")
     close("v")
-    fill(T.et[:], 0.0, "et")
+    fill(T.et[:], 0.0, "etz")
     close("v")
     for k, (sh, m) in enumerate([(0, 3), (0, 7), (3, 15), (2, 31), (0, 104), (0, 16), (3, 1)]):
         ts(T.fi[:, k:k + 1], T.pi[:, 0:1], sh, m, A.logical_shift_right, A.bitwise_and, ["pi"], ["fi%d" % k])
     close("v")
-    afill(T.pr[:, 0:360], 360, LOW, "prz0")
-    afill(T.pr[:, 360:720], 360, LOW, "prz1")
-    afill(T.km[:], 320, 0.0, "kmz")
-    afill(T.pb[:, 3:4], 1, LOW, "pad")
+    afill(T.pr[:, 0:420], 420, LOW, "prz0")
+    afill(T.pr[:, 420:840], 420, LOW, "prz1")
     afill(T.q0[:], 32, LOW, "top")
-    afill(T.q1[:], 32, LOW, "x1")
     close("a")
-    afill(T.q0[:, 0:1], 1, 0.0, "top")
+    afill(T.km[:], 280, 0.0, "kmz")
     close("a")
     col = lambda k: T.ff[:, k:k + 1]
+    fill(T.xa[:, 64:512], 0.0, "h7")
+    close("v")
     copy(T.ff[:, 0:7], T.fi[:, 0:7], ["fi%d" % k for k in range(7)], ["ff"])
+    close("v")
+    fill(T.st[:, 3:512:4], 0.0, "st3")
+    close("v")
+    ts(T.ke[:], T.kj[:, 0:8], col(1), None, A.is_equal, None, ["kj", "ff"], ["ke"])
+    ts(T.ma[:], T.kj[:], col(3), None, A.is_equal, None, ["kj", "ff"], ["ma"])
+    ts(col(8), col(1), 32.0, col(5), A.mult, A.add, ["ff"], ["f8"])
     close("v")
 
     order = [(r ^ k) % 4 for k in (1, 3, 0, 2)]
@@ -223,6 +232,8 @@ def rank_program(g, core, T, topo):
         copy(T.xt[:, 256 * k:256 * k + 256], T.xs[:, :, order[k], :], ["xs"], ["xt%d" % k])
     close("v")
     copy(T.xt[:, 768:1024], T.xs[:, :, order[3], :], ["xs"], ["xt3"])
+    close("v")
+    ts(T.l0[:], T.cl[:], col(4), None, A.add, None, ["cl", "ff"], ["l0"])
     close("v")
     quant(T.sq[:], T.ss[:], T.xt[:, 0:512], ["xt0", "xt1"], ["sq"])
     quant(T.lq[:, 192:320], T.ls[:, 192:320], T.xt[:, 512:1024], ["xt2", "xt3"], ["lown"])
@@ -249,118 +260,112 @@ def rank_program(g, core, T, topo):
     landed("lin", "arr0", 2 * len(e))
     landed("yin", "arry", 2 * len(e))
 
-    for k in range(3):
-        afill(T.hr[:, 368 * k:368 * k + 368], 368, 0.0, "hrz%d" % k)
-    afill(T.hz[:], 32, 0.0, "hzz")
+    kp = lambda j: 4 - j % 2
+    kh = lambda j: 5 - j % 2
+    afill(T.q0[:, 0:1], 1, 0.0, "top")
     afill(T.g3[:, 0:96:3], 32, 0.0, "g3z")
     afill(T.g4[:], 128, 0.0, "g4z")
+    afill(T.hz[:], 32, 0.0, "hzz")
+    for k in range(3):
+        afill(T.hr[:, 368 * k:368 * k + 368], 368, 0.0, "hrz%d" % k)
+    afill(run(T.hr, 1108, 124, 5), 124, 0.0, "hrz3")
+    close("a")
+    afill(T.k7[:], 384, 0.0, "k7z")
+    close("a")
+    HRZ = ["hrz0", "hrz1", "hrz2", "hrz3"]
+    act(T.hz[:, 2:32:4], T.ke[:], ["ke", "hzz"], ["hc1"], scale=UNIT)
+    for j in range(1, 7):
+        act(run(T.hr, 184 * (j - 1) + 8 + 2 * kh(j), 8, 20), T.ke[:], ["ke"] + HRZ, ["hc%d" % (j + 1)], scale=(j + 1) * UNIT)
+    act(run(T.k7, 33, 32, 4), T.ma[:], ["ma", "k7z"], ["k70"])
+    act(run(T.k7, 193, 8, 4), T.ma[:, 4 * hb1:4 * hb1 + 4, 1 - b2, :], ["ma", "k7z"], ["k71"])
+    act(run(T.k7, 225, 8, 4), T.ma[:, 4 * hb1:4 * hb1 + 4, b2, :], ["ma", "k7z"], ["k72"])
+    act(run(T.k7, 257, 16, 4), T.ma[:, 4 * ha1:4 * ha1 + 4, :, :], ["ma", "k7z"], ["k73"])
+    act(run(T.k7, 353, 8, 4), T.ma[:, 2 * qb2:2 * qb2 + 2, :, :], ["ma", "k7z"], ["k74"])
     afill(T.mu[:, 0:128], 128, 0.0, "muz")
     close("a")
-    fill(T.xa[:], 0.0, "xaz")
-    fill(T.xb[:], 0.0, "xbz")
-    close("v")
-    iota(T.xa[0:1, 1:128:4], [[1, 16], [0, 2]], 0, 0, "xa1", rd=["xaz"])
-    iota(T.xb[0:1, 1:64:4], [[2 * b2 - 1, 2], [2, 4], [0, 2]], 1 - b2, 0, "xb1", rd=["xbz"])
-    iota(T.xb[0:1, 65:128:4], [[1, 8], [0, 2]], 0, 0, "xb2", rd=["xbz"])
-    close("g")
-    for b in range(4):
-        ts(T.et[:, 512 * b + b:512 * b + 512:4], T.vv[:], 0.0, None, A.is_equal, None, ["vv", "et"], ["et%d" % b])
-    close("v")
-    ts(T.ke[:], T.kj[:, 0:8], col(1), None, A.is_equal, None, ["kj", "ff"], ["ke"])
-    ts(T.ma[:], T.kj[:], col(3), 1.0 / UNIT, A.is_equal, A.mult, ["kj", "ff"], ["ma"])
-    ts(col(8), col(1), 32.0, col(5), A.mult, A.add, ["ff"], ["f8"])
-    close("v")
-    quant(T.eq[:], T.es[:], T.et[:], ["et0", "et1", "et2", "et3"], ["eq"])
-    ts(col(9), col(6), 2.0, col(8), A.mult, A.add, ["ff", "f8"], ["f9"])
+    K7 = ["k7%d" % k for k in range(5)]
+    ts(T.et[:, 4:516:4], T.vv[:], 0.0, None, A.is_equal, None, ["vv", "etz"], ["et"])
     close("v")
     ts(T.mk[:], T.uu[:], col(2), None, A.is_equal, None, ["uu", "ff"], ["mk"])
-    ts(T.l0[:], T.cl[:], col(4), None, A.add, None, ["cl", "ff"], ["l0"])
+    ts(col(9), col(6), 2.0, col(8), A.mult, A.add, ["ff", "f8"], ["f9"])
+    ts(col(10), col(2), 1.0, 32.0, A.add, A.mult, ["ff"], ["f10"])
+    ts(col(11), col(2), -32.0, None, A.mult, None, ["ff"], ["f11"])
+    close("v")
+    for b in range(4):
+        op("v", lambda: V.quantize_mx(T.eq[:, 128 * b:128 * b + 128], T.es[:, 128 * b:128 * b + 128], T.et[:, 4 - b:516 - b]),
+           r=["et"], w=["eq%d" % b])
     close("v")
     for u in range(2):
         ts(T.lg[:, 2 * u:2 * u + 2], T.kj[:, u:8:4], col(9), None, A.add, None, ["kj", "f9"], ["lg%d" % u])
     close("v")
+    for t, s in enumerate((col(10), col(11), -32.0)):
+        ts(T.st[:, t:512:4], T.tt[:], col(0), s, A.is_equal, A.mult, ["tt", "ff", "f10", "f11"], ["st%d" % t])
+    close("v")
     if not b0 and b1:
         quant(T.lq[:, 384:512], T.ls[:, 384:512], T.xt[:, 0:512], ["xt0", "xt1"], ["lpad"])
-    kp = lambda j: 3 + j % 2
-    kh = lambda j: 5 - j % 2
-    HRZ = ["hrz0", "hrz1", "hrz2"]
-    act(T.hz[:, 2:32:4], T.ke[:], ["ke", "hzz"], ["hc1"], scale=UNIT)
-    for j in range(1, 7):
-        a = 184 * (j - 1) + 8 + 2 * kh(j)
-        act(T.hr[:, a:a + 160:20], T.ke[:], ["ke"] + HRZ, ["hc%d" % (j + 1)], scale=(j + 1) * UNIT)
-    act(T.mb[:, 0:8], T.ma[:, 4 * hb1:4 * hb1 + 4, 1 - b2, :], ["ma"], ["mb0"])
-    act(T.mb[:, 8:16], T.ma[:, 4 * hb1:4 * hb1 + 4, b2, :], ["ma"], ["mb1"])
-    act(T.mb[:, 16:32], T.ma[:, 4 * ha1:4 * ha1 + 4, :, :], ["ma"], ["mb2"])
-    close("a")
-    fill(T.st[:], 0.0, "stz")
-    close("v")
-    ts(T.st[:, 0:512:4], T.tt[:], col(0), 4.0, A.is_equal, A.mult, ["tt", "ff", "stz"], ["st0"])
-    fill(T.st[0:1, 1:512:4], 32.0, "st1", ["stz"])
-    close("v")
-    quant(T.stq[:], T.sts[:], T.st[:], ["st0", "st1"], ["stq"])
-    path = T.h7[:, 31:32]
 
     def decode(n, q, s, rd):
         for b in range(4):
-            mm(b, n, T.eq[:, 128 * b:128 * b + 128], T.es[:, 128 * b:128 * b + 128], q, s, ["eq"] + rd)
-
-    def run(t, a, n, s):
-        return t[:, a:a + s * (n - 1) + 1:s]
+            mm(b, n, T.eq[:, 128 * b:128 * b + 128], T.es[:, 128 * b:128 * b + 128], q, s, ["eq%d" % b] + rd)
 
     def sums(j, back):
-        if j == 0:
-            return run(T.pb, 7 - 4 * back, 8, 4), ["pad", "p0"]
-        return run(T.pr, 120 * (j - 1) + 12 + kp(j) - 12 * back, 8, 12), ["prz0", "prz1", "p%d" % j]
+        return run(T.pr, 120 * j + 12 + kp(j) - 12 * back, 8, 12)
 
-    def step(name):
+    def step(name, k7, n7):
         kind, j = name[0], int(name[1])
         if kind in "ab":
-            t, k = (T.g3, 3) if kind == "a" else (T.g4, 4)
-            copy(run(t, 1 + j, 32, k), T.tb[:, 8 * j:256].indirect(T.lg[:, 2 * (k - 3):2 * (k - 3) + 2]),
-                 ["tb", "g%dz" % k, "lg%d" % (k - 3)], ["s" + name], True)
-        elif kind == "x":
-            tt(T.q1[:, 0:32:4], sums(0, 1)[0], sums(0, 0)[0], A.max, sums(0, 0)[1], ["x1"], True)
-        elif kind == "m":
-            tt(T.du[:], sums(0, 1)[0], sums(1, 1)[0], A.max, sums(0, 0)[1] + sums(1, 0)[1], ["du"], True)
+            t, k, u = (T.g4, 4, 0) if kind == "a" else (T.g3, 3, 1)
+            args = (run(t, 1 + j, 32, k), T.tb[:, 8 * j:256].indirect(T.lg[:, 2 * u:2 * u + 2]),
+                    ["tb", "g%dz" % k, "lg%d" % u], ["s" + name])
+            if name == "b0":
+                act(*args)
+                close("a")
+            else:
+                copy(*args, True)
         elif kind in "pq":
             k, n = kp(j), kp(j + 1)
-            if j == 0:
-                return scan(T.pb[:, 4:36], T.q0[:], T.tb[:, 0:256:8], LOW, A.add, ["tb", "top"], ["p0"])
-            at = 120 * (j - 1) + (12 + k if kind == "p" else 24) - n * (3 if j == 1 else 2)
+            at = 120 * j + (12 + k if kind == "p" else 24) - n * (2 if j else 3)
             out = T.p7[:] if j == 7 else run(T.pr, at, 8 * k, n)
-            if j == 1:
-                return scan(out, T.q1[:], T.tb[:, 1:256:8], LOW, A.add, ["tb", "x1", "prz0", "prz1"], [name])
-            t, u = (T.g3, "a") if k == 3 else (T.g4, "b")
-            scan(out, run(T.pr, 120 * (j - 2) + 12, 8 * k, n), t[:, 8 * k * (j // 2):8 * k * (j // 2 + 1)], LOW, A.add,
+            if j == 0:
+                return scan(out, T.q0[:], T.tb[:, 0:256:8], LOW, A.add, ["tb", "top", "prz0", "prz1"], [name])
+            t, u = (T.g3, "b") if k == 3 else (T.g4, "a")
+            scan(out, run(T.pr, 120 * (j - 1) + 12, 8 * k, n), t[:, 8 * k * (j // 2):8 * k * (j // 2 + 1)], LOW, A.add,
                  ["s%s0" % u, "s%s1" % u, "p%d" % (j - 1), "q%d" % (j - 1)], [name])
         elif kind in "dl":
-            m = T.du[:] if j == 1 else T.p7[:, 0:32:4] if j == 7 else run(T.pr, 120 * (j - 1) + 12 + kp(j) - 2 * kp(j + 1), 8, 12)
-            s, rd = sums(j - 1, int(kind == "d"))
-            if name == "d1":
-                m = sums(1, 1)[0]
-            tt(run(T.km, 40 * j + (0 if kind == "d" else 2), 8, kh(j)), s, m, A.is_ge if kind == "d" else A.is_gt,
-               rd + ["kmz", "p%d" % j] + (["du"] if name == "l1" else []), ["k" + name], True)
+            m = T.p7[:, 0:24:3] if j == 7 else run(T.pr, 120 * j + 12 + kp(j) - 2 * kp(j + 1), 8, 12)
+            at = 0 if kind == "d" else 2
+            out = run(T.k7, k7 + at, 8, 4) if j == 7 else run(T.km, 40 * j + at, 8, kh(j))
+            tt(out, sums(j - 1, int(kind == "d")), m, A.is_ge if kind == "d" else A.is_gt,
+               ["kmz", "k7z", "p%d" % (j - 1), "p%d" % j], ["k" + name], True)
         else:
             k, n = kh(j), kh(j + 1)
+            rd = HRZ + ["hc%d" % j, "h%d" % (j - 1), "g%d" % (j - 1), "kd%d" % j, "kl%d" % j]
+            if j == 7:
+                return scan(T.xa[:, 0:n7], run(T.hr, 184 * 5 + 8, n7, n), T.k7[:, k7:k7 + n7], 0.0, A.subtract, rd + K7, [name])
             at = 184 * (j - 1) + (8 + 3 * k if kind == "h" else 28 + k) - 3 * n
-            scan(T.h7[:] if j == 7 else run(T.hr, at, 8 * k, n), T.hz[:] if j == 1 else run(T.hr, 184 * (j - 2) + 8, 8 * k, n),
-                 T.km[:, 40 * j:40 * j + 8 * k], 0.0, A.subtract,
-                 HRZ + ["hc%d" % j, "h%d" % (j - 1), "g%d" % (j - 1), "kd%d" % j, "kl%d" % j], [name])
+            scan(run(T.hr, at, 8 * k, n), T.hz[:] if j == 1 else run(T.hr, 184 * (j - 2) + 8, 8 * k, n),
+                 T.km[:, 40 * j:40 * j + 8 * k], 0.0, A.subtract, rd, [name])
 
-    def align(x, n, m, rd, key, slot):
-        copy(T.gb[:], T.gm[:].indirect(T.l0[:]), ["gm0", "gm1", "gm2", "gm3", "l0"], ["gb"])
-        op("v", lambda: V.transpose(T.tb[:], T.gb[:]), r=["gb"], w=["tb"])
-        for name in ORDER:
-            step(name)
-        ts(x[:, 0:4 * n:4], m, path, None, A.mult, None, ["h7"] + rd, [key])
-        close("v")
-        act(T.pc[:, slot:slot + 1], path, ["h7"], ["pc%d" % slot], scale=1.0 / UNIT)
+    def gather():
+        GM = ["gm0", "gm1", "gm2", "gm3", "l0"]
+        act(T.gb[:, 128:256], T.gm[:].indirect(T.l0[:, 8:16]), GM, ["gb1"])
         close("a")
-        quant(T.xq[:], T.xsc[:], x[:], [key] + rd, ["xq"])
+        copy(T.gb[:, 0:128], T.gm[:].indirect(T.l0[:, 0:8]), GM, ["gb0"])
+        close("v")
+
+    def align(k7, n7, slot, aside):
+        op("v", lambda: V.transpose(T.tb[:], T.gb[:]), r=["gb0", "gb1"], w=["tb"])
+        step(ORDER[0], k7, n7)
+        aside()
+        for name in ORDER[1:]:
+            step(name, k7, n7)
+        act(T.pc[:, slot:slot + 1], T.xa[:, 31:32], ["h7"], ["pc%d" % slot], scale=1.0 / UNIT)
+        close("a")
+        quant(T.xq[:], T.xsc[:], T.xa[:], ["h7"], ["xq"])
         mm(5, 128, T.stq[:], T.sts[:], T.xq[:], T.xsc[:], ["stq", "xq"])
 
     def offsets(out, n, okey):
-        ts(out[:], bank[5][:, 0:n], col(0), None, A.add, None, ["b5", "ff"], [okey])
+        ts(out[:], bank[5][:, 8:8 + n], col(0), None, A.add, None, ["b5", "ff"], [okey])
         close("v")
 
     def masked(k, a, n, at):
@@ -380,16 +385,21 @@ def rank_program(g, core, T, topo):
     mm(4, 128, *win(u0), *win(a0), L)
     decode(256, T.lq[:, 0:256], T.ls[:, 0:256], L)
     masked(4, 0, 128, 0)
+    quant(T.stq[:], T.sts[:], T.st[:], ["st0", "st1", "st2", "st3"], ["stq"])
+    gather()
     op("s", lambda: g.sync.dma_start(T.wt[:], T.w[:]), r=["lin", "yin"], w=["wt"], dma=True)
     close("s")
-    for b in range(4):
-        act(T.d0[:, b:1024:4], bank[b][:, 0:256], ["b%d" % b], ["d0%d" % b], scale=0.5)
-    close("a")
-    D0 = ["d0%d" % b for b in range(4)]
     ay, uy = 256 + 64 * b0, 320 - 64 * b0
     Y = ["lin", "lown", "yin"] + (["lpad"] if not b0 and b1 else [])
     mm(6, 128, *win(uy - 64 * ha1), *win(256), Y)
-    align(T.xa, 32, T.ma[:], ["ma", "xaz", "xa1"], "xa0", 0)
+
+    def aside0():
+        for b in range(4):
+            act(T.d0[:, b:1024:4], bank[b][:, 0:256], ["b%d" % b], ["d0%d" % b], scale=0.5)
+        close("a")
+
+    D0 = ["d0%d" % b for b in range(4)]
+    align(0, 160, 0, aside0)
     masked(6, ay - 256, 64, 64 * ha1)
     offsets(T.o0, 32, "o0")
     blend(T.mt, 0, 512, T.d0[:, 4 * u0:4 * u0 + 512], T.o0[:], T.d0[:, 4 * a0:4 * a0 + 512], D0 + ["o0"], ["mt0"])
@@ -400,22 +410,28 @@ def rank_program(g, core, T, topo):
     mm(4, 128, T.m0q[:], T.m0s[:], T.m0q[:], T.m0s[:], ["m0"])
     decode(128, T.m0q[:], T.m0s[:], ["m0"])
     masked(4, 64 * ha1, 64, 64 * hb1)
-    for b in range(4):
-        act(T.d1a[:, :, :, b:32:4], bank[b][:, 64 * ha1:64 * ha1 + 64], ["b%d" % b], ["d1a%d" % b], scale=0.5)
-        act(T.d1b[:, b:256:4], bank[b][:, 64 * hb1:64 * hb1 + 64], ["b%d" % b], ["d1b%d" % b], scale=0.5)
+    gather()
+
+    def aside1():
+        for b in range(4):
+            act(T.d1a[:, :, :, b:32:4], bank[b][:, 64 * ha1:64 * ha1 + 64], ["b%d" % b], ["d1a%d" % b], scale=0.5)
+            act(T.d1f[:, b:512:4], bank[b][:, 0:128], ["b%d" % b], ["d1f%d" % b], scale=0.5)
+            close("a")
+        decode(128, *win(256), Y)
+        for h, par in enumerate((1 - b2, b2)):
+            act(T.d1s[:, 128 * h:128 * h + 128], T.d1a[:, :, par, :], ["d1a%d" % b for b in range(4)], ["d1s%d" % h])
         close("a")
-    decode(128, *win(256), Y)
-    for h, par in enumerate((1 - b2, b2)):
-        act(T.d1s[:, 128 * h:128 * h + 128], T.d1a[:, :, par, :], ["d1a%d" % b for b in range(4)], ["d1s%d" % h])
-    close("a")
-    for b in range(4):
-        act(T.dy[:, b:512:4], bank[b][:, 0:128], ["b%d" % b], ["dy%d" % b], scale=0.5)
-    close("a")
-    D1 = ["d1b%d" % b for b in range(4)] + ["d1s0", "d1s1"]
-    DY = ["dy%d" % b for b in range(4)]
-    align(T.xb, 32, T.mb[:], ["mb0", "mb1", "mb2", "xbz", "xb1", "xb2"], "xb0", 4)
+        for b in range(4):
+            for h in range(ha1 + 1):
+                act(run(T.dy, 256 * h + b, 64, 4), bank[b][:, uy - 256:uy - 192], ["b%d" % b], ["dy%d%d" % (h, b)], scale=0.5)
+            act(T.dz[:, b:256:4], bank[b][:, ay - 256:ay - 192], ["b%d" % b], ["dz%d" % b], scale=0.5)
+        close("a")
+
+    D1 = ["d1f%d" % b for b in range(4)] + ["d1s0", "d1s1"]
+    DY = ["dy%d%d" % (h, b) for b in range(4) for h in range(ha1 + 1)] + ["dz%d" % b for b in range(4)]
+    align(160, 160, 4, aside1)
     offsets(T.o1, 32, "o1")
-    blend(T.mt, 0, 128, T.d1b[:], T.o1[:, 0:8], T.d1s[:, 0:128], D1 + ["o1"], ["mt0"])
+    blend(T.mt, 0, 128, T.d1f[:], T.o1[:, 0:8], T.d1s[:, 0:128], D1 + ["o1"], ["mt0"])
     quant(T.m1q[:], T.m1s[:], T.mt[:], ["mt0"], ["m1"])
     need("g", ["m1"])
     e8 = topo.engines(core, c4)
@@ -425,9 +441,8 @@ def rank_program(g, core, T, topo):
     sent += 2 * len(e8)
     landed("hin", "arr2", 2 * len(e8))
 
-    blend(T.mu, 384, 128, T.d1b[:], T.o1[:, 8:16], T.d1s[:, 128:256], D1 + ["o1"], ["mu0"])
-    blend(T.mu, 128, 256, T.dy[:, 4 * (uy - 256):4 * (uy - 256) + 256], T.o1[:, 16:32],
-          T.dy[:, 4 * (ay - 256):4 * (ay - 256) + 256], DY + ["o1"], ["mu1"])
+    blend(T.mu, 384, 128, T.d1f[:], T.o1[:, 8:16], T.d1s[:, 128:256], D1 + ["o1"], ["mu0"])
+    blend(T.mu, 128, 256, T.dy[:, 0:256 * ha1 + 256], T.o1[:, 16:32], T.dz[:], DY + ["o1"], ["mu1"])
     quant(T.wq[:], T.ws[:], T.wt[:], ["wt"], ["wq"])
     quant(T.hq[:, 0:128], T.hs[:, 0:128], T.mu[:], ["mu0", "mu1", "muz"], ["hown"])
 
@@ -437,42 +452,46 @@ def rank_program(g, core, T, topo):
 
     prod(0, T.m0q[:], T.m0s[:], ["m0"])
     prod(2, T.m1q[:], T.m1s[:], ["m1"])
-    prod(6, T.hq[:, 0:128], T.hs[:, 0:128], ["hown"])
     for o in range(2):
         act(T.ya[:, 12 * o:12 * o + 8, b1, :], bank[o][:, 64:128], ["b%d" % o], ["ya0%d" % o])
         act(T.ya[:, 12 * o + 8:12 * o + 12, 1 - b2, :], bank[2 + o][:, 0:32], ["b%d" % (2 + o)], ["ya1%d" % o])
         close("a")
-    for o in range(2):
-        act(T.ya[:, 12 * o:12 * o + 8, 1 - b1, :], bank[6 + o][:, 32:96], ["b%d" % (6 + o)], ["ya2%d" % o])
-        act(T.ya[:, 12 * o + 8:12 * o + 12, b2, :], bank[6 + o][:, 96:128], ["b%d" % (6 + o)], ["ya3%d" % o])
-        close("a")
 
     H = ["hin", "hown"]
     mm(4, 128, T.hq[:, 32:160], T.hs[:, 32:160], T.hq[:, 32:160], T.hs[:, 32:160], H)
+    prod(6, T.hq[:, 0:128], T.hs[:, 0:128], ["hown"])
     decode(128, T.hq[:, 32:160], T.hs[:, 32:160], H)
     masked(4, 32 * qa2, 32, 32 * qb2)
-    for b in range(4):
-        act(T.d2[:, b:256:4], bank[b][:, 64:128], ["b%d" % b], ["d2%d" % b], scale=0.5)
-    close("a")
+    gather()
     store("s", T.pf[0:1, 64:128], T.pc[64 * ha1:64 * ha1 + 64, 4:5], ["pc4", "hin"], ["pfu"])
     close("s")
     store("s", T.pt[0:1, 128:192], T.pc[64 * hb1:64 * hb1 + 64, 4:5], ["pc4"])
-    for o in range(2):
-        store("sa"[o], T.y[:, 224 * o:224 * o + 192], T.ya[:, 12 * o:12 * o + 12, :, :], ["ya%d%d" % (u, o) for u in range(4)])
     close("s")
-    close("a")
-    act(T.p0[0:1, :, b1, :], T.pf[0:1, 0:64], ["pfk"], ["p0k"])
-    act(T.p0[0:1, :, 1 - b1, :], T.pf[0:1, 64:128], ["pfu"], ["p0u"])
-    close("a")
-    store("s", T.pt[0:1, 0:128], T.p0[0:1, :, :, :], ["p0k", "p0u"])
-    close("s")
-    align(T.xa, 8, T.ma[:, 2 * qb2:2 * qb2 + 2, :, :], ["ma", "xaz", "xa1"], "xa0", 8)
+
+    def aside2():
+        for o in range(2):
+            act(T.ya[:, 12 * o:12 * o + 8, 1 - b1, :], bank[6 + o][:, 32:96], ["b%d" % (6 + o)], ["ya2%d" % o])
+            act(T.ya[:, 12 * o + 8:12 * o + 12, b2, :], bank[6 + o][:, 96:128], ["b%d" % (6 + o)], ["ya3%d" % o])
+            close("a")
+        for b in range(4):
+            act(T.d2[:, b:512:4], bank[b][:, 0:128], ["b%d" % b], ["d2%d" % b], scale=0.5)
+            act(T.d2a[:, b:128:4], bank[b][:, 32 * qa2:32 * qa2 + 32], ["b%d" % b], ["d2a%d" % b], scale=0.5)
+        close("a")
+        for o in range(2):
+            store("s", T.y[:, 224 * o:224 * o + 192], T.ya[:, 12 * o:12 * o + 12, :, :], ["ya%d%d" % (u, o) for u in range(4)])
+        close("s")
+        act(T.p0[0:1, :, b1, :], T.pf[0:1, 0:64], ["pfk"], ["p0k"])
+        act(T.p0[0:1, :, 1 - b1, :], T.pf[0:1, 64:128], ["pfu"], ["p0u"])
+        close("a")
+        store("s", T.pt[0:1, 0:128], T.p0[0:1, :, :, :], ["p0k", "p0u"])
+        close("s")
+
+    align(320, 64, 8, aside2)
     store("a", T.pt[0:1, 192:224], T.pc[32 * qb2:32 * qb2 + 32, 8:9], ["pc8"])
     close("a")
-    D2 = ["d2%d" % b for b in range(4)]
+    D2 = ["d2%s%d" % (u, b) for b in range(4) for u in ("", "a")]
     offsets(T.o2, 8, "o2")
-    ha2, hb2 = qa2 - 2, qb2 - 2
-    blend(T.mt, 0, 128, T.d2[:, 128 * hb2:128 * hb2 + 128], T.o2[:], T.d2[:, 128 * ha2:128 * ha2 + 128], D2 + ["o2"], ["mt0"])
+    blend(T.mt, 0, 128, T.d2[:], T.o2[:], T.d2a[:], D2 + ["o2"], ["mt0"])
     quant(T.m2q[:], T.m2s[:], T.mt[:], ["mt0"], ["m2"])
     prod(6, T.m2q[:], T.m2s[:], ["m2"])
     store("s", T.oc[:, 0:128], T.m2q[:, 0:32].bitcast(dt.uint8), ["m2"])

@@ -4,7 +4,7 @@ from concourse.mybir import dt, AluOpType, ActivationFunctionType
 F32, BF, I32, U16, X4, U8 = "float32", "bfloat16", "int32", "uint16", "float8_e4m3fn_x4", "uint8"
 LOW = -1.0e29
 UNIT = 0.125
-ORDER = ("b0 p0 q0 b1 a0 a1 p1 q1 d1 p2 q2 l1 d2 p3 q3 h1 g1 l2 d3 p4 q4 l3 h2 g2 d4 p5 q5 l4 h3 g3 d5 p6 q6 l5 h4 g4 d6 "
+ORDER = ("p0 q0 t1 p1 q1 d1 p2 q2 l1 t2 d2 p3 q3 h1 g1 l2 d3 p4 q4 l3 h2 g2 d4 p5 q5 l4 h3 g3 d5 p6 q6 l5 h4 g4 d6 "
          "p7 l6 h5 g5 d7 l7 h6 g6 h7").split()
 
 
@@ -13,27 +13,31 @@ def _sb(shape, d):
 
 
 SCRATCH = {
-    "xs": _sb([8, 4, 32], BF), "xt": _sb([1024], BF), "wt": _sb([1024], BF),
-    "sq": _sb([128], X4), "ss": _sb([128], U8), "lq": _sb([512], X4), "ls": _sb([512], U8),
-    "wq": _sb([256], X4), "ws": _sb([256], U8),
+    "xs": _sb([1024], BF), "wt": _sb([1024], BF), "rq": _sb([256], X4), "rs": _sb([256], U8),
+    "lq": _sb([768], X4), "ls": _sb([768], U8), "wq": _sb([256], X4), "ws": _sb([256], U8),
     "et": _sb([520], BF), "eq": _sb([512], X4), "es": _sb([512], U8),
-    "st": _sb([512], BF), "stq": _sb([128], X4), "sts": _sb([128], U8),
-    "pi": _sb([2], I32), "fi": _sb([8], I32), "ff": _sb([12], F32),
-    "uu": _sb([128], F32), "vv": _sb([128], BF), "tt": _sb([128], BF), "zz": _sb([420], BF),
-    "mk": _sb([128], F32), "cl": _sb([16], F32), "l0": _sb([16], U16), "lg": _sb([4], U16),
-    "kj": _sb([32], F32), "ke": _sb([8], F32), "ma": _sb([8, 2, 2], F32),
-    "gm": _sb([128], F32), "gb": _sb([256], F32), "tb": _sb([256], F32), "g3": _sb([96], F32), "g4": _sb([128], F32),
-    "q0": _sb([32], F32), "pr": _sb([840], F32), "p7": _sb([24], F32),
-    "km": _sb([280], F32), "k7": _sb([384], F32), "hz": _sb([32], F32), "hr": _sb([1728], F32),
+    "st": _sb([512], BF), "stq": _sb([256], X4), "sts": _sb([256], U8),
+    "pi": _sb([2], I32), "fi": _sb([24], I32), "ff": _sb([24], F32),
+    "uu": _sb([256], BF), "vv": _sb([128], BF), "zz": _sb([320], BF),
+    "ip": _sb([16], F32), "i0": _sb([16], F32), "i1": _sb([16], F32), "ib": _sb([4], F32), "iy": _sb([8], F32),
+    "id": _sb([8], F32), "kj": _sb([32], F32), "ke": _sb([8], F32), "cx": _sb([2], F32),
+    "mka": _sb([128], F32), "mkb": _sb([64], F32),
+    "lp": _sb([16], U16), "lg0": _sb([16], U16), "lg1": _sb([16], U16), "lg2": _sb([16], U16), "lb": _sb([4], U16),
+    "ly": _sb([12], U16), "ld": _sb([8], U16),
+    "gm0": _sb([128], F32), "gm1": _sb([128], F32), "gm2": _sb([40], F32), "gb": _sb([256], F32),
+    "g8": _sb([568], F32), "g3": _sb([128], F32), "ic": _sb([4], F32), "ie": _sb([4], I32), "ig": _sb([4], F32),
+    "q0": _sb([32], F32), "pr0": _sb([108], F32), "pr3": _sb([648], F32), "pr8": _sb([648], F32), "p7": _sb([24], F32),
+    "km": _sb([280], F32), "k7": _sb([144], F32), "hz": _sb([32], F32), "hr4": _sb([540], F32), "hr5": _sb([840], F32),
     "xa": _sb([512], BF), "xq": _sb([128], X4), "xsc": _sb([128], U8),
-    "o0": _sb([32], U16), "o1": _sb([32], U16), "o2": _sb([8], U16),
-    "d0": _sb([1024], F32), "dy": _sb([512], F32), "dz": _sb([256], F32), "d2": _sb([512], F32), "d2a": _sb([128], F32),
-    "d1a": _sb([4, 2, 32], F32), "d1f": _sb([512], F32), "d1s": _sb([256], F32),
-    "mt": _sb([512], BF), "mu": _sb([512], BF),
-    "m0q": _sb([128], X4), "m0s": _sb([128], U8), "m1q": _sb([128], X4), "m1s": _sb([128], U8),
-    "hq": _sb([160], X4), "hs": _sb([160], U8), "m2q": _sb([128], X4), "m2s": _sb([128], U8),
-    "ya": _sb([24, 2, 8], F32), "y2": _sb([64], F32),
-    "pc": _sb([12], F32), "pf": _sb([128], F32), "p0": _sb([8, 2, 8], F32),
+    "o0": _sb([32], U16), "o1": _sb([16], U16), "oy": _sb([16], U16), "o2": _sb([8], U16),
+    "da0": _sb([512], F32), "db0": _sb([512], F32), "dt0": _sb([8, 2, 16], F32), "dty": _sb([8, 2, 16], F32),
+    "day": _sb([256], F32), "dby": _sb([256], F32), "da1": _sb([256], F32), "db1": _sb([256], F32),
+    "da2": _sb([128], F32), "db2": _sb([128], F32), "dc2": _sb([128], F32),
+    "mt": _sb([1024], BF), "mu": _sb([512], BF),
+    "m1q": _sb([128], X4), "m1s": _sb([128], U8), "hq": _sb([160], X4), "hs": _sb([160], U8),
+    "m2q": _sb([128], X4), "m2s": _sb([128], U8),
+    "ys": _sb([384], F32), "ya": _sb([384], F32), "y2": _sb([64], F32),
+    "pc": _sb([12], F32), "pf": _sb([192], F32), "pa": _sb([4, 2, 2, 8], F32), "pb": _sb([4, 2, 8], F32),
 }
 for _k in range(8):
     SCRATCH["b%d" % _k] = ("psum", [128, 512], F32)
@@ -142,6 +146,7 @@ def rank_program(g, core, T, topo):
             op("g", lambda: g.iota(out, pat, base, cm, allow_small_or_imprecise_dtypes=True), w=[key])
         else:
             op("g", lambda: g.iota(out, pat, base, cm), w=[key])
+        close("g")
 
     def fill(out, val, key, rd=()):
         op("v", lambda: V.memset(out, val), r=rd, w=[key])
@@ -161,17 +166,19 @@ def rank_program(g, core, T, topo):
     def copy(out, in_, rd, wr, cut=False):
         op("v", lambda: V.tensor_copy(out, in_), r=rd, w=wr, cut=cut)
 
-    def act(out, in_, rd, wr, scale=1.0, bias=None):
-        if bias is None:
-            op("a", lambda: S.activation(out, in_, ACT.Copy, scale=scale), r=rd, w=wr)
+    def act(out, in_, rd, wr, scale=None, bias=None, cut=False):
+        if scale is None:
+            op("a", lambda: S.activation(out, in_, ACT.Copy), r=rd, w=wr, cut=cut)
+        elif bias is None:
+            op("a", lambda: S.activation(out, in_, ACT.Copy, scale=scale), r=rd, w=wr, cut=cut)
         else:
-            op("a", lambda: S.activation(out, in_, ACT.Identity, bias=bias, scale=scale), r=rd, w=wr)
+            op("a", lambda: S.activation(out, in_, ACT.Identity, bias=bias, scale=scale), r=rd, w=wr, cut=cut)
 
-    def afill(out, n, val, key):
-        act(out, T.zz[:, 0:n], ["zz"], [key], scale=0.0, bias=val)
+    def afill(out, n, val, key, rd=(), rows=128):
+        act(out, T.zz[0:rows, 0:n], ["zz"] + list(rd), [key], scale=0.0, bias=val)
 
     def quant(q, s, tile, rd, wr):
-        op("v", lambda: V.quantize_mx(q, s, tile), r=rd, w=wr)
+        op("v", lambda: V.quantize_mx(q, s, tile), r=rd, w=wr, cut=True)
         close("v")
 
     def mm(k, n, lq, ls, rq, rs, rd):
@@ -184,60 +191,85 @@ def rank_program(g, core, T, topo):
     def run(t, a, n, s):
         return t[:, a:a + s * (n - 1) + 1:s]
 
+    def win(a, n=128):
+        return T.lq[:, a:a + n], T.ls[:, a:a + n]
+
     op("s", lambda: g.sync.dma_start(T.xs[:], T.x[:]), w=["xs"], dma=True)
     close("s")
 
-    ha1, hb1 = 1 - b1, b1
-    qa2, qb2 = 2 + b2, 3 - b2
-    iota(T.pi[:, 0:1], [[0, 1]], 0, 1, "pi", small=False)
-    close("g")
+    FIELDS = {"pk0": (3, 64) if b0 else (0, 192), "pk1": (6, 7) if b0 else (8, 3),
+              "e": (6, 3), "c": (6, 7), "s": (6, 15), "m": (9, 3), "a8": (8, 8), "a": (11, 1), "c2": (5, 14),
+              "g0": (6, 104), "g1": (9, 5), "m32": (3, 96), "h4": (8, 4), "q": (8, 31),
+              "s4": (4, 60), "i16": (4, 48), "y0": (3, 120) if b1 else (3, 64), "y1": (4, 28)}
+    place = {n: k for k, n in enumerate(FIELDS)}
+    col = lambda n: T.ff[:, place[n]:place[n] + 1]
+
+    def fields(names):
+        for n in names:
+            ts(T.fi[:, place[n]:place[n] + 1], T.pi[:, 0:1], FIELDS[n][0], FIELDS[n][1], A.logical_shift_right, A.bitwise_and,
+               ["pi"], ["fi" + n])
+        close("v")
+
+    def floats(names):
+        a, b = place[names[0]], place[names[-1]] + 1
+        copy(T.ff[:, a:b], T.fi[:, a:b], ["fi" + n for n in names], ["f" + n for n in names], True)
+        close("v")
+
+    names = list(FIELDS)
+    c = r % 4
+    iota(T.pi[:, 0:1], [[0, 1]], 0, 64, "pi", small=False)
+    for k, (u, v) in enumerate(((c, c ^ 1), (c ^ 3, c ^ 2))):
+        iota(T.ip[:, 8 * k:8 * k + 8], [[8 * (v - u), 2], [32, 2], [128 if b0 else 4, 2]], 8 * u, 0, "ip%d" % k)
     iota(T.kj[:], [[1, 32]], 0, 0, "kj")
-    iota(T.cl[:], [[1, 8], [16, 2]], 0, 0, "cl")
-    close("g")
-    iota(T.uu[:], [[1, 16], [0, 8]], 0, 0, "uu")
-    close("g")
     iota(T.vv[:], [[1, 128]], 0, -1, "vv")
-    close("g")
-    iota(T.tt[:], [[0, 8], [1, 4], [0, 4]], 0, 0, "tt")
-    close("g")
+    iota(T.uu[:], [[0, 8], [1, 4], [0, 8]], 0, 0, "uu")
+    iota(T.i0[:], [[1, 8], [16, 2]], 0, 0, "i0")
+    iota(T.ib[:], [[48, 2], [16, 2]], 0, 0, "ib")
     fill(T.zz[:], 0.0, "zz")
     close("v")
+    fields(names[:2])
     fill(T.et[:], 0.0, "etz")
     close("v")
-    for k, (sh, m) in enumerate([(0, 3), (0, 7), (3, 15), (2, 31), (0, 104), (0, 16), (3, 1)]):
-        ts(T.fi[:, k:k + 1], T.pi[:, 0:1], sh, m, A.logical_shift_right, A.bitwise_and, ["pi"], ["fi%d" % k])
+    floats(names[:2])
+    fields(names[2:13])
+    ts(T.lp[:], T.ip[:], col("pk0"), col("pk1"), A.add, A.add, ["ip0", "ip1", "fpk0", "fpk1"], ["lp"])
     close("v")
-    afill(T.pr[:, 0:420], 420, LOW, "prz0")
-    afill(T.pr[:, 420:840], 420, LOW, "prz1")
-    afill(T.q0[:], 32, LOW, "top")
-    close("a")
-    afill(T.km[:], 280, 0.0, "kmz")
-    close("a")
-    col = lambda k: T.ff[:, k:k + 1]
-    fill(T.xa[:, 64:512], 0.0, "h7")
-    close("v")
-    copy(T.ff[:, 0:7], T.fi[:, 0:7], ["fi%d" % k for k in range(7)], ["ff"])
-    close("v")
-    fill(T.st[:, 3:512:4], 0.0, "st3")
-    close("v")
-    ts(T.ke[:], T.kj[:, 0:8], col(1), None, A.is_equal, None, ["kj", "ff"], ["ke"])
-    ts(T.ma[:], T.kj[:], col(3), None, A.is_equal, None, ["kj", "ff"], ["ma"])
-    ts(col(8), col(1), 32.0, col(5), A.mult, A.add, ["ff"], ["f8"])
+    floats(names[2:13])
+    fill(T.xa[:], 0.0, "xaz")
     close("v")
 
-    order = [(r ^ k) % 4 for k in (1, 3, 0, 2)]
-    act(T.xt[:, 512:768], T.xs[:, :, order[2], :], ["xs"], ["xt2"])
+    kp = lambda j: 4 if j == 0 else 3 if j % 2 else 8
+    kh = lambda j: 5 - j % 2
+    sums_at = lambda j: (T.pr0, 8) if j == 0 else (T.pr3, 216 * (j // 2) + 21) if j % 2 else (T.pr8, 216 * (j // 2 - 1) + 16)
+    nums_at = lambda j: (T.hr4, 180 * (j // 2) + 4) if j % 2 else (T.hr5, 180 * (j // 2 - 1))
+    g8_at = lambda j: 64 * j + (24 if j > 1 else 0)
+    G8Z = ["g8z0", "g8z1", "g8z2"]
+    afill(T.g8[:, 1:568:2], 284, 0.0, "g8z0")
+    afill(T.g8[:, 130:154:2], 12, 0.0, "g8z1")
+    afill(T.g8[:, 538:568:2], 15, 0.0, "g8z2")
+    afill(T.q0[:], 32, LOW, "top0")
+    afill(T.pr0[:, 0:108:4], 27, LOW, "prz0")
+    afill(T.pr3[:, 0:648:3], 216, LOW, "prz1")
+    afill(T.pr8[:, 0:648:8], 81, LOW, "prz2")
+    afill(T.st[:, 1:512:2], 256, 0.0, "stz")
     close("a")
-    for k in (0, 1):
-        copy(T.xt[:, 256 * k:256 * k + 256], T.xs[:, :, order[k], :], ["xs"], ["xt%d" % k])
-    close("v")
-    copy(T.xt[:, 768:1024], T.xs[:, :, order[3], :], ["xs"], ["xt3"])
-    close("v")
-    ts(T.l0[:], T.cl[:], col(4), None, A.add, None, ["cl", "ff"], ["l0"])
-    close("v")
-    quant(T.sq[:], T.ss[:], T.xt[:, 0:512], ["xt0", "xt1"], ["sq"])
-    quant(T.lq[:, 192:320], T.ls[:, 192:320], T.xt[:, 512:1024], ["xt2", "xt3"], ["lown"])
-    need("g", ["lown", "sq"])
+    afill(T.q0[:, 0:1], 1, 0.0, "top", ["top0"])
+    afill(T.st[0:1, 1:512:4], 128, 2.0, "st1", ["stz"], 1)
+    afill(T.st[0:1, 3:512:4], 128, 32.0, "st3", ["stz"], 1)
+    close("a")
+
+    quant(T.rq[:], T.rs[:], T.xs[:], ["xs"], ["rq"])
+    slot = lambda s: 256 + 128 * (s & 1) + 64 * (1 - (s >> 1 & 1))
+
+    def pick(at, a, n, key):
+        copy(T.lq[:, at:at + 16 * n].bitcast(dt.uint32), T.rq[:].bitcast(dt.uint32).indirect(T.lp[:, a:a + n]),
+             ["rq", "lp"], ["q" + key], True)
+        close("v")
+        act(T.ls[:, at:at + 16 * n], T.rs[:].indirect(T.lp[:, a:a + n]), ["rq", "lp"], ["s" + key], cut=True)
+        close("a")
+
+    pick(0, 4, 12, "out")
+    pick(slot(r), 0, 4, "own")
     c1, c2, c3, c4 = (T.cores[r ^ k] for k in (1, 2, 3, 4))
     e = topo.engines(core, c1)
     n4 = len(e) // 4
@@ -247,92 +279,131 @@ def rank_program(g, core, T, topo):
         return t[:, a:a + 64].bitcast(dt.uint8) if codes else t[:, a:a + 64]
 
     for codes in (True, False):
-        src, mine = (T.sq, T.lq) if codes else (T.ss, T.ls)
+        t = T.lq if codes else T.ls
+        need("g", ["qout" if codes else "sout"])
         es = (e0, e1, e2 + e3) if codes else (e2, e3, e0 + e1)
-        pieces = [(src, 0, c1, 64), (src, 64, c3, 0), (mine, 256, c2, 128)]
-        g.remote_dma_fused([RemoteDMATransfer(dst_ids=[dst_id(c)], dma_engine_mask=mask_of(es[k]), remote_sem=T.sem.arr0,
-                                              src=view(t, a, codes), dst=view(mine, at, codes))
-                            for k, (t, a, c, at) in enumerate(pieces)], local_sem=T.sem.sent)
+        g.remote_dma_fused([RemoteDMATransfer(dst_ids=[dst_id(cc)], dma_engine_mask=mask_of(es[k]), remote_sem=T.sem.arr0,
+                                              src=view(t, 64 * k, codes), dst=view(t, slot(r), codes))
+                            for k, cc in enumerate((c1, c3, c2))], local_sem=T.sem.sent)
     rid, pid = int(topo.addr(c1)[0]), int(topo.addr(c1)[1])
-    g.remote_dma(view(T.lq, 320, True), view(T.sq, 64, True), T.sem.arry, T.sem.sent, pid, rid, mask_of(e))
-    g.remote_dma(view(T.ls, 320, False), view(T.ss, 64, False), T.sem.arry, T.sem.sent, pid, rid, mask_of(e))
+    g.remote_dma(view(T.lq, 192, True), view(T.lq, 64, True), T.sem.arry, T.sem.sent, pid, rid, mask_of(e))
+    g.remote_dma(view(T.ls, 192, False), view(T.ls, 64, False), T.sem.arry, T.sem.sent, pid, rid, mask_of(e))
     sent = 4 * len(e)
     landed("lin", "arr0", 2 * len(e))
     landed("yin", "arry", 2 * len(e))
 
-    kp = lambda j: 4 - j % 2
-    kh = lambda j: 5 - j % 2
-    afill(T.q0[:, 0:1], 1, 0.0, "top")
-    afill(T.g3[:, 0:96:3], 32, 0.0, "g3z")
-    afill(T.g4[:], 128, 0.0, "g4z")
+    at2, bt2 = 2 + b2, 3 - b2
+    iota(T.i1[:], [[8, 8], [2, 2]], 0, 0, "i1")
+    iota(T.iy[:], [[1, 4], [4 if b1 else 32, 2]], 0, 0, "iy")
+    iota(T.id[:], [[4, 4], [64, 2]], 0, 0, "id")
+    afill(T.km[:], 280, 0.0, "kmz")
     afill(T.hz[:], 32, 0.0, "hzz")
-    for k in range(3):
-        afill(T.hr[:, 368 * k:368 * k + 368], 368, 0.0, "hrz%d" % k)
-    afill(run(T.hr, 1108, 124, 5), 124, 0.0, "hrz3")
+    afill(T.hr4[:, 0:540:4], 135, 0.0, "hrz0")
+    afill(T.hr5[:, 0:840:5], 168, 0.0, "hrz1")
+    afill(T.k7[:], 144, 0.0, "k7z")
     close("a")
-    afill(T.k7[:], 384, 0.0, "k7z")
-    close("a")
-    HRZ = ["hrz0", "hrz1", "hrz2", "hrz3"]
-    act(T.hz[:, 2:32:4], T.ke[:], ["ke", "hzz"], ["hc1"], scale=UNIT)
-    for j in range(1, 7):
-        act(run(T.hr, 184 * (j - 1) + 8 + 2 * kh(j), 8, 20), T.ke[:], ["ke"] + HRZ, ["hc%d" % (j + 1)], scale=(j + 1) * UNIT)
-    act(run(T.k7, 33, 32, 4), T.ma[:], ["ma", "k7z"], ["k70"])
-    act(run(T.k7, 193, 8, 4), T.ma[:, 4 * hb1:4 * hb1 + 4, 1 - b2, :], ["ma", "k7z"], ["k71"])
-    act(run(T.k7, 225, 8, 4), T.ma[:, 4 * hb1:4 * hb1 + 4, b2, :], ["ma", "k7z"], ["k72"])
-    act(run(T.k7, 257, 16, 4), T.ma[:, 4 * ha1:4 * ha1 + 4, :, :], ["ma", "k7z"], ["k73"])
-    act(run(T.k7, 353, 8, 4), T.ma[:, 2 * qb2:2 * qb2 + 2, :, :], ["ma", "k7z"], ["k74"])
-    afill(T.mu[:, 0:128], 128, 0.0, "muz")
-    close("a")
-    K7 = ["k7%d" % k for k in range(5)]
+    HRZ = ["hrz0", "hrz1"]
     ts(T.et[:, 4:516:4], T.vv[:], 0.0, None, A.is_equal, None, ["vv", "etz"], ["et"])
+    ts(T.ic[:], T.ib[:], col("s"), None, A.add, None, ["ib", "fs"], ["ic"])
     close("v")
-    ts(T.mk[:], T.uu[:], col(2), None, A.is_equal, None, ["uu", "ff"], ["mk"])
-    ts(col(9), col(6), 2.0, col(8), A.mult, A.add, ["ff", "f8"], ["f9"])
-    ts(col(10), col(2), 1.0, 32.0, A.add, A.mult, ["ff"], ["f10"])
-    ts(col(11), col(2), -32.0, None, A.mult, None, ["ff"], ["f11"])
+    ts(T.mka[:], T.uu[:, 0:128], col("e"), None, A.is_equal, None, ["uu", "fe"], ["mka"])
+    ts(T.lg0[:], T.i0[:], col("g0"), None, A.add, None, ["i0", "fg0"], ["lg0"])
+    ts(T.ke[:], T.kj[:, 0:8], col("c"), None, A.is_equal, None, ["kj", "fc"], ["ke"])
+    close("v")
+    ts(T.ie[:], T.ic[:], -1.0, 1.0 / 3, A.add, A.mult, ["ic"], ["ie"])
     close("v")
     for b in range(4):
         op("v", lambda: V.quantize_mx(T.eq[:, 128 * b:128 * b + 128], T.es[:, 128 * b:128 * b + 128], T.et[:, 4 - b:516 - b]),
            r=["et"], w=["eq%d" % b])
+        if b == 1:
+            close("v")
+            tt(T.ig[:], T.ic[:], T.ie[:], A.add, ["ic", "ie"], ["ig"])
+            close("v")
     close("v")
-    for u in range(2):
-        ts(T.lg[:, 2 * u:2 * u + 2], T.kj[:, u:8:4], col(9), None, A.add, None, ["kj", "f9"], ["lg%d" % u])
+    ts(T.lb[:], T.ig[:], 2.0, col("h4"), A.mult, A.add, ["ig", "fh4"], ["lb"])
     close("v")
-    for t, s in enumerate((col(10), col(11), -32.0)):
-        ts(T.st[:, t:512:4], T.tt[:], col(0), s, A.is_equal, A.mult, ["tt", "ff", "f10", "f11"], ["st%d" % t])
+
+    def spreader(name, at):
+        for t, s in ((0, 32.0), (2, -32.0)):
+            ts(T.st[:, t:512:4], T.uu[:, 0:256:2], col(name), s, A.is_equal, A.mult, ["uu", "f" + name], ["st%d" % t])
+        close("v")
+
+    def hot(lo, hi, at, n, first, s1, s2, key, rd=()):
+        ts(T.k7[lo:hi, at:at + 2 * n:2], T.kj[lo:hi, first:first + n], T.ff[lo:hi, place[s1]:place[s1] + 1],
+           T.ff[lo:hi, place[s2]:place[s2] + 1], A.subtract, A.is_equal, ["kj", "k7z", "f" + s1, "f" + s2] + list(rd), [key])
+
+    spreader("m", 0)
+    hot(64, 128, 32, 16, 0, "a8", "c", "k7a")
+    hot(0, 64, 64, 16, 0, "a", "c2", "k7b")
     close("v")
-    if not b0 and b1:
-        quant(T.lq[:, 384:512], T.ls[:, 384:512], T.xt[:, 0:512], ["xt0", "xt1"], ["lpad"])
+    act(T.hz[:, 2:32:4], T.ke[:], ["ke", "hzz"], ["hc1"], scale=UNIT)
+    for j in range(1, 7):
+        t, at = nums_at(j)
+        act(run(t, at + 2 * kh(j), 8, 20), T.ke[:], ["ke"] + HRZ, ["hc%d" % (j + 1)], scale=(j + 1) * UNIT)
+    close("a")
+    beta = lambda a, n, s=1: run(T.xa, 65 + 4 * a, n, 4 * s)
+    afill(run(T.xa, 67, 32, 4), 32, 1.0, "xa3", ["xaz"])
+    afill(beta(0, 8), 8, 128.0, "xb0", ["xaz"])
+    afill(beta(8, 8), 8, 192.0, "xb1", ["xaz"])
+    afill(beta(17, 8, 2), 8, 64.0, "xb2", ["xaz"])
+    afill(T.mt[:, 0:192], 192, 0.0, "mtz0")
+    afill(T.mt[:, 704:1024], 320, 0.0, "mtz1")
+    afill(T.mu[:, 0:128], 128, 0.0, "muz")
+    close("a")
+    XB = ["xa3", "xb0", "xb1", "xb2"]
 
     def decode(n, q, s, rd):
         for b in range(4):
             mm(b, n, T.eq[:, 128 * b:128 * b + 128], T.es[:, 128 * b:128 * b + 128], q, s, ["eq%d" % b] + rd)
 
+    def halves(outs):
+        for b in range(4):
+            for name, out, a, n in outs:
+                act(out(b), bank[b][:, a:a + n], ["b%d" % b], ["%s%d" % (name, b)], scale=0.5)
+            close("a")
+        return [["%s%d" % (o[0], b) for b in range(4)] for o in outs]
+
     def sums(j, back):
-        return run(T.pr, 120 * j + 12 + kp(j) - 12 * back, 8, 12)
+        t, at = sums_at(j)
+        pitch = kp(j) * kp(j + 1)
+        return run(t, at + kp(j) - pitch * back, 8, pitch)
+
+    def turn(a, n, key):
+        op("v", lambda: V.transpose(run(T.g8, g8_at(a) + 2, 32 * n, 2), T.gb[:, 32 * a:32 * (a + n)]),
+           r=["gb%d" % j for j in range(a, a + n)] + G8Z, w=[key], cut=True)
+        close("v")
+
+    def thin(j, n, rd):
+        act(T.g3[:, 16 * j - 16:16 * j - 16 + 32 * n], T.g8[:, g8_at(j):g8_at(j) + 128 * n - 40].indirect(T.lb[:, 0:2 * n]),
+            rd + ["lb"], ["s%d" % j], cut=True)
+        close("a")
 
     def step(name, k7, n7):
         kind, j = name[0], int(name[1])
-        if kind in "ab":
-            t, k, u = (T.g4, 4, 0) if kind == "a" else (T.g3, 3, 1)
-            args = (run(t, 1 + j, 32, k), T.tb[:, 8 * j:256].indirect(T.lg[:, 2 * u:2 * u + 2]),
-                    ["tb", "g%dz" % k, "lg%d" % u], ["s" + name])
-            if name == "b0":
-                act(*args)
-                close("a")
-            else:
-                copy(*args, True)
+        if kind == "t":
+            turn(3 * j - 1, 3, name)
+            thin(1 + 2 * j, j, ["t1", name])
         elif kind in "pq":
             k, n = kp(j), kp(j + 1)
-            at = 120 * j + (12 + k if kind == "p" else 24) - n * (2 if j else 3)
-            out = T.p7[:] if j == 7 else run(T.pr, at, 8 * k, n)
+            if j < 7:
+                t, at = sums_at(j)
+                out = run(t, at + (k if kind == "p" else k * n) - n * (k - 1), 8 * k, n)
+            else:
+                out = T.p7[:]
             if j == 0:
-                return scan(out, T.q0[:], T.tb[:, 0:256:8], LOW, A.add, ["tb", "top", "prz0", "prz1"], [name])
-            t, u = (T.g3, "b") if k == 3 else (T.g4, "a")
-            scan(out, run(T.pr, 120 * (j - 1) + 12, 8 * k, n), t[:, 8 * k * (j // 2):8 * k * (j // 2 + 1)], LOW, A.add,
-                 ["s%s0" % u, "s%s1" % u, "p%d" % (j - 1), "q%d" % (j - 1)], [name])
+                return scan(out, T.q0[:], T.g8[:, 2:66:2], LOW, A.add, ["t0", "top", "prz0", "prz1", "prz2"], [name])
+            t, at = sums_at(j - 1)
+            if j % 2:
+                d1, rd = T.g3[:, 16 * j - 16:16 * j + 8], ["s%d" % min(j, 5)]
+            else:
+                d1, rd = T.g8[:, g8_at(j) + 1:g8_at(j) + 65], ["t%d" % (1 + j // 5)]
+            scan(out, run(t, at, 8 * k, kp(j - 1)), d1, LOW, A.add, rd + ["p%d" % (j - 1), "q%d" % (j - 1)], [name])
         elif kind in "dl":
-            m = T.p7[:, 0:24:3] if j == 7 else run(T.pr, 120 * j + 12 + kp(j) - 2 * kp(j + 1), 8, 12)
+            if j < 7:
+                t, at = sums_at(j)
+                m = run(t, at + kp(j) - kp(j + 1) * (kp(j) - 1), 8, kp(j) * kp(j + 1))
+            else:
+                m = T.p7[:, 0:24:3]
             at = 0 if kind == "d" else 2
             out = run(T.k7, k7 + at, 8, 4) if j == 7 else run(T.km, 40 * j + at, 8, kh(j))
             tt(out, sums(j - 1, int(kind == "d")), m, A.is_ge if kind == "d" else A.is_gt,
@@ -341,98 +412,133 @@ def rank_program(g, core, T, topo):
             k, n = kh(j), kh(j + 1)
             rd = HRZ + ["hc%d" % j, "h%d" % (j - 1), "g%d" % (j - 1), "kd%d" % j, "kl%d" % j]
             if j == 7:
-                return scan(T.xa[:, 0:n7], run(T.hr, 184 * 5 + 8, n7, n), T.k7[:, k7:k7 + n7], 0.0, A.subtract, rd + K7, [name])
-            at = 184 * (j - 1) + (8 + 3 * k if kind == "h" else 28 + k) - 3 * n
-            scan(run(T.hr, at, 8 * k, n), T.hz[:] if j == 1 else run(T.hr, 184 * (j - 2) + 8, 8 * k, n),
-                 T.km[:, 40 * j:40 * j + 8 * k], 0.0, A.subtract, rd, [name])
+                return scan(run(T.xa, 0, n7, 2), run(T.hr5, 360, n7, 5), T.k7[:, k7:k7 + n7], 0.0, A.subtract,
+                            rd + ["k7a", "k7b", "k7c", "xaz"], [name])
+            t, at = nums_at(j)
+            cells = 8 if kind == "h" else 7
+            src = T.hz[:, 0:cells * k] if j == 1 else run(nums_at(j - 1)[0], nums_at(j - 1)[1], cells * k, n)
+            scan(run(t, at + (3 * k if kind == "h" else k + 20) - 3 * n, cells * k, n), src,
+                 T.km[:, 40 * j:40 * j + cells * k], 0.0, A.subtract, rd, [name])
 
-    def gather():
-        GM = ["gm0", "gm1", "gm2", "gm3", "l0"]
-        act(T.gb[:, 128:256], T.gm[:].indirect(T.l0[:, 8:16]), GM, ["gb1"])
-        close("a")
-        copy(T.gb[:, 0:128], T.gm[:].indirect(T.l0[:, 0:8]), GM, ["gb0"])
-        close("v")
+    def gather(q, gm, lst, a, n, rd):
+        args = (T.gb[:, 32 * a:32 * (a + n)], gm.indirect(lst[:, 2 * a:2 * (a + n)]), rd, ["gb%d" % j for j in range(a, a + n)])
+        if q == "a":
+            act(*args, cut=True)
+        else:
+            copy(*args, True)
+        close(q)
 
-    def align(k7, n7, slot, aside):
-        op("v", lambda: V.transpose(T.tb[:], T.gb[:]), r=["gb0", "gb1"], w=["tb"])
-        step(ORDER[0], k7, n7)
-        aside()
-        for name in ORDER[1:]:
+    def first(gm, lst, rd):
+        gather("a", gm, lst, 1, 1, rd)
+        gather("v", gm, lst, 0, 1, rd)
+
+    def align(k7, n7, slot, w, gm, lst, rd, aside):
+        gather("a", gm, lst, 2, 3, rd)
+        turn(0, 2, "t0")
+        thin(1, 1, ["t0"])
+        gather("a", gm, lst, 5, 3, rd)
+        for name in ORDER:
             step(name, k7, n7)
-        act(T.pc[:, slot:slot + 1], T.xa[:, 31:32], ["h7"], ["pc%d" % slot], scale=1.0 / UNIT)
+            if name == "t2":
+                aside()
+        act(T.pc[:, slot:slot + 1], T.xa[:, 62:63], ["h7"], ["pc%d" % slot], scale=1.0 / UNIT)
         close("a")
-        quant(T.xq[:], T.xsc[:], T.xa[:], ["h7"], ["xq"])
-        mm(5, 128, T.stq[:], T.sts[:], T.xq[:], T.xsc[:], ["stq", "xq"])
+        quant(T.xq[:], T.xsc[:], T.xa[:], ["h7"] + XB, ["xq"])
+        mm(5, 128, T.stq[:, w:w + 128], T.sts[:, w:w + 128], T.xq[:], T.xsc[:], ["stq%d" % w, "xq"])
 
-    def offsets(out, n, okey):
-        ts(out[:], bank[5][:, 8:8 + n], col(0), None, A.add, None, ["b5", "ff"], [okey])
+    def masked(out, k, a, n, mk, rd, key):
+        tt(out, bank[k][:, a:a + n], mk, A.mult, ["b%d" % k] + rd, [key], True)
         close("v")
 
-    def masked(k, a, n, at):
-        tt(T.gm[:, at:at + n], bank[k][:, a:a + n], T.mk[:, at:at + n], A.mult, ["b%d" % k, "mk"],
-           ["gm%d" % q for q in range(at // 32, (at + n) // 32)])
+    def blend(out, window, lst, da, rd, wr):
+        tt(out, window.indirect(lst), da, A.add, rd, wr, True)
         close("v")
 
-    def blend(tile, at, n, win, lst, da, rd, wr):
-        tt(tile[:, at:at + n], win.indirect(lst), da, A.add, rd, wr)
-        close("v")
-
-    def win(a):
-        return T.lq[:, a:a + 128], T.ls[:, a:a + 128]
-
-    L = ["lin", "lown"]
-    a0, u0 = 128 * (1 - b0), 128 * b0
-    mm(4, 128, *win(u0), *win(a0), L)
-    decode(256, T.lq[:, 0:256], T.ls[:, 0:256], L)
-    masked(4, 0, 128, 0)
-    quant(T.stq[:], T.sts[:], T.st[:], ["st0", "st1", "st2", "st3"], ["stq"])
-    gather()
+    L = ["lin", "qown", "sown"]
+    mm(4, 128, *win(256), *win(384), L)
+    decode(256, *win(256, 256), L)
+    masked(T.gm0[:], 4, 0, 128, T.mka[:], ["mka"], "gm0")
+    first(T.gm0[:], T.lg0, ["gm0", "lg0"])
+    quant(T.stq[:, 0:128], T.sts[:, 0:128], T.st[:], ["st0", "st1", "st2", "st3"], ["stq0"])
     op("s", lambda: g.sync.dma_start(T.wt[:], T.w[:]), r=["lin", "yin"], w=["wt"], dma=True)
     close("s")
-    ay, uy = 256 + 64 * b0, 320 - 64 * b0
-    Y = ["lin", "lown", "yin"] + (["lpad"] if not b0 and b1 else [])
-    mm(6, 128, *win(uy - 64 * ha1), *win(256), Y)
+    Y = L + ["yin", "qout", "sout"]
+    mm(6, 128, *win(128 + 64 * b0), *win(128), Y)
+    D = {}
 
     def aside0():
-        for b in range(4):
-            act(T.d0[:, b:1024:4], bank[b][:, 0:256], ["b%d" % b], ["d0%d" % b], scale=0.5)
+        D["a0"], D["b0"], u0, u1 = halves([("da0", lambda b: T.da0[:, b:256:4], 64, 64), ("db0", lambda b: T.db0[:, b:512:4], 128, 128),
+                                           ("dt0", lambda b: T.dt0[:, :, 0, b:16:4], 0, 32), ("dt1", lambda b: T.dt0[:, :, 1, b:16:4], 32, 32)])
+        decode(128, *win(128), Y)
+        act(T.da0[:, 256:512], T.dt0[:], u0 + u1, ["da0u"])
         close("a")
 
-    D0 = ["d0%d" % b for b in range(4)]
-    align(0, 160, 0, aside0)
-    masked(6, ay - 256, 64, 64 * ha1)
-    offsets(T.o0, 32, "o0")
-    blend(T.mt, 0, 512, T.d0[:, 4 * u0:4 * u0 + 512], T.o0[:], T.d0[:, 4 * a0:4 * a0 + 512], D0 + ["o0"], ["mt0"])
-    quant(T.m0q[:], T.m0s[:], T.mt[:], ["mt0"], ["m0"])
-    store("s", T.pf[0:1, 0:64], T.pc[64:128, 0:1], ["pc0"], ["pfk"])
+    align(0, 96, 0, 0, T.gm0[:], T.lg0, ["gm0", "lg0"], aside0)
+    ay, by = 64 * b0, 64 - 64 * b0
+    for lo, row, f, adds in ((64, T.i1, "g1", (0.0, 48.0)), (0, T.i0, "g0", (16.0, 0.0))):
+        for (a, b), add in zip(((0, 4), (4, 16)), adds):
+            ts(T.lg1[lo:lo + 64, a:b], row[lo:lo + 64, a:b], T.ff[lo:lo + 64, place[f]:place[f] + 1], add, A.add, A.add,
+               ["i0", "i1", "f" + f], ["lg1%d%d" % (lo, a)])
+    for k in range(2):
+        ts(T.mkb[:, 32 * k:32 * k + 32], T.uu[:, 0:256:8], col("e"), None, A.is_equal, None, ["uu", "fe"], ["mkb%d" % k])
+    close("v")
+    if b1:
+        D["by"], u0, u1 = halves([("dby", lambda b: T.dby[:, b:256:4], by, 64), ("dy0", lambda b: T.dty[:, :, 0, b:16:4], ay, 32),
+                                  ("dy1", lambda b: T.dty[:, :, 1, b:16:4], ay + 32, 32)])
+        act(T.day[:], T.dty[:], u0 + u1, ["day"])
+        D["ay"] = ["day"]
+    else:
+        D["by"], D["ay"] = halves([("dby", lambda b: T.dby[:, b:256:4], by, 64), ("day", lambda b: T.day[:, b:256:4], ay, 64)])
+        afill(beta(16, 8), 8, 0.0, "xb2", ["xq"])
+        afill(beta(24, 8), 8, 64.0, "xb3", ["xq"])
+        XB.append("xb3")
+    afill(beta(0, 16), 16, 0.0, "xb0", ["xq", "xb1"])
+    close("a")
+    masked(T.gm1[:, 16:80], 6, by, 64, T.mka[:, 0:64], ["mka"], "gmy")
+    ts(T.o0[:], bank[5][:, 16:48], col("m32"), col("e"), A.add, A.add, ["b5", "fm32", "fe"], ["o0"], True)
+    close("v")
+    if not b1:
+        hot(0, 64, 64, 16, 0, "a8", "c", "k7b")
+    close("v")
+    blend(T.mt[:, 192:512], T.db0[:], T.o0[:, 0:20], T.da0[:, 0:320], D["a0"] + D["b0"] + ["da0u", "o0"], ["mt1"])
+    blend(T.mt[:, 512:704], T.db0[:], T.o0[:, 20:32], T.da0[:, 320:512], D["b0"] + ["da0u", "o0"], ["mt2"])
+    quant(*win(512), T.mt[:, 0:512], ["mtz0", "mt1"], ["m01"])
+    quant(*win(640), T.mt[:, 512:1024], ["mtz1", "mt2"], ["m02"])
+    fields(names[13:])
+    own = 64 * (1 - b1)
+    store("s", T.pf[0:1, 128:192], T.pc[own:own + 64, 0:1], ["pc0"], ["pf0"])
     close("s")
 
-    mm(4, 128, T.m0q[:], T.m0s[:], T.m0q[:], T.m0s[:], ["m0"])
-    decode(128, T.m0q[:], T.m0s[:], ["m0"])
-    masked(4, 64 * ha1, 64, 64 * hb1)
-    gather()
+    mm(4, 128, *win(496), *win(512), L + ["m01"])
+    mm(7, 128, *win(496), *win(640), L + ["m01", "m02"])
+    decode(128, *win(560), ["m01", "m02"])
+    masked(T.gm1[:, 0:16], 4, 112, 16, T.mkb[:, 0:16], ["mkb0"], "gm1")
+    floats(names[13:])
+    masked(T.gm1[:, 80:128], 7, 0, 48, T.mkb[:, 0:48], ["mkb0", "mkb1"], "gm1b")
+    first(T.gm1[:, 0:80], T.lg1, ["gm1", "gmy", "lg1640", "lg100"])
 
     def aside1():
-        for b in range(4):
-            act(T.d1a[:, :, :, b:32:4], bank[b][:, 64 * ha1:64 * ha1 + 64], ["b%d" % b], ["d1a%d" % b], scale=0.5)
-            act(T.d1f[:, b:512:4], bank[b][:, 0:128], ["b%d" % b], ["d1f%d" % b], scale=0.5)
-            close("a")
-        decode(128, *win(256), Y)
-        for h, par in enumerate((1 - b2, b2)):
-            act(T.d1s[:, 128 * h:128 * h + 128], T.d1a[:, :, par, :], ["d1a%d" % b for b in range(4)], ["d1s%d" % h])
-        close("a")
-        for b in range(4):
-            for h in range(ha1 + 1):
-                act(run(T.dy, 256 * h + b, 64, 4), bank[b][:, uy - 256:uy - 192], ["b%d" % b], ["dy%d%d" % (h, b)], scale=0.5)
-            act(T.dz[:, b:256:4], bank[b][:, ay - 256:ay - 192], ["b%d" % b], ["dz%d" % b], scale=0.5)
-        close("a")
+        D["a1"], D["b1"] = halves([("da1", lambda b: T.da1[:, b:256:4], 0, 64), ("db1", lambda b: T.db1[:, b:256:4], 64, 64)])
 
-    D1 = ["d1f%d" % b for b in range(4)] + ["d1s0", "d1s1"]
-    DY = ["dy%d%d" % (h, b) for b in range(4) for h in range(ha1 + 1)] + ["dz%d" % b for b in range(4)]
-    align(160, 160, 4, aside1)
-    offsets(T.o1, 32, "o1")
-    blend(T.mt, 0, 128, T.d1f[:], T.o1[:, 0:8], T.d1s[:, 0:128], D1 + ["o1"], ["mt0"])
-    quant(T.m1q[:], T.m1s[:], T.mt[:], ["mt0"], ["m1"])
+    align(0, 96, 4, 0, T.gm1[:, 16:128], T.lg1, ["gm1b", "gmy", "lg1644", "lg104"], aside1)
+    act(beta(0, 8), T.uu[:, 0:32:4], ["uu", "xq"], ["xb0"], scale=0.5)
+    close("a")
+    quant(T.wq[:], T.ws[:], T.wt[:], ["wt"], ["wq"])
+    ts(T.lg2[:], T.kj[:, 0:16], 2.0, col("g1"), A.mult, A.add, ["kj", "fg1"], ["lg2"])
+    ts(run(T.k7, 128, 8, 2), T.kj[:, 8 * at2:8 * at2 + 8], col("q"), None, A.is_equal, None, ["kj", "fq", "k7z"], ["k7c"])
+    fill(T.gm2[:], 0.0, "gm2")
+    close("v")
+    ts(T.o1[:], bank[5][:, 16:32], 8.0, col("s"), A.mult, A.add, ["b5", "fs"], ["o1"], True)
+    close("v")
+    ts(T.oy[:], bank[5][:, 32:48], col("m32"), col("e"), A.add, A.add, ["b5", "fm32", "fe"], ["oy"], True)
+    close("v")
+
+    def blend1(out, a, wr):
+        blend(out, T.db1[:, 16 * a:256], T.o1[:, 8 * a:8 * a + 8], T.da1[:, 128 * a:128 * a + 128], D["a1"] + D["b1"] + ["o1"], wr)
+
+    blend1(T.mt[:, 0:128], 1 - b2, ["mtz0"])
+    blend1(T.mu[:, 384:512], b2, ["mu0"])
+    quant(T.m1q[:], T.m1s[:], T.mt[:, 0:512], ["mtz0", "mt1"], ["m1"])
     need("g", ["m1"])
     e8 = topo.engines(core, c4)
     rid, pid = int(topo.addr(c4)[0]), int(topo.addr(c4)[1])
@@ -441,58 +547,69 @@ def rank_program(g, core, T, topo):
     sent += 2 * len(e8)
     landed("hin", "arr2", 2 * len(e8))
 
-    blend(T.mu, 384, 128, T.d1f[:], T.o1[:, 8:16], T.d1s[:, 128:256], D1 + ["o1"], ["mu0"])
-    blend(T.mu, 128, 256, T.dy[:, 0:256 * ha1 + 256], T.o1[:, 16:32], T.dz[:], DY + ["o1"], ["mu1"])
-    quant(T.wq[:], T.ws[:], T.wt[:], ["wt"], ["wq"])
+    blend(T.mu[:, 128:384], T.dby[:], T.oy[:], T.day[:], D["ay"] + D["by"] + ["oy"], ["mu1"])
+    spreader("e", 128)
     quant(T.hq[:, 0:128], T.hs[:, 0:128], T.mu[:], ["mu0", "mu1", "muz"], ["hown"])
+    quant(T.stq[:, 128:256], T.sts[:, 128:256], T.st[:], ["st0", "st1", "st2", "st3"], ["stq128"])
+    if b1:
+        ts(T.ly[:, 0:8], T.iy[:], col("y0"), None, A.add, None, ["iy", "fy0"], ["ly0"])
+    else:
+        ts(T.ly[:, 0:8], T.iy[:], col("y0"), col("y1"), A.add, A.add, ["iy", "fy0", "fy1"], ["ly0"])
+    ts(T.ly[:, 8:12], T.kj[:, 0:4], col("s4"), 128.0, A.add, A.add, ["kj", "fs4"], ["ly1"])
+    ts(T.ld[:], T.id[:], col("i16"), col("e"), A.add, A.add, ["id", "fi16", "fe"], ["ld"])
+    close("v")
 
     def prod(k, q, s, rd):
         for o in range(2):
             mm(k + o, 128, T.wq[:, 128 * o:128 * o + 128], T.ws[:, 128 * o:128 * o + 128], q, s, ["wq"] + rd)
 
-    prod(0, T.m0q[:], T.m0s[:], ["m0"])
+    def stage(k, a, n, at, key):
+        for o in range(2):
+            act(T.ys[:, 192 * o + at:192 * o + at + n], bank[k + o][:, a:a + n], ["b%d" % (k + o)], ["ys%s%d" % (key, o)])
+            close("a")
+
+    prod(0, *win(560), ["m01", "m02"])
     prod(2, T.m1q[:], T.m1s[:], ["m1"])
-    for o in range(2):
-        act(T.ya[:, 12 * o:12 * o + 8, b1, :], bank[o][:, 64:128], ["b%d" % o], ["ya0%d" % o])
-        act(T.ya[:, 12 * o + 8:12 * o + 12, 1 - b2, :], bank[2 + o][:, 0:32], ["b%d" % (2 + o)], ["ya1%d" % o])
-        close("a")
+    stage(0, 64 * b1, 64, 64 * b1, "a")
+    stage(2, 0, 32, 160 - 32 * b2, "b")
 
     H = ["hin", "hown"]
     mm(4, 128, T.hq[:, 32:160], T.hs[:, 32:160], T.hq[:, 32:160], T.hs[:, 32:160], H)
     prod(6, T.hq[:, 0:128], T.hs[:, 0:128], ["hown"])
     decode(128, T.hq[:, 32:160], T.hs[:, 32:160], H)
-    masked(4, 32 * qa2, 32, 32 * qb2)
-    gather()
-    store("s", T.pf[0:1, 64:128], T.pc[64 * ha1:64 * ha1 + 64, 4:5], ["pc4", "hin"], ["pfu"])
-    close("s")
-    store("s", T.pt[0:1, 128:192], T.pc[64 * hb1:64 * hb1 + 64, 4:5], ["pc4"])
+    masked(T.gm2[:, 4 * (at2 & 1):4 * (at2 & 1) + 32], 4, 32 * bt2, 32, T.mkb[:, 0:32], ["mkb0"], "gm2")
+    first(T.gm2[:], T.lg2, ["gm2", "lg2"])
+    store("s", T.pf[0:1, 0:128], T.pc[:, 4:5], ["pc4", "hin"], ["pf1"])
     close("s")
 
     def aside2():
+        D["a2"], D["b2"] = halves([("da2", lambda b: T.da2[:, b:128:4], 32 * at2, 32), ("db2", lambda b: T.db2[:, b:128:4], 32 * bt2, 32)])
+        stage(6, 32, 64, 64 - 64 * b1, "c")
+        stage(6, 96, 32, 128 + 32 * b2, "d")
+        act(T.dc2[:], T.da2[:].indirect(T.ld[:]), D["a2"] + ["ld"], ["dc2"])
+        close("a")
         for o in range(2):
-            act(T.ya[:, 12 * o:12 * o + 8, 1 - b1, :], bank[6 + o][:, 32:96], ["b%d" % (6 + o)], ["ya2%d" % o])
-            act(T.ya[:, 12 * o + 8:12 * o + 12, b2, :], bank[6 + o][:, 96:128], ["b%d" % (6 + o)], ["ya3%d" % o])
+            act(T.ya[:, 192 * o:192 * o + 192], T.ys[:, 192 * o:192 * o + 192].indirect(T.ly[:]),
+                ["ys%s%d" % (u, o) for u in "abcd"] + ["ly0", "ly1"], ["ya%d" % o])
             close("a")
-        for b in range(4):
-            act(T.d2[:, b:512:4], bank[b][:, 0:128], ["b%d" % b], ["d2%d" % b], scale=0.5)
-            act(T.d2a[:, b:128:4], bank[b][:, 32 * qa2:32 * qa2 + 32], ["b%d" % b], ["d2a%d" % b], scale=0.5)
-        close("a")
-        for o in range(2):
-            store("s", T.y[:, 224 * o:224 * o + 192], T.ya[:, 12 * o:12 * o + 12, :, :], ["ya%d%d" % (u, o) for u in range(4)])
+            store("s", T.y[:, 224 * o:224 * o + 192], T.ya[:, 192 * o:192 * o + 192], ["ya%d" % o])
         close("s")
-        act(T.p0[0:1, :, b1, :], T.pf[0:1, 0:64], ["pfk"], ["p0k"])
-        act(T.p0[0:1, :, 1 - b1, :], T.pf[0:1, 64:128], ["pfu"], ["p0u"])
+        for a in range(2):
+            act(T.pa[0:1, :, a, b1, :], T.pf[0:1, 128 + 32 * a:160 + 32 * a], ["pf0"], ["pa0%d" % a])
+            act(T.pa[0:1, :, a, 1 - b1, :], T.pf[0:1, 32 * a:32 * a + 32], ["pf1"], ["pa1%d" % a])
+            act(T.pb[0:1, :, a, :], T.pf[0:1, 64 + 32 * a:96 + 32 * a], ["pf1"], ["pb%d" % a])
         close("a")
-        store("s", T.pt[0:1, 0:128], T.p0[0:1, :, :, :], ["p0k", "p0u"])
+        store("s", T.pt[0:1, 0:128], T.pa[0:1, :, :, :, :], ["pa00", "pa01", "pa10", "pa11"])
+        store("s", T.pt[0:1, 128:192], T.pb[0:1, :, :, :], ["pb0", "pb1"])
         close("s")
 
-    align(320, 64, 8, aside2)
-    store("a", T.pt[0:1, 192:224], T.pc[32 * qb2:32 * qb2 + 32, 8:9], ["pc8"])
+    align(96, 48, 8, 128, T.gm2[:], T.lg2, ["gm2", "lg2"], aside2)
+    store("a", T.pt[0:1, 192:224], T.pc[32 * at2:32 * at2 + 32, 8:9], ["pc8"])
     close("a")
-    D2 = ["d2%s%d" % (u, b) for b in range(4) for u in ("", "a")]
-    offsets(T.o2, 8, "o2")
-    blend(T.mt, 0, 128, T.d2[:], T.o2[:], T.d2a[:], D2 + ["o2"], ["mt0"])
-    quant(T.m2q[:], T.m2s[:], T.mt[:], ["mt0"], ["m2"])
+    ts(T.o2[:], bank[5][:, 16:24], 4.0, col("e"), A.mult, A.add, ["b5", "fe"], ["o2"], True)
+    close("v")
+    blend(T.mt[:, 0:128], T.db2[:], T.o2[:], T.dc2[:], D["b2"] + ["dc2", "o2"], ["mtz0"])
+    quant(T.m2q[:], T.m2s[:], T.mt[:, 0:512], ["mtz0", "mt1"], ["m2"])
     prod(6, T.m2q[:], T.m2s[:], ["m2"])
     store("s", T.oc[:, 0:128], T.m2q[:, 0:32].bitcast(dt.uint8), ["m2"])
     for k in range(4):

@@ -1,11 +1,14 @@
+import math
 from concourse.bass import DstId, RemoteDMATransfer
 from concourse.mybir import dt, AluOpType, ActivationFunctionType
 
 F32, BF, I32, U16, X4, U8 = "float32", "bfloat16", "int32", "uint16", "float8_e4m3fn_x4", "uint8"
 LOW = -1.0e29
 UNIT = 0.125
-ORDER = ("p0 q0 t1 p1 q1 d1 p2 q2 l1 t2 d2 p3 q3 h1 g1 l2 d3 p4 q4 l3 h2 g2 d4 p5 q5 l4 h3 g3 d5 p6 q6 l5 h4 g4 d6 "
-         "p7 l6 h5 g5 d7 l7 h6 g6 h7").split()
+ORDER = ("p0 q0 t1 p1 q1 d1 p2 q2 l1 t2 d2 p3 q3 h1 g1 l2 d3 p4 l3 h2 g2 p5 q5 d4 l4 h3 d5 p6 q6 l5 h4 g4 "
+         "p7 l6 d6 h5 g5 d7 l7 h6 h7").split()
+ORDER_AHEAD = ("t0 t1 t3 p1 q1 t2 d1 l1 p2 q2 h1 g1 p3 d2 l2 p4 q4 l3 h2 g2 d3 p5 q5 d4 l4 h3 d5 p6 q6 l5 h4 g4 "
+               "p7 l6 d6 h5 g5 d7 l7 h6 h7").split()
 
 
 def _sb(shape, d):
@@ -14,27 +17,27 @@ def _sb(shape, d):
 
 SCRATCH = {
     "xs": _sb([1024], BF), "wt": _sb([1024], BF), "rq": _sb([256], X4), "rs": _sb([256], U8),
-    "lq": _sb([768], X4), "ls": _sb([768], U8), "wq": _sb([256], X4), "ws": _sb([256], U8),
-    "et": _sb([520], BF), "eq": _sb([512], X4), "es": _sb([512], U8),
+    "lq": _sb([960], X4), "ls": _sb([960], U8), "wq": _sb([256], X4), "ws": _sb([256], U8),
+    "eq": _sb([512], X4), "es": _sb([512], U8),
     "st": _sb([512], BF), "stq": _sb([256], X4), "sts": _sb([256], U8),
     "pi": _sb([2], I32), "fi": _sb([24], I32), "ff": _sb([24], F32),
-    "uu": _sb([256], BF), "vv": _sb([128], BF), "zz": _sb([320], BF),
-    "ip": _sb([16], F32), "i0": _sb([16], F32), "i1": _sb([16], F32), "ib": _sb([4], F32), "iy": _sb([8], F32),
+    "uu": _sb([256], BF), "zz": _sb([608], BF),
+    "ip": _sb([16], F32), "i0": _sb([16], F32), "i1": _sb([16], F32), "ib": _sb([16], F32), "iy": _sb([8], F32),
     "id": _sb([8], F32), "kj": _sb([32], F32), "ke": _sb([8], F32), "cx": _sb([2], F32),
-    "mka": _sb([128], F32), "mkb": _sb([64], F32),
-    "lp": _sb([16], U16), "lg0": _sb([16], U16), "lg1": _sb([16], U16), "lg2": _sb([16], U16), "lb": _sb([4], U16),
+    "mka": _sb([128], F32), "mkb": _sb([32], F32),
+    "lp": _sb([16], U16), "lg0": _sb([16], U16), "lg1": _sb([16], U16), "lg2": _sb([16], U16), "lb": _sb([16], U16),
     "ly": _sb([12], U16), "ld": _sb([8], U16),
-    "gm0": _sb([128], F32), "gm1": _sb([128], F32), "gm2": _sb([40], F32), "gb": _sb([256], F32),
-    "g8": _sb([568], F32), "g3": _sb([128], F32), "ic": _sb([4], F32), "ie": _sb([4], I32), "ig": _sb([4], F32),
-    "q0": _sb([32], F32), "pr0": _sb([108], F32), "pr3": _sb([648], F32), "pr8": _sb([648], F32), "p7": _sb([24], F32),
-    "km": _sb([280], F32), "k7": _sb([144], F32), "hz": _sb([32], F32), "hr4": _sb([540], F32), "hr5": _sb([840], F32),
-    "xa": _sb([512], BF), "xq": _sb([128], X4), "xsc": _sb([128], U8),
-    "o0": _sb([32], U16), "o1": _sb([16], U16), "oy": _sb([16], U16), "o2": _sb([8], U16),
-    "da0": _sb([512], F32), "db0": _sb([512], F32), "dt0": _sb([8, 2, 16], F32), "dty": _sb([8, 2, 16], F32),
-    "day": _sb([256], F32), "dby": _sb([256], F32), "da1": _sb([256], F32), "db1": _sb([256], F32),
-    "da2": _sb([128], F32), "db2": _sb([128], F32), "dc2": _sb([128], F32),
-    "mt": _sb([1024], BF), "mu": _sb([512], BF),
-    "m1q": _sb([128], X4), "m1s": _sb([128], U8), "hq": _sb([160], X4), "hs": _sb([160], U8),
+    "gm0": _sb([128], F32), "gm1": _sb([64], F32), "gm2": _sb([40], F32), "gb": _sb([256], F32),
+    "g8": _sb([624], F32), "g3": _sb([224], F32), "ic": _sb([16], F32), "ie": _sb([16], I32), "ig": _sb([16], F32),
+    "q0": _sb([32], F32), "pr3": _sb([534], F32), "pr4": _sb([224], F32), "pr5": _sb([280], F32), "pr8": _sb([576], F32),
+    "p7": _sb([64], F32), "km": _sb([288], F32), "k7": _sb([176], F32), "hz": _sb([32], F32),
+    "hr4": _sb([812], F32), "hr5": _sb([670], F32), "hr6": _sb([246], F32),
+    "xa": _sb([512], BF), "xq": _sb([448], X4), "xsc": _sb([448], U8),
+    "o0": _sb([32], U16), "o1": _sb([8], U16), "of": _sb([8], U16), "o2": _sb([8], U16),
+    "da0": _sb([512], F32), "db0": _sb([512], F32), "dt0": _sb([8, 2, 16], F32),
+    "d1": _sb([384], F32), "df": _sb([384], F32), "d2": _sb([256], F32), "dc2": _sb([128], F32),
+    "mt": _sb([1088], BF), "mu": _sb([512], BF),
+    "hq": _sb([288], X4), "hs": _sb([288], U8), "dq": _sb([128], X4), "ds": _sb([128], U8),
     "m2q": _sb([128], X4), "m2s": _sb([128], U8),
     "ys": _sb([384], F32), "ya": _sb([384], F32), "y2": _sb([64], F32),
     "pc": _sb([12], F32), "pf": _sb([192], F32), "pa": _sb([4, 2, 2, 8], F32), "pb": _sb([4, 2, 8], F32),
@@ -42,7 +45,7 @@ SCRATCH = {
 for _k in range(8):
     SCRATCH["b%d" % _k] = ("psum", [128, 512], F32)
 NPOOL = 140
-SEMAPHORES = ["arr0", "arry", "arr2", "sent"] + ["s%d" % _k for _k in range(NPOOL)]
+SEMAPHORES = ["arr0", "arrj", "arry", "arr1", "arr2", "arr3", "sent"] + ["s%d" % _k for _k in range(NPOOL)]
 
 
 def make_order(g, T):
@@ -175,7 +178,7 @@ def rank_program(g, core, T, topo):
             op("a", lambda: S.activation(out, in_, ACT.Identity, bias=bias, scale=scale), r=rd, w=wr, cut=cut)
 
     def afill(out, n, val, key, rd=(), rows=128):
-        act(out, T.zz[0:rows, 0:n], ["zz"] + list(rd), [key], scale=0.0, bias=val)
+        act(out, T.zz[0:rows, 1:2 * n:2], ["zz"] + list(rd), [key], scale=0.0, bias=val)
 
     def quant(q, s, tile, rd, wr):
         op("v", lambda: V.quantize_mx(q, s, tile), r=rd, w=wr, cut=True)
@@ -194,13 +197,14 @@ def rank_program(g, core, T, topo):
     def win(a, n=128):
         return T.lq[:, a:a + n], T.ls[:, a:a + n]
 
-    op("s", lambda: g.sync.dma_start(T.xs[:], T.x[:]), w=["xs"], dma=True)
-    close("s")
+    for h in range(2):
+        store("s", T.xs[:, 512 * h:512 * h + 512], T.x[:, 512 * h:512 * h + 512], [], ["xs%d" % h])
+        close("s")
 
     FIELDS = {"pk0": (3, 64) if b0 else (0, 192), "pk1": (6, 7) if b0 else (8, 3),
               "e": (6, 3), "c": (6, 7), "s": (6, 15), "m": (9, 3), "a8": (8, 8), "a": (11, 1), "c2": (5, 14),
-              "g0": (6, 104), "g1": (9, 5), "m32": (3, 96), "h4": (8, 4), "q": (8, 31),
-              "s4": (4, 60), "i16": (4, 48), "y0": (3, 120) if b1 else (3, 64), "y1": (4, 28)}
+              "g0": (6, 104), "g1": (9, 5), "m32": (3, 96), "h4": (8, 4), "q": (8, 31), "u": (9, 1),
+              "s4": (4, 60), "i16": (4, 48), "y0": (3, 120 if b1 else 64), "y1": (4, 0 if b1 else 28)}
     place = {n: k for k, n in enumerate(FIELDS)}
     col = lambda n: T.ff[:, place[n]:place[n] + 1]
 
@@ -219,56 +223,57 @@ def rank_program(g, core, T, topo):
     c = r % 4
     iota(T.pi[:, 0:1], [[0, 1]], 0, 64, "pi", small=False)
     for k, (u, v) in enumerate(((c, c ^ 1), (c ^ 3, c ^ 2))):
-        iota(T.ip[:, 8 * k:8 * k + 8], [[8 * (v - u), 2], [32, 2], [128 if b0 else 4, 2]], 8 * u, 0, "ip%d" % k)
+        iota(T.ip[:, 8 * k:8 * k + 8], [[8 * (v - u), 2], [32 - 64 * b2, 2], [128 if b0 else 4, 2]], 8 * u + 32 * b2, 0, "ip%d" % k)
     iota(T.kj[:], [[1, 32]], 0, 0, "kj")
-    iota(T.vv[:], [[1, 128]], 0, -1, "vv")
-    iota(T.uu[:], [[0, 8], [1, 4], [0, 8]], 0, 0, "uu")
     iota(T.i0[:], [[1, 8], [16, 2]], 0, 0, "i0")
-    iota(T.ib[:], [[48, 2], [16, 2]], 0, 0, "ib")
+    iota(T.ib[:], [[-1, 2], [0, 2], [16, 4]], 4, 0, "ib")
+    iota(T.ie[:, 12:16], [[0, 4]], 0, 0, "ie4", small=False)
+    iota(T.uu[:], [[0, 8], [1, 4], [0, 8]], 0, 0, "uu")
     fill(T.zz[:], 0.0, "zz")
     close("v")
     fields(names[:2])
-    fill(T.et[:], 0.0, "etz")
-    close("v")
+    fields(names[2:7])
     floats(names[:2])
-    fields(names[2:13])
+    fields(names[7:13])
     ts(T.lp[:], T.ip[:], col("pk0"), col("pk1"), A.add, A.add, ["ip0", "ip1", "fpk0", "fpk1"], ["lp"])
     close("v")
     floats(names[2:13])
-    fill(T.xa[:], 0.0, "xaz")
-    close("v")
 
-    kp = lambda j: 4 if j == 0 else 3 if j % 2 else 8
-    kh = lambda j: 5 - j % 2
-    sums_at = lambda j: (T.pr0, 8) if j == 0 else (T.pr3, 216 * (j // 2) + 21) if j % 2 else (T.pr8, 216 * (j // 2 - 1) + 16)
-    nums_at = lambda j: (T.hr4, 180 * (j // 2) + 4) if j % 2 else (T.hr5, 180 * (j // 2 - 1))
+    KP = [4, 3, 8, 5, 6, 4, 3, 8, 3]
+    STEPS = {3: (0, 1, 2), 4: (0, 2, 3), 5: (0, 1, 2), 6: (1, 2, 3), 8: (0, 1, 7)}
+    pp = lambda j: math.lcm(KP[j], KP[j + 1])
+    KH = [0, 4, 5, 8, 6, 5, 8, 6]
+    hp = lambda j: math.lcm(KH[j], KH[j + 1])
+    left = lambda j: 4 if KH[j] == 6 else 3
+    km_at = lambda j: 8 * sum(KH[:j])
+    sums_at = lambda j: [(T.pr4, 8), (T.pr3, 21), (T.pr8, 32), (T.pr5, 20), (T.pr3, 222), (T.pr4, 116), (T.pr3, 339), (T.pr8, 376)][j]
+    nums_at = lambda j: [(T.hr4, 4), (T.hr5, 10), (T.hr4, 164), (T.hr6, 6), (T.hr5, 340), (T.hr4, 364)][j - 1]
     g8_at = lambda j: 64 * j + (24 if j > 1 else 0)
-    G8Z = ["g8z0", "g8z1", "g8z2"]
+    g3_at = {1: 0, 3: 32, 4: 80, 5: 128, 6: 160, 8: 192}
+    G8Z = ["g8z0", "g8z1"]
+    afill(T.q0[:, 1:32], 31, LOW, "top0")
+    afill(T.q0[:, 0:1], 1, 0.0, "top")
+    afill(T.pr4[:, 0:224:4], 56, LOW, "prz0")
+    afill(T.pr3[:, 0:534:3], 178, LOW, "prz1")
+    afill(T.pr8[:, 0:576:8], 72, LOW, "prz2")
+    afill(T.pr5[:, 0:280:5], 56, LOW, "prz3")
     afill(T.g8[:, 1:568:2], 284, 0.0, "g8z0")
     afill(T.g8[:, 130:154:2], 12, 0.0, "g8z1")
-    afill(T.g8[:, 538:568:2], 15, 0.0, "g8z2")
-    afill(T.q0[:], 32, LOW, "top0")
-    afill(T.pr0[:, 0:108:4], 27, LOW, "prz0")
-    afill(T.pr3[:, 0:648:3], 216, LOW, "prz1")
-    afill(T.pr8[:, 0:648:8], 81, LOW, "prz2")
-    afill(T.st[:, 1:512:2], 256, 0.0, "stz")
-    close("a")
-    afill(T.q0[:, 0:1], 1, 0.0, "top", ["top0"])
-    afill(T.st[0:1, 1:512:4], 128, 2.0, "st1", ["stz"], 1)
-    afill(T.st[0:1, 3:512:4], 128, 32.0, "st3", ["stz"], 1)
     close("a")
 
-    quant(T.rq[:], T.rs[:], T.xs[:], ["xs"], ["rq"])
+    for h in range(2):
+        quant(T.rq[:, 128 * h:128 * h + 128], T.rs[:, 128 * h:128 * h + 128], T.xs[:, 512 * h:512 * h + 512], ["xs%d" % h], ["rq%d" % h])
     slot = lambda s: 256 + 128 * (s & 1) + 64 * (1 - (s >> 1 & 1))
 
     def pick(at, a, n, key):
         copy(T.lq[:, at:at + 16 * n].bitcast(dt.uint32), T.rq[:].bitcast(dt.uint32).indirect(T.lp[:, a:a + n]),
-             ["rq", "lp"], ["q" + key], True)
+             ["rq0", "rq1", "lp"], ["q" + key], True)
         close("v")
-        act(T.ls[:, at:at + 16 * n], T.rs[:].indirect(T.lp[:, a:a + n]), ["rq", "lp"], ["s" + key], cut=True)
+        act(T.ls[:, at:at + 16 * n], T.rs[:].indirect(T.lp[:, a:a + n]), ["rq0", "rq1", "lp"], ["s" + key], cut=True)
         close("a")
 
-    pick(0, 4, 12, "out")
+    pick(0, 4, 4, "one")
+    pick(64, 8, 8, "out")
     pick(slot(r), 0, 4, "own")
     c1, c2, c3, c4 = (T.cores[r ^ k] for k in (1, 2, 3, 4))
     e = topo.engines(core, c1)
@@ -278,50 +283,69 @@ def rank_program(g, core, T, topo):
     def view(t, a, codes):
         return t[:, a:a + 64].bitcast(dt.uint8) if codes else t[:, a:a + 64]
 
-    for codes in (True, False):
+    for keys, pieces in ((["qone"], (0,)), (["qout"], (1, 2)), (["sone", "sout"], (0, 1, 2))):
+        codes = keys[0][0] == "q"
         t = T.lq if codes else T.ls
-        need("g", ["qout" if codes else "sout"])
+        need("g", keys)
         es = (e0, e1, e2 + e3) if codes else (e2, e3, e0 + e1)
-        g.remote_dma_fused([RemoteDMATransfer(dst_ids=[dst_id(cc)], dma_engine_mask=mask_of(es[k]), remote_sem=T.sem.arr0,
+        g.remote_dma_fused([RemoteDMATransfer(dst_ids=[dst_id((c1, c3, c2)[k])], dma_engine_mask=mask_of(es[k]), remote_sem=T.sem.arr0,
                                               src=view(t, 64 * k, codes), dst=view(t, slot(r), codes))
-                            for k, cc in enumerate((c1, c3, c2))], local_sem=T.sem.sent)
-    rid, pid = int(topo.addr(c1)[0]), int(topo.addr(c1)[1])
-    g.remote_dma(view(T.lq, 192, True), view(T.lq, 64, True), T.sem.arry, T.sem.sent, pid, rid, mask_of(e))
-    g.remote_dma(view(T.ls, 192, False), view(T.ls, 64, False), T.sem.arry, T.sem.sent, pid, rid, mask_of(e))
-    sent = 4 * len(e)
+                            for k in pieces], local_sem=T.sem.sent)
+    sent = [2 * len(e)]
     landed("lin", "arr0", 2 * len(e))
-    landed("yin", "arry", 2 * len(e))
+    e8 = topo.engines(core, c4)
+    rest = [k for k in e if k not in e8]
 
-    at2, bt2 = 2 + b2, 3 - b2
+    def send(cc, es, q, s, a, at, n, sem, rd, key):
+        need("g", rd)
+        rid, pid = int(topo.addr(cc)[0]), int(topo.addr(cc)[1])
+        g.remote_dma(q[:, at:at + n].bitcast(dt.uint8), q[:, a:a + n].bitcast(dt.uint8), T.sem[sem], T.sem.sent, pid, rid, mask_of(es))
+        g.remote_dma(s[:, at:at + n], s[:, a:a + n], T.sem[sem], T.sem.sent, pid, rid, mask_of(es))
+        sent[0] += 2 * len(es)
+        landed(key, sem, 2 * len(es))
+
+    def send_numbers(cc, es, a, at, sem, key):
+        need("g", ["xq"])
+        h = len(es) // 2
+        g.remote_dma_fused([RemoteDMATransfer(dst_ids=[dst_id(cc)], dma_engine_mask=mask_of(x), remote_sem=T.sem[sem], src=src, dst=dst)
+                            for x, src, dst in ((es[:h], T.xq[:, a:a + 8].bitcast(dt.uint8), T.xq[:, at:at + 8].bitcast(dt.uint8)),
+                                                (es[h:], T.xsc[:, a:a + 32], T.xsc[:, at:at + 32]))], local_sem=T.sem.sent)
+        sent[0] += len(es)
+        landed(key, sem, len(es))
+
+    at2 = 3 - 3 * b2
+
+    def gfill(out, n, val, key, rd=()):
+        op("g", lambda: g.iota(out, [[0, n]], val, 0, allow_small_or_imprecise_dtypes=True), r=rd, w=[key])
+        close("g")
+
+    gfill(T.k7[:], 176, 0, "k7z")
+    op("g", lambda: g.affine_select(T.zz[:, 4:516:4], T.zz[:, 4:516:4], [[1, 128]], A.not_equal, 1.0, 0, -1), r=["zz"], w=["et"])
+    close("g")
+    gfill(T.st[:, 1:512:2], 256, 0, "stz")
     iota(T.i1[:], [[8, 8], [2, 2]], 0, 0, "i1")
-    iota(T.iy[:], [[1, 4], [4 if b1 else 32, 2]], 0, 0, "iy")
+    gfill(T.st[0:1, 1:512:4], 128, 2, "st1", ["stz"])
+    gfill(T.st[0:1, 3:512:4], 128, 32, "st3", ["stz"])
+    gfill(T.xa[:], 512, 0, "xaz")
+    gfill(T.mt[:, 0:192], 192, 0, "mtz0")
+    beta = lambda a, n, s=1: run(T.xa, 97 + 4 * a, n, 4 * s)
+    gfill(run(T.xa, 99, 32, 4), 32, 1, "xa3", ["xaz"])
+    op("g", lambda: g.iota(beta(0, 16), [[64, 2], [0, 8]], 128, 0, allow_small_or_imprecise_dtypes=True), r=["xaz"], w=["xb0"])
+    gfill(beta(17, 8, 2), 8, 64, "xb2", ["xaz"])
+    gfill(T.mt[:, 704:1088], 384, 0, "mtz1")
+    gfill(T.mu[:, 0:384], 384, 0, "muz")
+    gfill(T.g8[:, 568:624], 56, 0, "g8z3")
+    XB = ["xa3", "xb0", "xb2"]
+    sy = 4 if b1 else 32
+    iota(T.iy[:], [[1, 4], [sy - 2 * sy * b2, 2]], sy * b2, 0, "iy")
     iota(T.id[:], [[4, 4], [64, 2]], 0, 0, "id")
-    afill(T.km[:], 280, 0.0, "kmz")
+    afill(T.km[:], 288, 0.0, "kmz")
     afill(T.hz[:], 32, 0.0, "hzz")
-    afill(T.hr4[:, 0:540:4], 135, 0.0, "hrz0")
-    afill(T.hr5[:, 0:840:5], 168, 0.0, "hrz1")
-    afill(T.k7[:], 144, 0.0, "k7z")
+    afill(T.hr4[:, 0:812:4], 203, 0.0, "hrz0")
+    afill(T.hr5[:, 0:670:5], 134, 0.0, "hrz1")
+    afill(T.hr6[:, 0:246:6], 41, 0.0, "hrz2")
     close("a")
-    HRZ = ["hrz0", "hrz1"]
-    ts(T.et[:, 4:516:4], T.vv[:], 0.0, None, A.is_equal, None, ["vv", "etz"], ["et"])
-    ts(T.ic[:], T.ib[:], col("s"), None, A.add, None, ["ib", "fs"], ["ic"])
-    close("v")
-    ts(T.mka[:], T.uu[:, 0:128], col("e"), None, A.is_equal, None, ["uu", "fe"], ["mka"])
-    ts(T.lg0[:], T.i0[:], col("g0"), None, A.add, None, ["i0", "fg0"], ["lg0"])
-    ts(T.ke[:], T.kj[:, 0:8], col("c"), None, A.is_equal, None, ["kj", "fc"], ["ke"])
-    close("v")
-    ts(T.ie[:], T.ic[:], -1.0, 1.0 / 3, A.add, A.mult, ["ic"], ["ie"])
-    close("v")
-    for b in range(4):
-        op("v", lambda: V.quantize_mx(T.eq[:, 128 * b:128 * b + 128], T.es[:, 128 * b:128 * b + 128], T.et[:, 4 - b:516 - b]),
-           r=["et"], w=["eq%d" % b])
-        if b == 1:
-            close("v")
-            tt(T.ig[:], T.ic[:], T.ie[:], A.add, ["ic", "ie"], ["ig"])
-            close("v")
-    close("v")
-    ts(T.lb[:], T.ig[:], 2.0, col("h4"), A.mult, A.add, ["ig", "fh4"], ["lb"])
-    close("v")
+    HRZ = ["hrz0", "hrz1", "hrz2"]
 
     def spreader(name, at):
         for t, s in ((0, 32.0), (2, -32.0)):
@@ -332,93 +356,114 @@ def rank_program(g, core, T, topo):
         ts(T.k7[lo:hi, at:at + 2 * n:2], T.kj[lo:hi, first:first + n], T.ff[lo:hi, place[s1]:place[s1] + 1],
            T.ff[lo:hi, place[s2]:place[s2] + 1], A.subtract, A.is_equal, ["kj", "k7z", "f" + s1, "f" + s2] + list(rd), [key])
 
+    ts(T.ic[:], T.ib[:], col("s"), None, A.add, None, ["ib", "fs"], ["ic"])
+    ts(T.ke[:], T.kj[:, 0:8], col("c"), None, A.is_equal, None, ["kj", "fc"], ["ke"])
+    close("v")
+    ts(T.mka[:], T.uu[:, 0:128], col("e"), None, A.is_equal, None, ["uu", "fe"], ["mka"])
+    ts(T.lg0[:], T.i0[:], col("g0"), None, A.add, None, ["i0", "fg0"], ["lg0"])
+    close("v")
+    for a, half, k in ((0, -5.0, 3), (4, -6.0, -5), (8, -5.5, -6)):
+        ts(T.ie[:, a:a + 4], T.ic[:, a:a + 4], half, 1.0 / k, A.add, A.mult, ["ic"], ["ie%d" % abs(k)])
+    close("v")
     spreader("m", 0)
-    hot(64, 128, 32, 16, 0, "a8", "c", "k7a")
-    hot(0, 64, 64, 16, 0, "a", "c2", "k7b")
+    ts(T.mkb[:], T.uu[:, 0:256:8], col("e"), None, A.is_equal, None, ["uu", "fe"], ["mkb0"])
+    close("v")
+    tt(T.ig[:], T.ic[:], T.ie[:], A.add, ["ic", "ie3", "ie4", "ie5", "ie6"], ["ig"])
+    close("v")
+    fields(names[13:16])
+    tt(T.ig[:, 8:12], T.ig[:, 8:12], T.ie[:, 8:12], A.add, ["ig", "ie6"], ["ig"])
+    close("v")
+    fields(names[16:])
+    ts(T.lb[:], T.ig[:], 2.0, col("h4"), A.mult, A.add, ["ig", "fh4"], ["lb"])
+    close("v")
+    hot(64, 128, 48, 16, 0, "a8", "c", "k7a")
+    hot(0, 64, 80, 16, 0, "a", "c2", "k7b")
     close("v")
     act(T.hz[:, 2:32:4], T.ke[:], ["ke", "hzz"], ["hc1"], scale=UNIT)
     for j in range(1, 7):
         t, at = nums_at(j)
-        act(run(t, at + 2 * kh(j), 8, 20), T.ke[:], ["ke"] + HRZ, ["hc%d" % (j + 1)], scale=(j + 1) * UNIT)
+        act(run(t, at + 2 * hp(j) // KH[j + 1], 8, hp(j)), T.ke[:], ["ke"] + HRZ, ["hc%d" % (j + 1)], scale=(j + 1) * UNIT)
     close("a")
-    beta = lambda a, n, s=1: run(T.xa, 65 + 4 * a, n, 4 * s)
-    afill(run(T.xa, 67, 32, 4), 32, 1.0, "xa3", ["xaz"])
-    afill(beta(0, 8), 8, 128.0, "xb0", ["xaz"])
-    afill(beta(8, 8), 8, 192.0, "xb1", ["xaz"])
-    afill(beta(17, 8, 2), 8, 64.0, "xb2", ["xaz"])
-    afill(T.mt[:, 0:192], 192, 0.0, "mtz0")
-    afill(T.mt[:, 704:1024], 320, 0.0, "mtz1")
-    afill(T.mu[:, 0:128], 128, 0.0, "muz")
-    close("a")
-    XB = ["xa3", "xb0", "xb1", "xb2"]
 
     def decode(n, q, s, rd):
         for b in range(4):
             mm(b, n, T.eq[:, 128 * b:128 * b + 128], T.es[:, 128 * b:128 * b + 128], q, s, ["eq%d" % b] + rd)
 
-    def halves(outs):
-        for b in range(4):
-            for name, out, a, n in outs:
-                act(out(b), bank[b][:, a:a + n], ["b%d" % b], ["%s%d" % (name, b)], scale=0.5)
+    def halves(name, outs, bs=range(4)):
+        for b in bs:
+            for k, (t, at, a, n) in enumerate(outs):
+                act(T.dt0[:, :, at, b:16:4] if t is None else run(t, 4 * at + b, n, 4), bank[b][:, a:a + n], ["b%d" % b], ["%s%d%d" % (name, k, b)], scale=0.5)
             close("a")
-        return [["%s%d" % (o[0], b) for b in range(4)] for o in outs]
+        D[name] = ["%s%d%d" % (name, k, b) for k in range(len(outs)) for b in range(4)]
+
+    D = {}
 
     def sums(j, back):
         t, at = sums_at(j)
-        pitch = kp(j) * kp(j + 1)
-        return run(t, at + kp(j) - pitch * back, 8, pitch)
+        return run(t, at + pp(j) // KP[j + 1] * STEPS[KP[j + 1]][1] - pp(j) * back, 8, pp(j))
 
-    def turn(a, n, key):
-        op("v", lambda: V.transpose(run(T.g8, g8_at(a) + 2, 32 * n, 2), T.gb[:, 32 * a:32 * (a + n)]),
-           r=["gb%d" % j for j in range(a, a + n)] + G8Z, w=[key], cut=True)
+    def turn(a, n, sh=0):
+        op("v", lambda: V.transpose(run(T.g8, g8_at(a + sh) + 2, 32 * n, 2), T.gb[:, 32 * a:32 * (a + n)]),
+           r=["gb%d" % j for j in range(a, a + n)] + G8Z + ["g8z3"] * sh, w=["t%d" % (j + sh) for j in range(a, a + n)], cut=True)
         close("v")
 
-    def thin(j, n, rd):
-        act(T.g3[:, 16 * j - 16:16 * j - 16 + 32 * n], T.g8[:, g8_at(j):g8_at(j) + 128 * n - 40].indirect(T.lb[:, 0:2 * n]),
-            rd + ["lb"], ["s%d" % j], cut=True)
+    def thin(j):
+        a, n, wide = {3: (0, 2, 96), 5: (4, 3, 96), 6: (8, 3, 80), 4: (12, 2, 73)}[KP[j]]
+        act(T.g3[:, g3_at[j]:g3_at[j] + 16 * n], T.g8[:, g8_at(j) - 8:g8_at(j) - 8 + wide].indirect(T.lb[:, a:a + n]),
+            ["t%d" % u for u in range(j - 1, j + 1 + (j in (3, 4, 6)))] + ["lb"], ["s%d" % j], cut=True)
         close("a")
 
-    def step(name, k7, n7):
+    def step(name, k7, n7, sh=0):
         kind, j = name[0], int(name[1])
+        u = j + sh
         if kind == "t":
-            turn(3 * j - 1, 3, name)
-            thin(1 + 2 * j, j, ["t1", name])
+            if sh:
+                turn(*((1, 1), (2, 2), (5, 3), (4, 1))[j], sh)
+            else:
+                turn(*((2, 4), (6, 2))[j - 1])
+            for v in (((), (3,), (6, 8), (4, 5)) if sh else ((), (3, 4, 5), (6,)))[j]:
+                thin(v)
         elif kind in "pq":
-            k, n = kp(j), kp(j + 1)
+            k = KP[u]
             if j < 7:
-                t, at = sums_at(j)
-                out = run(t, at + (k if kind == "p" else k * n) - n * (k - 1), 8 * k, n)
+                t, at = sums_at(u)
+                n, far = pp(u) // k, pp(u) // KP[u + 1]
+                there = far * STEPS[KP[u + 1]][1] if kind == "p" else far * STEPS[KP[u + 1]][0] + pp(u)
+                out = run(t, at + there - n * STEPS[k][2], 8 * k, n)
             else:
-                out = T.p7[:]
+                out = T.p7[:, 0:8 * k]
+            if u == 0:
+                d1, rd = T.g8[:, 2:66:2], ["t0"]
+            elif k != 8:
+                d1, rd = T.g3[:, g3_at[u]:g3_at[u] + 8 * k], ["s%d" % u]
+            else:
+                d1, rd = T.g8[:, g8_at(u) + 1:g8_at(u) + 65], ["t%d" % u]
             if j == 0:
-                return scan(out, T.q0[:], T.g8[:, 2:66:2], LOW, A.add, ["t0", "top", "prz0", "prz1", "prz2"], [name])
-            t, at = sums_at(j - 1)
-            if j % 2:
-                d1, rd = T.g3[:, 16 * j - 16:16 * j + 8], ["s%d" % min(j, 5)]
-            else:
-                d1, rd = T.g8[:, g8_at(j) + 1:g8_at(j) + 65], ["t%d" % (1 + j // 5)]
-            scan(out, run(t, at, 8 * k, kp(j - 1)), d1, LOW, A.add, rd + ["p%d" % (j - 1), "q%d" % (j - 1)], [name])
+                return scan(out, T.q0[:, 0:8 * k], d1, LOW, A.add, rd + ["top", "top0", "prz0", "prz1", "prz2", "prz3"], [name])
+            scan(out, run(*sums_at(u - 1), 8 * k, pp(u - 1) // k), d1, LOW, A.add, rd + ["p%d" % (j - 1), "q%d" % (j - 1)], [name])
         elif kind in "dl":
             if j < 7:
-                t, at = sums_at(j)
-                m = run(t, at + kp(j) - kp(j + 1) * (kp(j) - 1), 8, kp(j) * kp(j + 1))
+                t, at = sums_at(u)
+                diagonal, _, done = STEPS[KP[u]]
+                m = run(t, at + pp(u) // KP[u + 1] * STEPS[KP[u + 1]][1] + pp(u) // KP[u] * (diagonal - done), 8, pp(u))
             else:
-                m = T.p7[:, 0:24:3]
+                m = T.p7[:, 0:8 * KP[u]:KP[u]]
             at = 0 if kind == "d" else 2
-            out = run(T.k7, k7 + at, 8, 4) if j == 7 else run(T.km, 40 * j + at, 8, kh(j))
-            tt(out, sums(j - 1, int(kind == "d")), m, A.is_ge if kind == "d" else A.is_gt,
+            out = run(T.k7, k7 + at, 8, KH[7]) if j == 7 else run(T.km, km_at(j) + at, 8, KH[j])
+            tt(out, sums(u - 1, int(kind == "d")), m, A.is_ge if kind == "d" else A.is_gt,
                ["kmz", "k7z", "p%d" % (j - 1), "p%d" % j], ["k" + name], True)
         else:
-            k, n = kh(j), kh(j + 1)
+            k = KH[j]
             rd = HRZ + ["hc%d" % j, "h%d" % (j - 1), "g%d" % (j - 1), "kd%d" % j, "kl%d" % j]
             if j == 7:
-                return scan(run(T.xa, 0, n7, 2), run(T.hr5, 360, n7, 5), T.k7[:, k7:k7 + n7], 0.0, A.subtract,
+                return scan(run(T.xa, 0, n7, 2), run(*nums_at(6), n7, 4), T.k7[:, k7:k7 + n7], 0.0, A.subtract,
                             rd + ["k7a", "k7b", "k7c", "xaz"], [name])
             t, at = nums_at(j)
-            cells = 8 if kind == "h" else 7
-            src = T.hz[:, 0:cells * k] if j == 1 else run(nums_at(j - 1)[0], nums_at(j - 1)[1], cells * k, n)
-            scan(run(t, at + (3 * k if kind == "h" else k + 20) - 3 * n, cells * k, n), src,
-                 T.km[:, 40 * j:40 * j + cells * k], 0.0, A.subtract, rd, [name])
+            n = 7 * k + (left(j) + 1 if kind == "h" else 0)
+            src = T.hz[:, 0:n] if j == 1 else run(*nums_at(j - 1), n, hp(j - 1) // k)
+            there = hp(j) // KH[j + 1] * left(j + 1) if kind == "h" else hp(j) // KH[j + 1] + hp(j)
+            scan(run(t, at + there - hp(j) // k * left(j), n, hp(j) // k), src,
+                 T.km[:, km_at(j):km_at(j) + n], 0.0, A.subtract, rd, [name])
 
     def gather(q, gm, lst, a, n, rd):
         args = (T.gb[:, 32 * a:32 * (a + n)], gm.indirect(lst[:, 2 * a:2 * (a + n)]), rd, ["gb%d" % j for j in range(a, a + n)])
@@ -428,23 +473,38 @@ def rank_program(g, core, T, topo):
             copy(*args, True)
         close(q)
 
+    later = []
+
+    def gap(n):
+        close("v")
+        for fn in later[:n]:
+            fn()
+        del later[:n]
+        close("v")
+
     def first(gm, lst, rd):
         gather("a", gm, lst, 1, 1, rd)
         gather("v", gm, lst, 0, 1, rd)
 
-    def align(k7, n7, slot, w, gm, lst, rd, aside):
-        gather("a", gm, lst, 2, 3, rd)
-        turn(0, 2, "t0")
-        thin(1, 1, ["t0"])
-        gather("a", gm, lst, 5, 3, rd)
-        for name in ORDER:
-            step(name, k7, n7)
-            if name == "t2":
-                aside()
-        act(T.pc[:, slot:slot + 1], T.xa[:, 62:63], ["h7"], ["pc%d" % slot], scale=1.0 / UNIT)
-        close("a")
-        quant(T.xq[:], T.xsc[:], T.xa[:], ["h7"] + XB, ["xq"])
-        mm(5, 128, T.stq[:, w:w + 128], T.sts[:, w:w + 128], T.xq[:], T.xsc[:], ["stq%d" % w, "xq"])
+    def start(gm, lst, rd):
+        gather("a", gm, lst, 2, 4, rd)
+        turn(0, 2)
+        gap(2)
+        thin(1)
+        gather("a", gm, lst, 6, 2, rd)
+
+    def align(k7, n7, slot, at, w, aside, sh=0):
+        for name in ORDER_AHEAD if sh else ORDER:
+            step(name, k7, n7, sh)
+            if name in ("q1", "t2"):
+                aside(name == "t2")
+            if name in ("q1", "h6", "h7"):
+                gap(2)
+        q = T.xq[:, at:at + 128], T.xsc[:, at:at + 128]
+        quant(*q, T.xa[:], ["h7"] + XB, ["xq"])
+        ts(T.pc[:, slot:slot + 1], T.xa[:, 94:95], 1.0 / UNIT, None, A.mult, None, ["h7"], ["pc%d" % slot], True)
+        close("v")
+        mm(5, 128, T.stq[:, w:w + 128], T.sts[:, w:w + 128], *q, ["stq%d" % w, "xq"])
 
     def masked(out, k, a, n, mk, rd, key):
         tt(out, bank[k][:, a:a + n], mk, A.mult, ["b%d" % k] + rd, [key], True)
@@ -456,107 +516,91 @@ def rank_program(g, core, T, topo):
 
     L = ["lin", "qown", "sown"]
     mm(4, 128, *win(256), *win(384), L)
-    decode(256, *win(256, 256), L)
+
+    def decode0(b):
+        e_b = T.eq[:, 128 * b:128 * b + 128], T.es[:, 128 * b:128 * b + 128]
+        quant(*e_b, T.zz[:, 4 - b:516 - b], ["et"], ["eq%d" % b])
+        mm(b, 256, *e_b, *win(256, 256), ["eq%d" % b] + L)
+
     masked(T.gm0[:], 4, 0, 128, T.mka[:], ["mka"], "gm0")
+    decode0(0)
     first(T.gm0[:], T.lg0, ["gm0", "lg0"])
-    quant(T.stq[:, 0:128], T.sts[:, 0:128], T.st[:], ["st0", "st1", "st2", "st3"], ["stq0"])
-    op("s", lambda: g.sync.dma_start(T.wt[:], T.w[:]), r=["lin", "yin"], w=["wt"], dma=True)
+    decode0(1)
+    op("s", lambda: g.sync.dma_start(T.wt[:], T.w[:]), r=["lin"], w=["wt"], dma=True)
     close("s")
-    Y = L + ["yin", "qout", "sout"]
-    mm(6, 128, *win(128 + 64 * b0), *win(128), Y)
-    D = {}
 
-    def aside0():
-        D["a0"], D["b0"], u0, u1 = halves([("da0", lambda b: T.da0[:, b:256:4], 64, 64), ("db0", lambda b: T.db0[:, b:512:4], 128, 128),
-                                           ("dt0", lambda b: T.dt0[:, :, 0, b:16:4], 0, 32), ("dt1", lambda b: T.dt0[:, :, 1, b:16:4], 32, 32)])
-        decode(128, *win(128), Y)
-        act(T.da0[:, 256:512], T.dt0[:], u0 + u1, ["da0u"])
-        close("a")
+    def aside0(second):
+        halves("d0", [(T.db0, 0, 128, 128), (T.da0, 0, 64, 64), (None, 0, 0, 32), (None, 1, 32, 32)], (1, 2, 3) if second else (0,))
+        if second:
+            act(T.da0[:, 256:512], T.dt0[:], D["d0"], ["d0u"])
+            close("a")
+            D["d0"].append("d0u")
 
-    align(0, 96, 0, 0, T.gm0[:], T.lg0, ["gm0", "lg0"], aside0)
-    ay, by = 64 * b0, 64 - 64 * b0
-    for lo, row, f, adds in ((64, T.i1, "g1", (0.0, 48.0)), (0, T.i0, "g0", (16.0, 0.0))):
-        for (a, b), add in zip(((0, 4), (4, 16)), adds):
-            ts(T.lg1[lo:lo + 64, a:b], row[lo:lo + 64, a:b], T.ff[lo:lo + 64, place[f]:place[f] + 1], add, A.add, A.add,
-               ["i0", "i1", "f" + f], ["lg1%d%d" % (lo, a)])
-    for k in range(2):
-        ts(T.mkb[:, 32 * k:32 * k + 32], T.uu[:, 0:256:8], col("e"), None, A.is_equal, None, ["uu", "fe"], ["mkb%d" % k])
-    close("v")
-    if b1:
-        D["by"], u0, u1 = halves([("dby", lambda b: T.dby[:, b:256:4], by, 64), ("dy0", lambda b: T.dty[:, :, 0, b:16:4], ay, 32),
-                                  ("dy1", lambda b: T.dty[:, :, 1, b:16:4], ay + 32, 32)])
-        act(T.day[:], T.dty[:], u0 + u1, ["day"])
-        D["ay"] = ["day"]
-    else:
-        D["by"], D["ay"] = halves([("dby", lambda b: T.dby[:, b:256:4], by, 64), ("day", lambda b: T.day[:, b:256:4], ay, 64)])
-        afill(beta(16, 8), 8, 0.0, "xb2", ["xq"])
-        afill(beta(24, 8), 8, 64.0, "xb3", ["xq"])
-        XB.append("xb3")
-    afill(beta(0, 16), 16, 0.0, "xb0", ["xq", "xb1"])
+    idle = lambda: None
+    later += [lambda: decode0(2), idle, lambda: decode0(3), idle,
+              lambda: quant(T.stq[:, 0:128], T.sts[:, 0:128], T.st[:], ["st0", "st1", "st2", "st3"], ["stq0"]), idle,
+              lambda: ts(T.lg1[:], T.i1[:], col("g1"), None, A.add, None, ["i1", "fg1"], ["lg1"]),
+              lambda: floats(names[13:])]
+    start(T.gm0[:], T.lg0, ["gm0", "lg0"])
+    align(0, 112, 0, 0, 0, aside0)
+    send_numbers(c2, rest, 16, 128, "arrj", "pin")
+    afill(beta(0, 16), 16, 0.0, "xb0", ["xq"])
     close("a")
-    masked(T.gm1[:, 16:80], 6, by, 64, T.mka[:, 0:64], ["mka"], "gmy")
-    ts(T.o0[:], bank[5][:, 16:48], col("m32"), col("e"), A.add, A.add, ["b5", "fm32", "fe"], ["o0"], True)
+    ts(T.lg2[:], T.kj[:, 0:16], 2.0, col("u"), A.mult, A.add, ["kj", "fu"], ["lg2"])
+    ts(run(T.k7, 160, 8, 2), T.kj[:, 8 * at2:8 * at2 + 8], col("q"), None, A.is_equal, None, ["kj", "fq", "k7z"], ["k7c"])
     close("v")
-    if not b1:
-        hot(0, 64, 64, 16, 0, "a8", "c", "k7b")
+    spreader("e", 128)
+    ts(T.o0[:], bank[5][:, 24:56], col("m32"), col("e"), A.add, A.add, ["b5", "fm32", "fe"], ["o0"], True)
     close("v")
-    blend(T.mt[:, 192:512], T.db0[:], T.o0[:, 0:20], T.da0[:, 0:320], D["a0"] + D["b0"] + ["da0u", "o0"], ["mt1"])
-    blend(T.mt[:, 512:704], T.db0[:], T.o0[:, 20:32], T.da0[:, 320:512], D["b0"] + ["da0u", "o0"], ["mt2"])
+    blend(T.mt[:, 192:512], T.db0[:], T.o0[:, 0:20], T.da0[:, 0:320], D["d0"] + ["o0"], ["mt1"])
+    blend(T.mt[:, 576:704], T.db0[:], T.o0[:, 20:28], T.da0[:, 320:448], D["d0"] + ["o0"], ["mt2"])
     quant(*win(512), T.mt[:, 0:512], ["mtz0", "mt1"], ["m01"])
-    quant(*win(640), T.mt[:, 512:1024], ["mtz1", "mt2"], ["m02"])
-    fields(names[13:])
+    blend(T.mt[:, 512:576], T.db0[:], T.o0[:, 28:32], T.da0[:, 448:512], D["d0"] + ["o0"], ["mt3"])
+    quant(*win(640), T.mt[:, 576:1088], ["mtz1", "mt2"], ["m0a"])
     own = 64 * (1 - b1)
     store("s", T.pf[0:1, 128:192], T.pc[own:own + 64, 0:1], ["pc0"], ["pf0"])
     close("s")
 
     mm(4, 128, *win(496), *win(512), L + ["m01"])
-    mm(7, 128, *win(496), *win(640), L + ["m01", "m02"])
-    decode(128, *win(560), ["m01", "m02"])
+    mm(7, 128, *win(496), *win(544), L + ["m01", "m0a"])
     masked(T.gm1[:, 0:16], 4, 112, 16, T.mkb[:, 0:16], ["mkb0"], "gm1")
-    floats(names[13:])
-    masked(T.gm1[:, 80:128], 7, 0, 48, T.mkb[:, 0:48], ["mkb0", "mkb1"], "gm1b")
-    first(T.gm1[:, 0:80], T.lg1, ["gm1", "gmy", "lg1640", "lg100"])
+    quant(*win(672), T.mt[:, 512:1024], ["mtz1", "mt2", "mt3", "m0a"], ["m02"])
+    send(c4, e8, T.lq, T.ls, 592, 800, 96, "arr1", ["m01", "m02"], "fin")
+    send(c2, rest, T.lq, T.ls, 624 - 64 * b1, 896, 64, "arry", ["m01", "m02"], "yin")
+    mm(6, 128, *win(496), *win(672), L + ["m01", "m02"])
+    decode(128, *win(560), ["m01", "m02"])
+    first(T.gm1[:, 0:16], T.lg1, ["gm1", "lg1"])
+    masked(T.gm1[:, 16:48], 7, 96, 32, T.mkb[:], ["mkb0"], "gm1b")
 
-    def aside1():
-        D["a1"], D["b1"] = halves([("da1", lambda b: T.da1[:, b:256:4], 0, 64), ("db1", lambda b: T.db1[:, b:256:4], 64, 64)])
+    def aside1(second):
+        halves("d1", [(T.d1, 0, 0, 32), (T.d1, 32, 64, 64)], (2, 3) if second else (0, 1))
+        if second:
+            mm(6, 128, T.eq[:, 256:384], T.es[:, 256:384], T.xq[:, 8:136], T.xsc[:, 8:136], ["eq2", "xq", "pin"])
+            act(T.pc[:, 2:3], bank[6][:, 127:128], ["b6"], ["pc2"], scale=1.0 / UNIT)
+            close("a")
+            store("s", T.pf[0:1, 0:64], T.pc[own:own + 64, 2:3], ["pc2"], ["pf2"])
+            close("s")
+            decode(128, *win(768), ["m02", "fin"])
+            halves("df", [(T.df, 0, 32, 96)])
 
-    align(0, 96, 4, 0, T.gm1[:, 16:128], T.lg1, ["gm1b", "gmy", "lg1644", "lg104"], aside1)
+    later += [lambda: ts(T.ly[:, 0:8], T.iy[:], col("y0"), col("y1"), A.add, A.add, ["iy", "fy0", "fy1"], ["ly0"]),
+              lambda: ts(T.ly[:, 8:12], T.kj[:, 0:4], col("s4"), 128.0, A.add, A.add, ["kj", "fs4"], ["ly1"]),
+              lambda: ts(T.ld[:], T.id[:], col("i16"), col("e"), A.add, A.add, ["id", "fi16", "fe"], ["ld"]),
+              idle, lambda: quant(T.stq[:, 128:256], T.sts[:, 128:256], T.st[:], ["st0", "st1", "st2", "st3"], ["stq128"])]
+    gather("a", T.gm1[:, 0:48], T.lg1, 3, 3, ["gm1", "gm1b", "lg1"])
+    turn(0, 2)
+    gather("v", T.gm1[:, 0:48], T.lg1, 2, 1, ["gm1", "gm1b", "lg1"])
+    masked(T.gm1[:, 48:64], 6, 0, 16, T.mkb[:, 0:16], ["mkb0"], "gm1c")
+    thin(1)
+    gather("a", T.gm1[:], T.lg1, 6, 2, ["gm1", "gm1b", "gm1c", "lg1"])
+    align(0, 80, 4, 160, 0, aside1)
+    send_numbers(c4, e8, 192, 288, "arr2", "jin")
+    quant(T.wq[:], T.ws[:], T.wt[:], ["wt"], ["wq"])
     act(beta(0, 8), T.uu[:, 0:32:4], ["uu", "xq"], ["xb0"], scale=0.5)
     close("a")
-    quant(T.wq[:], T.ws[:], T.wt[:], ["wt"], ["wq"])
-    ts(T.lg2[:], T.kj[:, 0:16], 2.0, col("g1"), A.mult, A.add, ["kj", "fg1"], ["lg2"])
-    ts(run(T.k7, 128, 8, 2), T.kj[:, 8 * at2:8 * at2 + 8], col("q"), None, A.is_equal, None, ["kj", "fq", "k7z"], ["k7c"])
-    fill(T.gm2[:], 0.0, "gm2")
-    close("v")
-    ts(T.o1[:], bank[5][:, 16:32], 8.0, col("s"), A.mult, A.add, ["b5", "fs"], ["o1"], True)
-    close("v")
-    ts(T.oy[:], bank[5][:, 32:48], col("m32"), col("e"), A.add, A.add, ["b5", "fm32", "fe"], ["oy"], True)
-    close("v")
-
-    def blend1(out, a, wr):
-        blend(out, T.db1[:, 16 * a:256], T.o1[:, 8 * a:8 * a + 8], T.da1[:, 128 * a:128 * a + 128], D["a1"] + D["b1"] + ["o1"], wr)
-
-    blend1(T.mt[:, 0:128], 1 - b2, ["mtz0"])
-    blend1(T.mu[:, 384:512], b2, ["mu0"])
-    quant(T.m1q[:], T.m1s[:], T.mt[:, 0:512], ["mtz0", "mt1"], ["m1"])
-    need("g", ["m1"])
-    e8 = topo.engines(core, c4)
-    rid, pid = int(topo.addr(c4)[0]), int(topo.addr(c4)[1])
-    g.remote_dma(T.hq[:, 128:160].bitcast(dt.uint8), T.m1q[:, 0:32].bitcast(dt.uint8), T.sem.arr2, T.sem.sent, pid, rid, mask_of(e8))
-    g.remote_dma(T.hs[:, 128:160], T.m1s[:, 0:32], T.sem.arr2, T.sem.sent, pid, rid, mask_of(e8))
-    sent += 2 * len(e8)
-    landed("hin", "arr2", 2 * len(e8))
-
-    blend(T.mu[:, 128:384], T.dby[:], T.oy[:], T.day[:], D["ay"] + D["by"] + ["oy"], ["mu1"])
-    spreader("e", 128)
-    quant(T.hq[:, 0:128], T.hs[:, 0:128], T.mu[:], ["mu0", "mu1", "muz"], ["hown"])
-    quant(T.stq[:, 128:256], T.sts[:, 128:256], T.st[:], ["st0", "st1", "st2", "st3"], ["stq128"])
-    if b1:
-        ts(T.ly[:, 0:8], T.iy[:], col("y0"), None, A.add, None, ["iy", "fy0"], ["ly0"])
-    else:
-        ts(T.ly[:, 0:8], T.iy[:], col("y0"), col("y1"), A.add, A.add, ["iy", "fy0", "fy1"], ["ly0"])
-    ts(T.ly[:, 8:12], T.kj[:, 0:4], col("s4"), 128.0, A.add, A.add, ["kj", "fs4"], ["ly1"])
-    ts(T.ld[:], T.id[:], col("i16"), col("e"), A.add, A.add, ["id", "fi16", "fe"], ["ld"])
+    if b2:
+        quant(T.dq[:], T.ds[:], T.mt[:, 512:1024], ["mt2", "mt3", "mtz1"], ["dq", "dq0"])
+    ts(T.o1[:], bank[5][:, 24:32], 8.0, col("s"), A.mult, A.add, ["b5", "fs"], ["o1"], True)
     close("v")
 
     def prod(k, q, s, rd):
@@ -568,57 +612,106 @@ def rank_program(g, core, T, topo):
             act(T.ys[:, 192 * o + at:192 * o + at + n], bank[k + o][:, a:a + n], ["b%d" % (k + o)], ["ys%s%d" % (key, o)])
             close("a")
 
-    prod(0, *win(560), ["m01", "m02"])
-    prod(2, T.m1q[:], T.m1s[:], ["m1"])
-    stage(0, 64 * b1, 64, 64 * b1, "a")
-    stage(2, 0, 32, 160 - 32 * b2, "b")
+    def spread8():
+        lst = T.lg2[:, 0:4]
+        copy(T.dq[:, 0:64].bitcast(dt.uint32), T.hq[:, 96:128].bitcast(dt.uint32).indirect(lst), ["hk", "lg2"], ["dq"], True)
+        close("v")
+        act(T.ds[:, 0:64], T.hs[:, 96:128].indirect(lst), ["hk", "lg2", "dq0"], ["ds"], cut=True)
+        close("a")
 
-    H = ["hin", "hown"]
-    mm(4, 128, T.hq[:, 32:160], T.hs[:, 32:160], T.hq[:, 32:160], T.hs[:, 32:160], H)
-    prod(6, T.hq[:, 0:128], T.hs[:, 0:128], ["hown"])
-    decode(128, T.hq[:, 32:160], T.hs[:, 32:160], H)
-    masked(T.gm2[:, 4 * (at2 & 1):4 * (at2 & 1) + 32], 4, 32 * bt2, 32, T.mkb[:, 0:32], ["mkb0"], "gm2")
-    first(T.gm2[:], T.lg2, ["gm2", "lg2"])
-    store("s", T.pf[0:1, 0:128], T.pc[:, 4:5], ["pc4", "hin"], ["pf1"])
+    K, F = (T.hq[:, 0:128], T.hs[:, 0:128]), (T.hq[:, 128:256], T.hs[:, 128:256])
+    prod(0, *win(560), ["m01", "m02"])
+    prod(2, *win(832), ["fin", "yin"])
+    stage(0, 64 * b1, 64, 64 * b1, "a")
+    for out, key in ((T.mt[:, 0:16], "mtf"),) + (() if b2 else ((T.mu[:, 256:272], "mu1"),)):
+        tt(out, T.df[:, 144:160], T.df[:, 0:16], A.add, D["df"] + ["muz", "mtz0"], [key], True)
+    close("v")
+    blend(T.mu[:, 384:512], T.d1[:, 128:384], T.o1[:], T.d1[:, 0:128], D["d1"] + ["o1"], ["mu0"])
+    quant(*K, T.mu[:], ["muz", "mu0", "mu1"], ["hk"])
+    mm(6, 128, T.stq[:, 0:128], T.sts[:, 0:128], T.xq[:, 168:296], T.xsc[:, 168:296], ["stq0", "xq", "jin"])
+    if not b2:
+        mm(7, 128, *K, *K, ["hk"])
+    ts(T.of[:, 0:7], bank[6][:, 121:128], 8.0, col("s"), A.mult, A.add, ["b6", "fs"], ["of"], True)
+    close("v")
+    if b2:
+        spread8()
+    blend(T.mt[:, 16:128], T.df[:, 144:384], T.of[:, 0:7], T.df[:, 16:128], D["df"] + ["of"], ["mtz0"])
+    if not b2:
+        masked(T.gm2[:, 32:40], 7, 64, 8, T.mkb[:, 0:8], ["mkb0"], "gme")
+        gather("a", T.gm2[:, 32:40], T.lg2, 0, 1, ["gme", "lg2"])
+    stage(2, 64, 64, 64 - 64 * b1, "c")
+    quant(*F, T.mt[:, 0:512], ["mtz0", "mtf", "mt1"], ["hf"])
+    send(c4, e8, T.hq, T.hs, 128, 256, 32, "arr3", ["hf"], "bin")
+    if not b2:
+        turn(0, 1, 1)
+        thin(1)
+
+    H = ["hk", "hf"]
+    if b2:
+        mm(4, 128, *F, T.dq[:], T.ds[:], ["hf", "dq", "ds"])
+        mm(7, 128, *F, *K, H)
+    else:
+        mm(4, 128, *K, *F, H)
+    decode(128, T.hq[:, 96:224], T.hs[:, 96:224], H)
+    if b2:
+        tt(T.gb[:, 0:64], bank[4][:, 0:64], T.mka[:, 0:64], A.mult, ["b4", "mka"], ["gb0", "gb1"], True)
+        close("v")
+        masked(T.gm2[:, 0:32], 7, 96, 32, T.mkb[:, 0:32], ["mkb0"], "gm2")
+        turn(0, 2)
+        gather("a", T.gm2[:, 0:32], T.lg2, 4, 2, ["gm2", "lg2"])
+        gather("v", T.gm2[:, 0:32], T.lg2, 2, 2, ["gm2", "lg2"])
+        thin(1)
+        gather("a", T.gm2[:, 0:32], T.lg2, 6, 2, ["gm2", "lg2"])
+    else:
+        masked(T.gm2[:, 0:32], 4, 0, 32, T.mkb[:, 0:32], ["mkb0"], "gm2")
+        for q, a, n in (("a", 2, 2), ("v", 1, 1), ("a", 4, 1), ("a", 5, 3)):
+            gather(q, T.gm2[:, 0:32], T.lg2, a, n, ["gm2", "lg2"])
+        step("p0", 0, 0, 1)
+        step("q0", 0, 0, 1)
+    prod(5, *K, ["hk"])
+    store("s", T.pf[0:1, 64:128], T.pc[64:128, 4:5], ["pc4", "jin"], ["pf1"])
     close("s")
 
-    def aside2():
-        D["a2"], D["b2"] = halves([("da2", lambda b: T.da2[:, b:128:4], 32 * at2, 32), ("db2", lambda b: T.db2[:, b:128:4], 32 * bt2, 32)])
-        stage(6, 32, 64, 64 - 64 * b1, "c")
-        stage(6, 96, 32, 128 + 32 * b2, "d")
-        act(T.dc2[:], T.da2[:].indirect(T.ld[:]), D["a2"] + ["ld"], ["dc2"])
+    def aside2(second):
+        if not second:
+            halves("d2", [(T.d2, 0, 0, 64)])
+            return
+        stage(5, 96, 32, 128 + 32 * b2, "d")
+        prod(0, T.hq[:, 160:288], T.hs[:, 160:288], ["hf", "bin"])
+        act(T.dc2[:], T.d2[:, 128 * b2:128 * b2 + 128].indirect(T.ld[:]), D["d2"] + ["ld"], ["dc2"])
         close("a")
+        stage(0, 96, 32, 160 - 32 * b2, "b")
         for o in range(2):
             act(T.ya[:, 192 * o:192 * o + 192], T.ys[:, 192 * o:192 * o + 192].indirect(T.ly[:]),
                 ["ys%s%d" % (u, o) for u in "abcd"] + ["ly0", "ly1"], ["ya%d" % o])
             close("a")
             store("s", T.y[:, 224 * o:224 * o + 192], T.ya[:, 192 * o:192 * o + 192], ["ya%d" % o])
         close("s")
-        for a in range(2):
-            act(T.pa[0:1, :, a, b1, :], T.pf[0:1, 128 + 32 * a:160 + 32 * a], ["pf0"], ["pa0%d" % a])
-            act(T.pa[0:1, :, a, 1 - b1, :], T.pf[0:1, 32 * a:32 * a + 32], ["pf1"], ["pa1%d" % a])
-            act(T.pb[0:1, :, a, :], T.pf[0:1, 64 + 32 * a:96 + 32 * a], ["pf1"], ["pb%d" % a])
-        close("a")
-        store("s", T.pt[0:1, 0:128], T.pa[0:1, :, :, :, :], ["pa00", "pa01", "pa10", "pa11"])
-        store("s", T.pt[0:1, 128:192], T.pb[0:1, :, :, :], ["pb0", "pb1"])
-        close("s")
 
-    align(96, 48, 8, 128, T.gm2[:], T.lg2, ["gm2", "lg2"], aside2)
-    store("a", T.pt[0:1, 192:224], T.pc[32 * at2:32 * at2 + 32, 8:9], ["pc8"])
-    close("a")
-    ts(T.o2[:], bank[5][:, 16:24], 4.0, col("e"), A.mult, A.add, ["b5", "fe"], ["o2"], True)
+    align(112, 64, 8, 320, 128, aside2, 1 - b2)
+    store("s", T.pt[0:1, 192:224], T.pc[32 * at2:32 * at2 + 32, 8:9], ["pc8"])
+    close("s")
+    for a in range(2):
+        copy(T.pa[0:1, :, a ^ b2, b1, :], T.pf[0:1, 128 + 32 * a:160 + 32 * a], ["pf0"], ["pa0%d" % a])
+        copy(T.pa[0:1, :, a ^ b2, 1 - b1, :], T.pf[0:1, 32 * a:32 * a + 32], ["pf2"], ["pa1%d" % a])
+        copy(T.pb[0:1, :, a ^ b2, :], T.pf[0:1, 64 + 32 * a:96 + 32 * a], ["pf1"], ["pb%d" % a])
     close("v")
-    blend(T.mt[:, 0:128], T.db2[:], T.o2[:], T.dc2[:], D["b2"] + ["dc2", "o2"], ["mtz0"])
+    store("s", T.pt[0:1, 0:128], T.pa[0:1, :, :, :, :], ["pa00", "pa01", "pa10", "pa11"])
+    store("s", T.pt[0:1, 128:192], T.pb[0:1, :, :, :], ["pb0", "pb1"])
+    close("s")
+    ts(T.o2[:], bank[5][:, 24:32], 4.0, col("e"), A.mult, A.add, ["b5", "fe"], ["o2"], True)
+    close("v")
+    blend(T.mt[:, 0:128], T.d2[:, 128 - 128 * b2:256 - 128 * b2], T.o2[:], T.dc2[:], D["d2"] + ["dc2", "o2"], ["mtz0", "mtf"])
     quant(T.m2q[:], T.m2s[:], T.mt[:, 0:512], ["mtz0", "mt1"], ["m2"])
     prod(6, T.m2q[:], T.m2s[:], ["m2"])
     store("s", T.oc[:, 0:128], T.m2q[:, 0:32].bitcast(dt.uint8), ["m2"])
     for k in range(4):
         store("sa"[k % 2], T.osc[4 * k:4 * k + 4, 0:32], T.m2s[32 * k:32 * k + 4, 0:32], ["m2"])
-    copy(T.y2[:, 0:32], bank[6][:, 0:32], ["b6"], ["y20"])
-    close("v")
-    act(T.y2[:, 32:64], bank[7][:, 0:32], ["b7"], ["y21"])
+    act(T.y2[:, 0:32], bank[6][:, 0:32], ["b6"], ["y20"])
     close("a")
-    store("s", T.y[:, 192:224], T.y2[:, 0:32], ["y20"])
-    store("a", T.y[:, 416:448], T.y2[:, 32:64], ["y21"])
-    g.wait_ge(T.sem.sent, sent)
+    copy(T.y2[:, 32:64], bank[7][:, 0:32], ["b7"], ["y21"])
+    close("v")
+    store("a", T.y[:, 192:224], T.y2[:, 0:32], ["y20"])
+    store("s", T.y[:, 416:448], T.y2[:, 32:64], ["y21"])
+    g.wait_ge(T.sem.sent, sent[0])
     finish("s")

import math
from concourse.bass import DstId, RemoteDMATransfer
from concourse.mybir import dt, AluOpType, ActivationFunctionType

F32, BF, I32, U16, X4, U8 = "float32", "bfloat16", "int32", "uint16", "float8_e4m3fn_x4", "uint8"
LOW = -1.0e29
UNIT = 0.125
ORDER = ("p0 q0 t1 p1 q1 d1 p2 q2 l1 t2 d2 p3 q3 h1 g1 l2 d3 p4 l3 h2 g2 p5 q5 d4 l4 h3 d5 p6 q6 l5 h4 g4 "
         "p7 l6 d6 h5 g5 d7 l7 h6 h7").split()
ORDER_AHEAD = ("t0 t1 t3 p1 q1 t2 d1 l1 p2 q2 h1 g1 p3 d2 l2 p4 q4 l3 h2 g2 d3 p5 q5 d4 l4 h3 d5 p6 q6 l5 h4 g4 "
               "p7 l6 d6 h5 g5 d7 l7 h6 h7").split()


def _sb(shape, d):
    return ("sbuf", [128] + list(shape), d)


SCRATCH = {
    "xs": _sb([1024], BF), "wt": _sb([1024], BF), "rq": _sb([256], X4), "rs": _sb([256], U8),
    "lq": _sb([960], X4), "ls": _sb([960], U8), "wq": _sb([256], X4), "ws": _sb([256], U8),
    "eq": _sb([512], X4), "es": _sb([512], U8),
    "st": _sb([512], BF), "stq": _sb([256], X4), "sts": _sb([256], U8),
    "pi": _sb([2], I32), "fi": _sb([24], I32), "ff": _sb([24], F32),
    "uu": _sb([256], BF), "zz": _sb([608], BF),
    "ip": _sb([16], F32), "i0": _sb([16], F32), "i1": _sb([16], F32), "ib": _sb([16], F32), "iy": _sb([8], F32),
    "id": _sb([8], F32), "kj": _sb([32], F32), "ke": _sb([8], F32), "cx": _sb([2], F32),
    "mka": _sb([128], F32), "mkb": _sb([32], F32),
    "lp": _sb([16], U16), "lg0": _sb([16], U16), "lg1": _sb([16], U16), "lg2": _sb([16], U16), "lb": _sb([16], U16),
    "ly": _sb([12], U16), "ld": _sb([8], U16),
    "gm0": _sb([128], F32), "gm1": _sb([64], F32), "gm2": _sb([40], F32), "gb": _sb([256], F32),
    "g8": _sb([624], F32), "g3": _sb([224], F32), "ic": _sb([16], F32), "ie": _sb([16], I32), "ig": _sb([16], F32),
    "q0": _sb([32], F32), "pr3": _sb([534], F32), "pr4": _sb([224], F32), "pr5": _sb([280], F32), "pr8": _sb([576], F32),
    "p7": _sb([64], F32), "km": _sb([288], F32), "k7": _sb([176], F32), "hz": _sb([32], F32),
    "hr4": _sb([812], F32), "hr5": _sb([670], F32), "hr6": _sb([246], F32),
    "xa": _sb([512], BF), "xq": _sb([448], X4), "xsc": _sb([448], U8),
    "o0": _sb([32], U16), "o1": _sb([8], U16), "of": _sb([8], U16), "o2": _sb([8], U16),
    "da0": _sb([512], F32), "db0": _sb([512], F32), "dt0": _sb([8, 2, 16], F32),
    "d1": _sb([384], F32), "df": _sb([384], F32), "d2": _sb([256], F32), "dc2": _sb([128], F32),
    "mt": _sb([1088], BF), "mu": _sb([512], BF),
    "hq": _sb([288], X4), "hs": _sb([288], U8), "dq": _sb([128], X4), "ds": _sb([128], U8),
    "m2q": _sb([128], X4), "m2s": _sb([128], U8),
    "ys": _sb([384], F32), "ya": _sb([384], F32), "y2": _sb([64], F32),
    "pc": _sb([12], F32), "pf": _sb([192], F32), "pa": _sb([4, 2, 2, 8], F32), "pb": _sb([4, 2, 8], F32),
}
for _k in range(8):
    SCRATCH["b%d" % _k] = ("psum", [128, 512], F32)
NPOOL = 140
SEMAPHORES = ["arr0", "arrj", "arry", "arr1", "arr2", "arr3", "sent"] + ["s%d" % _k for _k in range(NPOOL)]


def make_order(g, T):
    Q = {"v": g.vector, "a": g.scalar, "t": g.tensor, "g": g, "s": g.sync}
    known = {k: set() for k in Q}
    st = {"next": 0}
    free, total, batches, opened, wrote, read = {}, {}, [], {}, {}, {}

    def wait(q, b):
        if b in known[q]:
            return
        B = batches[b]
        if opened.get(B["own"]) == b:
            del opened[B["own"]]
        Q[q].wait_ge(T.sem[B["sem"]], B["val"])
        B["waited"] = True
        known[q].add(b)
        known[q].update(B["known"])

    def new_sem(own):
        for b in free.setdefault(own, []):
            if b in known[own[0]]:
                free[own].remove(b)
                return batches[b]["sem"]
        st["next"] += 1
        assert st["next"] <= NPOOL
        return "s%d" % (st["next"] - 1)

    def op(q, fn, r=(), w=(), dma=False, cut=False):
        deps = set()
        for k in list(r) + list(w):
            if k in wrote:
                deps.add(wrote[k])
        for k in w:
            deps.update(read.get(k, ()))
        for k in r:
            if k[0] == "b" and len(k) == 2:
                deps.update(b for b in read.get(k, ()) if batches[b]["own"][0] != q)
        for b in sorted(deps, reverse=True):
            wait(q, b)
        own = (q, dma)
        if cut and own in opened:
            del opened[own]
        if own not in opened:
            sem = new_sem(own)
            batches.append({"own": own, "sem": sem, "val": total.get(sem, 0), "known": set(), "waited": False})
            opened[own] = len(batches) - 1
            free[own].append(opened[own])
        b = opened[own]
        B = batches[b]
        n = 16 if dma else 1
        fn().then_inc(T.sem[B["sem"]], n)
        B["val"] += n
        total[B["sem"]] = B["val"]
        B["known"].update(known[q])
        for k in r:
            read.setdefault(k, set()).add(b)
        for k in w:
            wrote[k] = b
            read[k] = set()

    def need(q, keys):
        for k in keys:
            wait(q, wrote[k])

    def landed(key, sem, val):
        batches.append({"own": None, "sem": sem, "val": val, "known": set(), "waited": False})
        wrote[key] = len(batches) - 1

    def close(q):
        for dma in (False, True):
            opened.pop((q, dma), None)

    def finish(q):
        for b in range(len(batches)):
            if not batches[b]["waited"]:
                wait(q, b)

    return op, need, landed, close, finish


def rank_program(g, core, T, topo):
    r = T.rank_of(core)
    if r is None:
        return
    op, need, landed, close, finish = make_order(g, T)
    A, ACT = AluOpType, ActivationFunctionType
    V, S, PE = g.vector, g.scalar, g.tensor
    b0, b1, b2 = r & 1, (r >> 1) & 1, (r >> 2) & 1
    bank = [T["b%d" % k] for k in range(8)]

    def mask_of(e):
        return sum(1 << k for k in e)

    def dst_id(c):
        a = topo.addr(c)
        return DstId(rid=int(a[0]), pnc=int(a[1]))

    def iota(out, pat, base, cm, key, small=True):
        if small:
            op("g", lambda: g.iota(out, pat, base, cm, allow_small_or_imprecise_dtypes=True), w=[key])
        else:
            op("g", lambda: g.iota(out, pat, base, cm), w=[key])
        close("g")

    def fill(out, val, key, rd=()):
        op("v", lambda: V.memset(out, val), r=rd, w=[key])

    def ts(out, in0, s1, s2, o0, o1, rd, wr, cut=False):
        if o1 is None:
            op("v", lambda: V.tensor_scalar(out, in0, s1, None, o0), r=rd, w=wr, cut=cut)
        else:
            op("v", lambda: V.tensor_scalar(out, in0, s1, s2, o0, o1), r=rd, w=wr, cut=cut)

    def tt(out, in0, in1, o, rd, wr, cut=False):
        op("v", lambda: V.tensor_tensor(out, in0, in1, o), r=rd, w=wr, cut=cut)

    def scan(out, d0, d1, init, o1, rd, wr):
        op("v", lambda: V.tensor_tensor_scan(out, d0, d1, init, A.max, o1), r=rd, w=wr, cut=True)

    def copy(out, in_, rd, wr, cut=False):
        op("v", lambda: V.tensor_copy(out, in_), r=rd, w=wr, cut=cut)

    def act(out, in_, rd, wr, scale=None, bias=None, cut=False):
        if scale is None:
            op("a", lambda: S.activation(out, in_, ACT.Copy), r=rd, w=wr, cut=cut)
        elif bias is None:
            op("a", lambda: S.activation(out, in_, ACT.Copy, scale=scale), r=rd, w=wr, cut=cut)
        else:
            op("a", lambda: S.activation(out, in_, ACT.Identity, bias=bias, scale=scale), r=rd, w=wr, cut=cut)

    def afill(out, n, val, key, rd=(), rows=128):
        act(out, T.zz[0:rows, 1:2 * n:2], ["zz"] + list(rd), [key], scale=0.0, bias=val)

    def quant(q, s, tile, rd, wr):
        op("v", lambda: V.quantize_mx(q, s, tile), r=rd, w=wr, cut=True)
        close("v")

    def mm(k, n, lq, ls, rq, rs, rd):
        op("t", lambda: PE.matmul_mx(bank[k][:, 0:n], lq, ls, rq, rs, True, True), r=rd, w=["b%d" % k], cut=True)

    def store(q, out, in_, rd, wr=()):
        eng = {"s": g.sync, "a": S}[q]
        op(q, lambda: eng.dma_start(out, in_), r=rd, w=wr, dma=True)

    def run(t, a, n, s):
        return t[:, a:a + s * (n - 1) + 1:s]

    def win(a, n=128):
        return T.lq[:, a:a + n], T.ls[:, a:a + n]

    for h in range(2):
        store("s", T.xs[:, 512 * h:512 * h + 512], T.x[:, 512 * h:512 * h + 512], [], ["xs%d" % h])
        close("s")

    FIELDS = {"pk0": (3, 64) if b0 else (0, 192), "pk1": (6, 7) if b0 else (8, 3),
              "e": (6, 3), "c": (6, 7), "s": (6, 15), "m": (9, 3), "a8": (8, 8), "a": (11, 1), "c2": (5, 14),
              "g0": (6, 104), "g1": (9, 5), "m32": (3, 96), "h4": (8, 4), "q": (8, 31), "u": (9, 1),
              "s4": (4, 60), "i16": (4, 48), "y0": (3, 120 if b1 else 64), "y1": (4, 0 if b1 else 28)}
    place = {n: k for k, n in enumerate(FIELDS)}
    col = lambda n: T.ff[:, place[n]:place[n] + 1]

    def fields(names):
        for n in names:
            ts(T.fi[:, place[n]:place[n] + 1], T.pi[:, 0:1], FIELDS[n][0], FIELDS[n][1], A.logical_shift_right, A.bitwise_and,
               ["pi"], ["fi" + n])
        close("v")

    def floats(names):
        a, b = place[names[0]], place[names[-1]] + 1
        copy(T.ff[:, a:b], T.fi[:, a:b], ["fi" + n for n in names], ["f" + n for n in names], True)
        close("v")

    names = list(FIELDS)
    c = r % 4
    iota(T.pi[:, 0:1], [[0, 1]], 0, 64, "pi", small=False)
    for k, (u, v) in enumerate(((c, c ^ 1), (c ^ 3, c ^ 2))):
        iota(T.ip[:, 8 * k:8 * k + 8], [[8 * (v - u), 2], [32 - 64 * b2, 2], [128 if b0 else 4, 2]], 8 * u + 32 * b2, 0, "ip%d" % k)
    iota(T.kj[:], [[1, 32]], 0, 0, "kj")
    iota(T.i0[:], [[1, 8], [16, 2]], 0, 0, "i0")
    iota(T.ib[:], [[-1, 2], [0, 2], [16, 4]], 4, 0, "ib")
    iota(T.ie[:, 12:16], [[0, 4]], 0, 0, "ie4", small=False)
    iota(T.uu[:], [[0, 8], [1, 4], [0, 8]], 0, 0, "uu")
    fill(T.zz[:], 0.0, "zz")
    close("v")
    fields(names[:2])
    fields(names[2:7])
    floats(names[:2])
    fields(names[7:13])
    ts(T.lp[:], T.ip[:], col("pk0"), col("pk1"), A.add, A.add, ["ip0", "ip1", "fpk0", "fpk1"], ["lp"])
    close("v")
    floats(names[2:13])

    KP = [4, 3, 8, 5, 6, 4, 3, 8, 3]
    STEPS = {3: (0, 1, 2), 4: (0, 2, 3), 5: (0, 1, 2), 6: (1, 2, 3), 8: (0, 1, 7)}
    pp = lambda j: math.lcm(KP[j], KP[j + 1])
    KH = [0, 4, 5, 8, 6, 5, 8, 6]
    hp = lambda j: math.lcm(KH[j], KH[j + 1])
    left = lambda j: 4 if KH[j] == 6 else 3
    km_at = lambda j: 8 * sum(KH[:j])
    sums_at = lambda j: [(T.pr4, 8), (T.pr3, 21), (T.pr8, 32), (T.pr5, 20), (T.pr3, 222), (T.pr4, 116), (T.pr3, 339), (T.pr8, 376)][j]
    nums_at = lambda j: [(T.hr4, 4), (T.hr5, 10), (T.hr4, 164), (T.hr6, 6), (T.hr5, 340), (T.hr4, 364)][j - 1]
    g8_at = lambda j: 64 * j + (24 if j > 1 else 0)
    g3_at = {1: 0, 3: 32, 4: 80, 5: 128, 6: 160, 8: 192}
    G8Z = ["g8z0", "g8z1"]
    afill(T.q0[:, 1:32], 31, LOW, "top0")
    afill(T.q0[:, 0:1], 1, 0.0, "top")
    afill(T.pr4[:, 0:224:4], 56, LOW, "prz0")
    afill(T.pr3[:, 0:534:3], 178, LOW, "prz1")
    afill(T.pr8[:, 0:576:8], 72, LOW, "prz2")
    afill(T.pr5[:, 0:280:5], 56, LOW, "prz3")
    afill(T.g8[:, 1:568:2], 284, 0.0, "g8z0")
    afill(T.g8[:, 130:154:2], 12, 0.0, "g8z1")
    close("a")

    for h in range(2):
        quant(T.rq[:, 128 * h:128 * h + 128], T.rs[:, 128 * h:128 * h + 128], T.xs[:, 512 * h:512 * h + 512], ["xs%d" % h], ["rq%d" % h])
    slot = lambda s: 256 + 128 * (s & 1) + 64 * (1 - (s >> 1 & 1))

    def pick(at, a, n, key):
        copy(T.lq[:, at:at + 16 * n].bitcast(dt.uint32), T.rq[:].bitcast(dt.uint32).indirect(T.lp[:, a:a + n]),
             ["rq0", "rq1", "lp"], ["q" + key], True)
        close("v")
        act(T.ls[:, at:at + 16 * n], T.rs[:].indirect(T.lp[:, a:a + n]), ["rq0", "rq1", "lp"], ["s" + key], cut=True)
        close("a")

    pick(0, 4, 4, "one")
    pick(64, 8, 8, "out")
    pick(slot(r), 0, 4, "own")
    c1, c2, c3, c4 = (T.cores[r ^ k] for k in (1, 2, 3, 4))
    e = topo.engines(core, c1)
    n4 = len(e) // 4
    e0, e1, e2, e3 = (e[n4 * k:n4 * k + n4] for k in range(4))

    def view(t, a, codes):
        return t[:, a:a + 64].bitcast(dt.uint8) if codes else t[:, a:a + 64]

    for keys, pieces in ((["qone"], (0,)), (["qout"], (1, 2)), (["sone", "sout"], (0, 1, 2))):
        codes = keys[0][0] == "q"
        t = T.lq if codes else T.ls
        need("g", keys)
        es = (e0, e1, e2 + e3) if codes else (e2, e3, e0 + e1)
        g.remote_dma_fused([RemoteDMATransfer(dst_ids=[dst_id((c1, c3, c2)[k])], dma_engine_mask=mask_of(es[k]), remote_sem=T.sem.arr0,
                                              src=view(t, 64 * k, codes), dst=view(t, slot(r), codes))
                            for k in pieces], local_sem=T.sem.sent)
    sent = [2 * len(e)]
    landed("lin", "arr0", 2 * len(e))
    e8 = topo.engines(core, c4)
    rest = [k for k in e if k not in e8]

    def send(cc, es, q, s, a, at, n, sem, rd, key):
        need("g", rd)
        rid, pid = int(topo.addr(cc)[0]), int(topo.addr(cc)[1])
        g.remote_dma(q[:, at:at + n].bitcast(dt.uint8), q[:, a:a + n].bitcast(dt.uint8), T.sem[sem], T.sem.sent, pid, rid, mask_of(es))
        g.remote_dma(s[:, at:at + n], s[:, a:a + n], T.sem[sem], T.sem.sent, pid, rid, mask_of(es))
        sent[0] += 2 * len(es)
        landed(key, sem, 2 * len(es))

    def send_numbers(cc, es, a, at, sem, key):
        need("g", ["xq"])
        h = len(es) // 2
        g.remote_dma_fused([RemoteDMATransfer(dst_ids=[dst_id(cc)], dma_engine_mask=mask_of(x), remote_sem=T.sem[sem], src=src, dst=dst)
                            for x, src, dst in ((es[:h], T.xq[:, a:a + 8].bitcast(dt.uint8), T.xq[:, at:at + 8].bitcast(dt.uint8)),
                                                (es[h:], T.xsc[:, a:a + 32], T.xsc[:, at:at + 32]))], local_sem=T.sem.sent)
        sent[0] += len(es)
        landed(key, sem, len(es))

    at2 = 3 - 3 * b2

    def gfill(out, n, val, key, rd=()):
        op("g", lambda: g.iota(out, [[0, n]], val, 0, allow_small_or_imprecise_dtypes=True), r=rd, w=[key])
        close("g")

    gfill(T.k7[:], 176, 0, "k7z")
    op("g", lambda: g.affine_select(T.zz[:, 4:516:4], T.zz[:, 4:516:4], [[1, 128]], A.not_equal, 1.0, 0, -1), r=["zz"], w=["et"])
    close("g")
    gfill(T.st[:, 1:512:2], 256, 0, "stz")
    iota(T.i1[:], [[8, 8], [2, 2]], 0, 0, "i1")
    gfill(T.st[0:1, 1:512:4], 128, 2, "st1", ["stz"])
    gfill(T.st[0:1, 3:512:4], 128, 32, "st3", ["stz"])
    gfill(T.xa[:], 512, 0, "xaz")
    gfill(T.mt[:, 0:192], 192, 0, "mtz0")
    beta = lambda a, n, s=1: run(T.xa, 97 + 4 * a, n, 4 * s)
    gfill(run(T.xa, 99, 32, 4), 32, 1, "xa3", ["xaz"])
    op("g", lambda: g.iota(beta(0, 16), [[64, 2], [0, 8]], 128, 0, allow_small_or_imprecise_dtypes=True), r=["xaz"], w=["xb0"])
    gfill(beta(17, 8, 2), 8, 64, "xb2", ["xaz"])
    gfill(T.mt[:, 704:1088], 384, 0, "mtz1")
    gfill(T.mu[:, 0:384], 384, 0, "muz")
    gfill(T.g8[:, 568:624], 56, 0, "g8z3")
    XB = ["xa3", "xb0", "xb2"]
    sy = 4 if b1 else 32
    iota(T.iy[:], [[1, 4], [sy - 2 * sy * b2, 2]], sy * b2, 0, "iy")
    iota(T.id[:], [[4, 4], [64, 2]], 0, 0, "id")
    afill(T.km[:], 288, 0.0, "kmz")
    afill(T.hz[:], 32, 0.0, "hzz")
    afill(T.hr4[:, 0:812:4], 203, 0.0, "hrz0")
    afill(T.hr5[:, 0:670:5], 134, 0.0, "hrz1")
    afill(T.hr6[:, 0:246:6], 41, 0.0, "hrz2")
    close("a")
    HRZ = ["hrz0", "hrz1", "hrz2"]

    def spreader(name, at):
        for t, s in ((0, 32.0), (2, -32.0)):
            ts(T.st[:, t:512:4], T.uu[:, 0:256:2], col(name), s, A.is_equal, A.mult, ["uu", "f" + name], ["st%d" % t])
        close("v")

    def hot(lo, hi, at, n, first, s1, s2, key, rd=()):
        ts(T.k7[lo:hi, at:at + 2 * n:2], T.kj[lo:hi, first:first + n], T.ff[lo:hi, place[s1]:place[s1] + 1],
           T.ff[lo:hi, place[s2]:place[s2] + 1], A.subtract, A.is_equal, ["kj", "k7z", "f" + s1, "f" + s2] + list(rd), [key])

    ts(T.ic[:], T.ib[:], col("s"), None, A.add, None, ["ib", "fs"], ["ic"])
    ts(T.ke[:], T.kj[:, 0:8], col("c"), None, A.is_equal, None, ["kj", "fc"], ["ke"])
    close("v")
    ts(T.mka[:], T.uu[:, 0:128], col("e"), None, A.is_equal, None, ["uu", "fe"], ["mka"])
    ts(T.lg0[:], T.i0[:], col("g0"), None, A.add, None, ["i0", "fg0"], ["lg0"])
    close("v")
    for a, half, k in ((0, -5.0, 3), (4, -6.0, -5), (8, -5.5, -6)):
        ts(T.ie[:, a:a + 4], T.ic[:, a:a + 4], half, 1.0 / k, A.add, A.mult, ["ic"], ["ie%d" % abs(k)])
    close("v")
    spreader("m", 0)
    ts(T.mkb[:], T.uu[:, 0:256:8], col("e"), None, A.is_equal, None, ["uu", "fe"], ["mkb0"])
    close("v")
    tt(T.ig[:], T.ic[:], T.ie[:], A.add, ["ic", "ie3", "ie4", "ie5", "ie6"], ["ig"])
    close("v")
    fields(names[13:16])
    tt(T.ig[:, 8:12], T.ig[:, 8:12], T.ie[:, 8:12], A.add, ["ig", "ie6"], ["ig"])
    close("v")
    fields(names[16:])
    ts(T.lb[:], T.ig[:], 2.0, col("h4"), A.mult, A.add, ["ig", "fh4"], ["lb"])
    close("v")
    hot(64, 128, 48, 16, 0, "a8", "c", "k7a")
    hot(0, 64, 80, 16, 0, "a", "c2", "k7b")
    close("v")
    act(T.hz[:, 2:32:4], T.ke[:], ["ke", "hzz"], ["hc1"], scale=UNIT)
    for j in range(1, 7):
        t, at = nums_at(j)
        act(run(t, at + 2 * hp(j) // KH[j + 1], 8, hp(j)), T.ke[:], ["ke"] + HRZ, ["hc%d" % (j + 1)], scale=(j + 1) * UNIT)
    close("a")

    def decode(n, q, s, rd):
        for b in range(4):
            mm(b, n, T.eq[:, 128 * b:128 * b + 128], T.es[:, 128 * b:128 * b + 128], q, s, ["eq%d" % b] + rd)

    def halves(name, outs, bs=range(4)):
        for b in bs:
            for k, (t, at, a, n) in enumerate(outs):
                act(T.dt0[:, :, at, b:16:4] if t is None else run(t, 4 * at + b, n, 4), bank[b][:, a:a + n], ["b%d" % b], ["%s%d%d" % (name, k, b)], scale=0.5)
            close("a")
        D[name] = ["%s%d%d" % (name, k, b) for k in range(len(outs)) for b in range(4)]

    D = {}

    def sums(j, back):
        t, at = sums_at(j)
        return run(t, at + pp(j) // KP[j + 1] * STEPS[KP[j + 1]][1] - pp(j) * back, 8, pp(j))

    def turn(a, n, sh=0):
        op("v", lambda: V.transpose(run(T.g8, g8_at(a + sh) + 2, 32 * n, 2), T.gb[:, 32 * a:32 * (a + n)]),
           r=["gb%d" % j for j in range(a, a + n)] + G8Z + ["g8z3"] * sh, w=["t%d" % (j + sh) for j in range(a, a + n)], cut=True)
        close("v")

    def thin(j):
        a, n, wide = {3: (0, 2, 96), 5: (4, 3, 96), 6: (8, 3, 80), 4: (12, 2, 73)}[KP[j]]
        act(T.g3[:, g3_at[j]:g3_at[j] + 16 * n], T.g8[:, g8_at(j) - 8:g8_at(j) - 8 + wide].indirect(T.lb[:, a:a + n]),
            ["t%d" % u for u in range(j - 1, j + 1 + (j in (3, 4, 6)))] + ["lb"], ["s%d" % j], cut=True)
        close("a")

    def step(name, k7, n7, sh=0):
        kind, j = name[0], int(name[1])
        u = j + sh
        if kind == "t":
            if sh:
                turn(*((1, 1), (2, 2), (5, 3), (4, 1))[j], sh)
            else:
                turn(*((2, 4), (6, 2))[j - 1])
            for v in (((), (3,), (6, 8), (4, 5)) if sh else ((), (3, 4, 5), (6,)))[j]:
                thin(v)
        elif kind in "pq":
            k = KP[u]
            if j < 7:
                t, at = sums_at(u)
                n, far = pp(u) // k, pp(u) // KP[u + 1]
                there = far * STEPS[KP[u + 1]][1] if kind == "p" else far * STEPS[KP[u + 1]][0] + pp(u)
                out = run(t, at + there - n * STEPS[k][2], 8 * k, n)
            else:
                out = T.p7[:, 0:8 * k]
            if u == 0:
                d1, rd = T.g8[:, 2:66:2], ["t0"]
            elif k != 8:
                d1, rd = T.g3[:, g3_at[u]:g3_at[u] + 8 * k], ["s%d" % u]
            else:
                d1, rd = T.g8[:, g8_at(u) + 1:g8_at(u) + 65], ["t%d" % u]
            if j == 0:
                return scan(out, T.q0[:, 0:8 * k], d1, LOW, A.add, rd + ["top", "top0", "prz0", "prz1", "prz2", "prz3"], [name])
            scan(out, run(*sums_at(u - 1), 8 * k, pp(u - 1) // k), d1, LOW, A.add, rd + ["p%d" % (j - 1), "q%d" % (j - 1)], [name])
        elif kind in "dl":
            if j < 7:
                t, at = sums_at(u)
                diagonal, _, done = STEPS[KP[u]]
                m = run(t, at + pp(u) // KP[u + 1] * STEPS[KP[u + 1]][1] + pp(u) // KP[u] * (diagonal - done), 8, pp(u))
            else:
                m = T.p7[:, 0:8 * KP[u]:KP[u]]
            at = 0 if kind == "d" else 2
            out = run(T.k7, k7 + at, 8, KH[7]) if j == 7 else run(T.km, km_at(j) + at, 8, KH[j])
            tt(out, sums(u - 1, int(kind == "d")), m, A.is_ge if kind == "d" else A.is_gt,
               ["kmz", "k7z", "p%d" % (j - 1), "p%d" % j], ["k" + name], True)
        else:
            k = KH[j]
            rd = HRZ + ["hc%d" % j, "h%d" % (j - 1), "g%d" % (j - 1), "kd%d" % j, "kl%d" % j]
            if j == 7:
                return scan(run(T.xa, 0, n7, 2), run(*nums_at(6), n7, 4), T.k7[:, k7:k7 + n7], 0.0, A.subtract,
                            rd + ["k7a", "k7b", "k7c", "xaz"], [name])
            t, at = nums_at(j)
            n = 7 * k + (left(j) + 1 if kind == "h" else 0)
            src = T.hz[:, 0:n] if j == 1 else run(*nums_at(j - 1), n, hp(j - 1) // k)
            there = hp(j) // KH[j + 1] * left(j + 1) if kind == "h" else hp(j) // KH[j + 1] + hp(j)
            scan(run(t, at + there - hp(j) // k * left(j), n, hp(j) // k), src,
                 T.km[:, km_at(j):km_at(j) + n], 0.0, A.subtract, rd, [name])

    def gather(q, gm, lst, a, n, rd):
        args = (T.gb[:, 32 * a:32 * (a + n)], gm.indirect(lst[:, 2 * a:2 * (a + n)]), rd, ["gb%d" % j for j in range(a, a + n)])
        if q == "a":
            act(*args, cut=True)
        else:
            copy(*args, True)
        close(q)

    later = []

    def gap(n):
        close("v")
        for fn in later[:n]:
            fn()
        del later[:n]
        close("v")

    def first(gm, lst, rd):
        gather("a", gm, lst, 1, 1, rd)
        gather("v", gm, lst, 0, 1, rd)

    def start(gm, lst, rd):
        gather("a", gm, lst, 2, 4, rd)
        turn(0, 2)
        gap(2)
        thin(1)
        gather("a", gm, lst, 6, 2, rd)

    def align(k7, n7, slot, at, w, aside, sh=0):
        for name in ORDER_AHEAD if sh else ORDER:
            step(name, k7, n7, sh)
            if name in ("q1", "t2"):
                aside(name == "t2")
            if name in ("q1", "h6", "h7"):
                gap(2)
        q = T.xq[:, at:at + 128], T.xsc[:, at:at + 128]
        quant(*q, T.xa[:], ["h7"] + XB, ["xq"])
        ts(T.pc[:, slot:slot + 1], T.xa[:, 94:95], 1.0 / UNIT, None, A.mult, None, ["h7"], ["pc%d" % slot], True)
        close("v")
        mm(5, 128, T.stq[:, w:w + 128], T.sts[:, w:w + 128], *q, ["stq%d" % w, "xq"])

    def masked(out, k, a, n, mk, rd, key):
        tt(out, bank[k][:, a:a + n], mk, A.mult, ["b%d" % k] + rd, [key], True)
        close("v")

    def blend(out, window, lst, da, rd, wr):
        tt(out, window.indirect(lst), da, A.add, rd, wr, True)
        close("v")

    L = ["lin", "qown", "sown"]
    mm(4, 128, *win(256), *win(384), L)

    def decode0(b):
        e_b = T.eq[:, 128 * b:128 * b + 128], T.es[:, 128 * b:128 * b + 128]
        quant(*e_b, T.zz[:, 4 - b:516 - b], ["et"], ["eq%d" % b])
        mm(b, 256, *e_b, *win(256, 256), ["eq%d" % b] + L)

    masked(T.gm0[:], 4, 0, 128, T.mka[:], ["mka"], "gm0")
    decode0(0)
    first(T.gm0[:], T.lg0, ["gm0", "lg0"])
    decode0(1)
    op("s", lambda: g.sync.dma_start(T.wt[:], T.w[:]), r=["lin"], w=["wt"], dma=True)
    close("s")

    def aside0(second):
        halves("d0", [(T.db0, 0, 128, 128), (T.da0, 0, 64, 64), (None, 0, 0, 32), (None, 1, 32, 32)], (1, 2, 3) if second else (0,))
        if second:
            act(T.da0[:, 256:512], T.dt0[:], D["d0"], ["d0u"])
            close("a")
            D["d0"].append("d0u")

    idle = lambda: None
    later += [lambda: decode0(2), idle, lambda: decode0(3), idle,
              lambda: quant(T.stq[:, 0:128], T.sts[:, 0:128], T.st[:], ["st0", "st1", "st2", "st3"], ["stq0"]), idle,
              lambda: ts(T.lg1[:], T.i1[:], col("g1"), None, A.add, None, ["i1", "fg1"], ["lg1"]),
              lambda: floats(names[13:])]
    start(T.gm0[:], T.lg0, ["gm0", "lg0"])
    align(0, 112, 0, 0, 0, aside0)
    send_numbers(c2, rest, 16, 128, "arrj", "pin")
    afill(beta(0, 16), 16, 0.0, "xb0", ["xq"])
    close("a")
    ts(T.lg2[:], T.kj[:, 0:16], 2.0, col("u"), A.mult, A.add, ["kj", "fu"], ["lg2"])
    ts(run(T.k7, 160, 8, 2), T.kj[:, 8 * at2:8 * at2 + 8], col("q"), None, A.is_equal, None, ["kj", "fq", "k7z"], ["k7c"])
    close("v")
    spreader("e", 128)
    ts(T.o0[:], bank[5][:, 24:56], col("m32"), col("e"), A.add, A.add, ["b5", "fm32", "fe"], ["o0"], True)
    close("v")
    blend(T.mt[:, 192:512], T.db0[:], T.o0[:, 0:20], T.da0[:, 0:320], D["d0"] + ["o0"], ["mt1"])
    blend(T.mt[:, 576:704], T.db0[:], T.o0[:, 20:28], T.da0[:, 320:448], D["d0"] + ["o0"], ["mt2"])
    quant(*win(512), T.mt[:, 0:512], ["mtz0", "mt1"], ["m01"])
    blend(T.mt[:, 512:576], T.db0[:], T.o0[:, 28:32], T.da0[:, 448:512], D["d0"] + ["o0"], ["mt3"])
    quant(*win(640), T.mt[:, 576:1088], ["mtz1", "mt2"], ["m0a"])
    own = 64 * (1 - b1)
    store("s", T.pf[0:1, 128:192], T.pc[own:own + 64, 0:1], ["pc0"], ["pf0"])
    close("s")

    mm(4, 128, *win(496), *win(512), L + ["m01"])
    mm(7, 128, *win(496), *win(544), L + ["m01", "m0a"])
    masked(T.gm1[:, 0:16], 4, 112, 16, T.mkb[:, 0:16], ["mkb0"], "gm1")
    quant(*win(672), T.mt[:, 512:1024], ["mtz1", "mt2", "mt3", "m0a"], ["m02"])
    send(c4, e8, T.lq, T.ls, 592, 800, 96, "arr1", ["m01", "m02"], "fin")
    send(c2, rest, T.lq, T.ls, 624 - 64 * b1, 896, 64, "arry", ["m01", "m02"], "yin")
    mm(6, 128, *win(496), *win(672), L + ["m01", "m02"])
    decode(128, *win(560), ["m01", "m02"])
    first(T.gm1[:, 0:16], T.lg1, ["gm1", "lg1"])
    masked(T.gm1[:, 16:48], 7, 96, 32, T.mkb[:], ["mkb0"], "gm1b")

    def aside1(second):
        halves("d1", [(T.d1, 0, 0, 32), (T.d1, 32, 64, 64)], (2, 3) if second else (0, 1))
        if second:
            mm(6, 128, T.eq[:, 256:384], T.es[:, 256:384], T.xq[:, 8:136], T.xsc[:, 8:136], ["eq2", "xq", "pin"])
            act(T.pc[:, 2:3], bank[6][:, 127:128], ["b6"], ["pc2"], scale=1.0 / UNIT)
            close("a")
            store("s", T.pf[0:1, 0:64], T.pc[own:own + 64, 2:3], ["pc2"], ["pf2"])
            close("s")
            decode(128, *win(768), ["m02", "fin"])
            halves("df", [(T.df, 0, 32, 96)])

    later += [lambda: ts(T.ly[:, 0:8], T.iy[:], col("y0"), col("y1"), A.add, A.add, ["iy", "fy0", "fy1"], ["ly0"]),
              lambda: ts(T.ly[:, 8:12], T.kj[:, 0:4], col("s4"), 128.0, A.add, A.add, ["kj", "fs4"], ["ly1"]),
              lambda: ts(T.ld[:], T.id[:], col("i16"), col("e"), A.add, A.add, ["id", "fi16", "fe"], ["ld"]),
              idle, lambda: quant(T.stq[:, 128:256], T.sts[:, 128:256], T.st[:], ["st0", "st1", "st2", "st3"], ["stq128"])]
    gather("a", T.gm1[:, 0:48], T.lg1, 3, 3, ["gm1", "gm1b", "lg1"])
    turn(0, 2)
    gather("v", T.gm1[:, 0:48], T.lg1, 2, 1, ["gm1", "gm1b", "lg1"])
    masked(T.gm1[:, 48:64], 6, 0, 16, T.mkb[:, 0:16], ["mkb0"], "gm1c")
    thin(1)
    gather("a", T.gm1[:], T.lg1, 6, 2, ["gm1", "gm1b", "gm1c", "lg1"])
    align(0, 80, 4, 160, 0, aside1)
    send_numbers(c4, e8, 192, 288, "arr2", "jin")
    quant(T.wq[:], T.ws[:], T.wt[:], ["wt"], ["wq"])
    act(beta(0, 8), T.uu[:, 0:32:4], ["uu", "xq"], ["xb0"], scale=0.5)
    close("a")
    if b2:
        quant(T.dq[:], T.ds[:], T.mt[:, 512:1024], ["mt2", "mt3", "mtz1"], ["dq", "dq0"])
    ts(T.o1[:], bank[5][:, 24:32], 8.0, col("s"), A.mult, A.add, ["b5", "fs"], ["o1"], True)
    close("v")

    def prod(k, q, s, rd):
        for o in range(2):
            mm(k + o, 128, T.wq[:, 128 * o:128 * o + 128], T.ws[:, 128 * o:128 * o + 128], q, s, ["wq"] + rd)

    def stage(k, a, n, at, key):
        for o in range(2):
            act(T.ys[:, 192 * o + at:192 * o + at + n], bank[k + o][:, a:a + n], ["b%d" % (k + o)], ["ys%s%d" % (key, o)])
            close("a")

    def spread8():
        lst = T.lg2[:, 0:4]
        copy(T.dq[:, 0:64].bitcast(dt.uint32), T.hq[:, 96:128].bitcast(dt.uint32).indirect(lst), ["hk", "lg2"], ["dq"], True)
        close("v")
        act(T.ds[:, 0:64], T.hs[:, 96:128].indirect(lst), ["hk", "lg2", "dq0"], ["ds"], cut=True)
        close("a")

    K, F = (T.hq[:, 0:128], T.hs[:, 0:128]), (T.hq[:, 128:256], T.hs[:, 128:256])
    prod(0, *win(560), ["m01", "m02"])
    prod(2, *win(832), ["fin", "yin"])
    stage(0, 64 * b1, 64, 64 * b1, "a")
    for out, key in ((T.mt[:, 0:16], "mtf"),) + (() if b2 else ((T.mu[:, 256:272], "mu1"),)):
        tt(out, T.df[:, 144:160], T.df[:, 0:16], A.add, D["df"] + ["muz", "mtz0"], [key], True)
    close("v")
    blend(T.mu[:, 384:512], T.d1[:, 128:384], T.o1[:], T.d1[:, 0:128], D["d1"] + ["o1"], ["mu0"])
    quant(*K, T.mu[:], ["muz", "mu0", "mu1"], ["hk"])
    mm(6, 128, T.stq[:, 0:128], T.sts[:, 0:128], T.xq[:, 168:296], T.xsc[:, 168:296], ["stq0", "xq", "jin"])
    if not b2:
        mm(7, 128, *K, *K, ["hk"])
    ts(T.of[:, 0:7], bank[6][:, 121:128], 8.0, col("s"), A.mult, A.add, ["b6", "fs"], ["of"], True)
    close("v")
    if b2:
        spread8()
    blend(T.mt[:, 16:128], T.df[:, 144:384], T.of[:, 0:7], T.df[:, 16:128], D["df"] + ["of"], ["mtz0"])
    if not b2:
        masked(T.gm2[:, 32:40], 7, 64, 8, T.mkb[:, 0:8], ["mkb0"], "gme")
        gather("a", T.gm2[:, 32:40], T.lg2, 0, 1, ["gme", "lg2"])
    stage(2, 64, 64, 64 - 64 * b1, "c")
    quant(*F, T.mt[:, 0:512], ["mtz0", "mtf", "mt1"], ["hf"])
    send(c4, e8, T.hq, T.hs, 128, 256, 32, "arr3", ["hf"], "bin")
    if not b2:
        turn(0, 1, 1)
        thin(1)

    H = ["hk", "hf"]
    if b2:
        mm(4, 128, *F, T.dq[:], T.ds[:], ["hf", "dq", "ds"])
        mm(7, 128, *F, *K, H)
    else:
        mm(4, 128, *K, *F, H)
    decode(128, T.hq[:, 96:224], T.hs[:, 96:224], H)
    if b2:
        tt(T.gb[:, 0:64], bank[4][:, 0:64], T.mka[:, 0:64], A.mult, ["b4", "mka"], ["gb0", "gb1"], True)
        close("v")
        masked(T.gm2[:, 0:32], 7, 96, 32, T.mkb[:, 0:32], ["mkb0"], "gm2")
        turn(0, 2)
        gather("a", T.gm2[:, 0:32], T.lg2, 4, 2, ["gm2", "lg2"])
        gather("v", T.gm2[:, 0:32], T.lg2, 2, 2, ["gm2", "lg2"])
        thin(1)
        gather("a", T.gm2[:, 0:32], T.lg2, 6, 2, ["gm2", "lg2"])
    else:
        masked(T.gm2[:, 0:32], 4, 0, 32, T.mkb[:, 0:32], ["mkb0"], "gm2")
        for q, a, n in (("a", 2, 2), ("v", 1, 1), ("a", 4, 1), ("a", 5, 3)):
            gather(q, T.gm2[:, 0:32], T.lg2, a, n, ["gm2", "lg2"])
        step("p0", 0, 0, 1)
        step("q0", 0, 0, 1)
    prod(5, *K, ["hk"])
    store("s", T.pf[0:1, 64:128], T.pc[64:128, 4:5], ["pc4", "jin"], ["pf1"])
    close("s")

    def aside2(second):
        if not second:
            halves("d2", [(T.d2, 0, 0, 64)])
            return
        stage(5, 96, 32, 128 + 32 * b2, "d")
        prod(0, T.hq[:, 160:288], T.hs[:, 160:288], ["hf", "bin"])
        act(T.dc2[:], T.d2[:, 128 * b2:128 * b2 + 128].indirect(T.ld[:]), D["d2"] + ["ld"], ["dc2"])
        close("a")
        stage(0, 96, 32, 160 - 32 * b2, "b")
        for o in range(2):
            act(T.ya[:, 192 * o:192 * o + 192], T.ys[:, 192 * o:192 * o + 192].indirect(T.ly[:]),
                ["ys%s%d" % (u, o) for u in "abcd"] + ["ly0", "ly1"], ["ya%d" % o])
            close("a")
            store("s", T.y[:, 224 * o:224 * o + 192], T.ya[:, 192 * o:192 * o + 192], ["ya%d" % o])
        close("s")

    align(112, 64, 8, 320, 128, aside2, 1 - b2)
    store("s", T.pt[0:1, 192:224], T.pc[32 * at2:32 * at2 + 32, 8:9], ["pc8"])
    close("s")
    for a in range(2):
        copy(T.pa[0:1, :, a ^ b2, b1, :], T.pf[0:1, 128 + 32 * a:160 + 32 * a], ["pf0"], ["pa0%d" % a])
        copy(T.pa[0:1, :, a ^ b2, 1 - b1, :], T.pf[0:1, 32 * a:32 * a + 32], ["pf2"], ["pa1%d" % a])
        copy(T.pb[0:1, :, a ^ b2, :], T.pf[0:1, 64 + 32 * a:96 + 32 * a], ["pf1"], ["pb%d" % a])
    close("v")
    store("s", T.pt[0:1, 0:128], T.pa[0:1, :, :, :, :], ["pa00", "pa01", "pa10", "pa11"])
    store("s", T.pt[0:1, 128:192], T.pb[0:1, :, :, :], ["pb0", "pb1"])
    close("s")
    ts(T.o2[:], bank[5][:, 24:32], 4.0, col("e"), A.mult, A.add, ["b5", "fe"], ["o2"], True)
    close("v")
    blend(T.mt[:, 0:128], T.d2[:, 128 - 128 * b2:256 - 128 * b2], T.o2[:], T.dc2[:], D["d2"] + ["dc2", "o2"], ["mtz0", "mtf"])
    quant(T.m2q[:], T.m2s[:], T.mt[:, 0:512], ["mtz0", "mt1"], ["m2"])
    prod(6, T.m2q[:], T.m2s[:], ["m2"])
    store("s", T.oc[:, 0:128], T.m2q[:, 0:32].bitcast(dt.uint8), ["m2"])
    for k in range(4):
        store("sa"[k % 2], T.osc[4 * k:4 * k + 4, 0:32], T.m2s[32 * k:32 * k + 4, 0:32], ["m2"])
    act(T.y2[:, 0:32], bank[6][:, 0:32], ["b6"], ["y20"])
    close("a")
    copy(T.y2[:, 32:64], bank[7][:, 0:32], ["b7"], ["y21"])
    close("v")
    store("a", T.y[:, 192:224], T.y2[:, 0:32], ["y20"])
    store("s", T.y[:, 416:448], T.y2[:, 32:64], ["y21"])
    g.wait_ge(T.sem.sent, sent[0])
    finish("s")
